import numpy as np
import ml_dtypes


def mxq(x, axis, fmt="e4m3"):
    dtype, down = {"e4m3": (ml_dtypes.float8_e4m3fn, 7), "e5m2": (ml_dtypes.float8_e5m2, 14)}[fmt]
    v = np.moveaxis(np.asarray(x, np.float32).astype(ml_dtypes.bfloat16).astype(np.float64), axis, -1)
    blocks = v.reshape(v.shape[:-1] + (-1, 32))
    amax = np.abs(blocks).max(-1, keepdims=True)
    byte = np.maximum(np.where(amax > 0, np.frexp(amax)[1] - 1 + 127, 0) - down, 1)
    scale = np.exp2(byte - 127.0)
    codes = (blocks / scale).astype(np.float32).astype(dtype).astype(np.float64)
    return np.moveaxis((codes * scale).reshape(v.shape), -1, axis)


WIDE = False


def mx_kscale(k):
    if not WIDE:
        return np.ones(k)
    levels = np.array([10, -10, 5, -5, 0])
    if k % 512:
        return np.exp2(np.random.permutation(np.resize(levels, k // 32))).repeat(32)
    a = np.empty((k // 512, 16))
    for p in range(k // 512):
        a[p, :8] = np.random.permutation(np.resize(levels, 8))
        for g in range(8):
            far = levels[np.abs(levels - a[p, g]) >= 10]
            a[p, g + 8] = far[np.random.randint(len(far))]
    return np.exp2(a.ravel()).repeat(32)


def f64(x):
    return np.asarray(x).astype(np.float64)


def striped8(idx):
    return np.concatenate([x.reshape(-1, 16).T for x in idx]).astype(np.uint16)


def runs(offs, k):
    lists = np.stack([offs[16 * r : 16 * r + 16].T.reshape(-1) for r in range(8)]).astype(np.int64)
    return lists[np.arange(k) % 512 // 64]


def pack_weight(w):
    k, n = w.shape
    w = f64(np.asarray(w, np.float32).astype(ml_dtypes.bfloat16)).reshape(k // 32, 32, n)
    amax = np.abs(w).max(1)
    byte = np.clip(np.where(amax > 0, np.frexp(amax)[1] - 1 + 127 - 7, 1), 1, 254)
    scaled = (w * np.exp2(127.0 - byte)[:, None, :]).reshape(k, n).astype(np.float32)
    words = np.ascontiguousarray(scaled.reshape(k // 512, 128, 4, n).transpose(0, 1, 3, 2)).astype(ml_dtypes.float8_e4m3fn).view(np.uint8)
    return words, np.ascontiguousarray(byte.astype(np.uint8).reshape(k // 512, 16, n))


def unpack_weight(words, scales):
    g, p, n, _ = words.shape
    vals = np.ascontiguousarray(words).view(ml_dtypes.float8_e4m3fn).astype(np.float64) * np.repeat(np.exp2(scales.astype(np.float64) - 127.0), 8, axis=1)[..., None]
    return vals.transpose(0, 1, 3, 2).reshape(g * 512, n)


E2M1 = np.array([0.0, 0.5, 1.0, 1.5, 2.0, 3.0, 4.0, 6.0, -0.0, -0.5, -1.0, -1.5, -2.0, -3.0, -4.0, -6.0])


def pack_fp4(w):
    k, n = w.shape
    w = f64(np.asarray(w, np.float32).astype(ml_dtypes.bfloat16)).reshape(k // 32, 32, n)
    amax = np.abs(w).max(1)
    mant, ex = np.frexp(amax / 6.0)
    byte = np.clip(np.where(amax > 0, np.where(mant > 0.5, ex, ex - 1) + 127, 1), 1, 254)
    scaled = (w * np.exp2(127.0 - byte)[:, None, :]).reshape(k, n).astype(np.float32)
    c = np.ascontiguousarray(scaled.reshape(k // 512, 128, 4, n).transpose(0, 1, 3, 2)).astype(ml_dtypes.float4_e2m1fn).view(np.uint8) & 0xF
    words = (c[..., 0::2] | (c[..., 1::2] << 4)).reshape(k // 512, 128, 2 * n)
    return np.ascontiguousarray(words), np.ascontiguousarray(byte.astype(np.uint8).reshape(k // 512, 16, n))


def unpack_fp4(words, scales):
    g, _, n = scales.shape
    words = np.ascontiguousarray(words).reshape(g, 128, n, 2)
    nib = np.empty((g, 128, n, 4), np.uint8)
    nib[..., 0::2] = words & 0xF
    nib[..., 1::2] = words >> 4
    vals = E2M1[nib] * np.repeat(np.exp2(scales.astype(np.float64) - 127.0), 8, axis=1)[..., None]
    return vals.transpose(0, 1, 3, 2).reshape(g * 512, n)


def planes(y):
    n, m = y.shape
    v = y.astype(np.float32).astype(ml_dtypes.bfloat16).astype(np.float64).reshape(n // 32, 32, m)
    top = np.abs(v).max(1)
    byte = np.clip(np.where(top > 0, np.frexp(top)[1] - 1 + 127 - 7, 1), 1, 254)
    codes = (v * np.exp2(127.0 - byte)[:, None, :]).reshape(n, m).astype(np.float32).astype(ml_dtypes.float8_e4m3fn).view(np.uint8)
    words = codes.reshape(n // 512, 128, 4, m).transpose(0, 1, 3, 2)
    return np.ascontiguousarray(words), np.ascontiguousarray(byte.astype(np.uint8).reshape(n // 512, 16, m))


K, T, S, N, H = 512, 2048, 512, 512, 512


def setup_inputs():
    n = np.random.standard_normal
    s = mx_kscale(K)[:, None]
    u = mx_kscale(H)
    packed_xT = pack_weight(n((K, T)) * s)
    packed_w2 = pack_fp4(n((K, H)) / np.sqrt(K) / s)
    packed_w3 = pack_fp4(n((H, N)) / np.sqrt(2 * H) / u[:, None])
    packed_w4 = pack_fp4(n((H, N)) / np.sqrt(2 * H) / u[:, None])
    return {
        "x_words": packed_xT[0],
        "x_scales": packed_xT[1],
        "w1": (n((K, H)) / np.sqrt(K) / s * u).astype(np.float32),
        "w2_words": packed_w2[0],
        "w2_scales": packed_w2[1],
        "w3_words": packed_w3[0],
        "w3_scales": packed_w3[1],
        "w4_words": packed_w4[0],
        "w4_scales": packed_w4[1],
        "offs": striped8(np.stack([np.random.permutation(T)[:S] for _ in range(8)])),
        "p1": striped8(np.stack([np.random.permutation(S) for _ in range(8)])),
        "p2": striped8(np.stack([np.random.permutation(S) for _ in range(8)])),
    }


def reference(x_words, x_scales, w1, w2_words, w2_scales, w3_words, w3_scales, w4_words, w4_scales, offs, p1, p2):
    xq = unpack_weight(x_words, x_scales)[np.arange(K)[:, None], runs(offs, K)]
    y = mxq(f64(w1), 0, "e4m3").T @ xq
    e = unpack_fp4(w2_words, w2_scales).T @ xq
    z = y * (0.5 * (e[np.arange(H)[:, None], runs(p1, H)] + e[np.arange(H)[:, None], runs(p2, H)]))
    o = unpack_fp4(w3_words, w3_scales).T @ mxq(y, 0, "e4m3") + unpack_fp4(w4_words, w4_scales).T @ mxq(z, 0, "e4m3")
    out_0 = o
    return (out_0,) + planes(out_0)

@@ -1,0 +1,245 @@
+from contextlib import ExitStack
+
+import concourse.mybir as mybir
+
+F32 = mybir.dt.float32
+BF16 = mybir.dt.bfloat16
+I32 = mybir.dt.int32
+U32 = mybir.dt.uint32
+U16 = mybir.dt.uint16
+U8 = mybir.dt.uint8
+FP8X4 = mybir.dt.float8_e4m3fn_x4
+FP4X4 = mybir.dt.float4_e2m1fn_x4
+ADD = mybir.AluOpType.add
+MULT = mybir.AluOpType.mult
+
+P = 128
+PACK = 4
+FIELDS = 2048
+PLACES = 512
+WIDTH = 512
+CHUNK = 128
+GROUP = 16
+QUADRANT = 32
+STRETCHES = ((0, 256), (256, 128), (384, 128))
+
+FLOPS = 4 * 2 * 512 * 512 * 512
+
+
+def tile_picked_pnn8_none_po_kernel(
+    tc, x_words, x_scales, w1, w2_words, w2_scales, w3_words, w3_scales, w4_words, w4_scales, offs, p1, p2,
+    out_0, out_1, out_2,
+):
+    nc = tc.nc
+    chunks = PLACES // CHUNK
+
+    with ExitStack() as ctx:
+        sb = ctx.enter_context(tc.tile_pool(name="sb", bufs=1))
+        ps = ctx.enter_context(tc.psum_pool(name="ps", bufs=1))
+
+        def tile(shape, dtype, name, tag=None):
+            return sb.tile(shape, dtype, name=name, tag=tag or name, align_bytes=64)
+
+        def load_scale_rows(queue, raw, scales):
+            rows = scales[0].bitcast(I32)
+            queue.dma_start(out=raw.bitcast(I32), in_=rows.unsqueeze(1).to_broadcast([16, 8, WIDTH // 4]))
+
+        def deal_scales(queue, name, raw, n, tag=None):
+            plane = tile([P, n, PACK, P], U8, name, tag)
+            nc.vector.tensor_copy(out=plane[:], in_=raw[:].rearrange("p w (m t) -> p w t m", t=PACK))
+            flat = plane[:].rearrange("p w t m -> p (w t m)")
+            for a in range(1, PACK):
+                queue.dma_start(out=flat[a:P:QUADRANT, :].bitcast(I32), in_=flat[8 * a : P : QUADRANT, :].bitcast(I32))
+            return plane
+
+        def deal_words(name, raw):
+            words = tile([P, PACK, 2 * P], U8, name)
+            nc.vector.tensor_copy(
+                out=words[:].bitcast(U16),
+                in_=raw.bitcast(U16).rearrange("p (m t) -> p t m", t=PACK),
+            )
+            return words
+
+        offs_sb = sb.tile([P, PLACES // GROUP], U16, name="offs_sb")
+        p1_sb = sb.tile([P, PLACES // GROUP], U16, name="p1_sb")
+        p2_sb = sb.tile([P, PLACES // GROUP], U16, name="p2_sb")
+        x_table = tile([P, FIELDS], U32, "x_table")
+        x_scale_table = tile([P, FIELDS], U8, "x_scale_table")
+        w2_raw = tile([P, 2 * WIDTH], U8, "w2_raw", "before_w1")
+        w34_rows = tile([P, 2, WIDTH], U8, "w34_rows")
+        w2_rows = tile([P, 1, WIDTH], U8, "w2_rows", "raw_rows")
+
+        x_rows = x_scales[0].bitcast(I32).rearrange("(r b) c -> b r c", b=2)
+        nc.sync.dma_start(offs_sb[:], offs)
+        for b, queue in enumerate((nc.scalar, nc.sync)):
+            queue.dma_start(
+                out=x_scale_table[b:P:2, :].bitcast(I32),
+                in_=x_rows[b].unsqueeze(1).to_broadcast([8, 8, FIELDS // 4]),
+            )
+        load_scale_rows(nc.scalar, w2_rows[:, 0, :], w2_scales)
+        nc.sync.dma_start(p1_sb[:], p1)
+        nc.scalar.dma_start(out=w2_raw[:].bitcast(I32), in_=w2_words[0].bitcast(I32))
+        nc.sync.dma_start(p2_sb[:], p2)
+        nc.scalar.dma_start(out=x_table[:].bitcast(I32), in_=x_words[0].rearrange("p c r -> p (c r)").bitcast(I32))
+        load_scale_rows(nc.gpsimd, w34_rows[:, 0, :], w3_scales)
+        load_scale_rows(nc.gpsimd, w34_rows[:, 1, :], w4_scales)
+
+        picked_rows = tile([P, PLACES], U8, "picked_rows")
+        x_plane = tile([P, PLACES], U8, "x_plane")
+        nc.vector.tensor_copy(picked_rows[:], x_scale_table[:].indirect(offs_sb[:]))
+        nc.vector.tensor_copy(out=x_plane[:].bitcast(I32), in_=picked_rows[:].bitcast(I32))
+        for b in range(2):
+            nc.scalar.dma_start(
+                out=x_plane[2 + b : P : QUADRANT, :].bitcast(I32),
+                in_=picked_rows[GROUP + b : P : QUADRANT, :].bitcast(I32),
+            )
+        w2_plane = deal_scales(nc.sync, "w2_plane", w2_rows, 1)[:, 0]
+        w2_codes = deal_words("w2_codes", w2_raw[:])
+
+        w34_raw = tile([P, 4 * WIDTH], U8, "w34_raw", "raw_rows")
+        w3_raw, w4_raw = w34_raw[:, : 2 * WIDTH], w34_raw[:, 2 * WIDTH :]
+        nc.sync.dma_start(out=w3_raw.bitcast(I32), in_=w3_words[0].bitcast(I32))
+        nc.sync.dma_start(out=w4_raw.bitcast(I32), in_=w4_words[0].bitcast(I32))
+        w1_raw = tile([P, 2, PACK, WIDTH // 2], F32, "w1_raw", "before_w1")
+        w1_rows = w1.rearrange("(p j) (h c) -> h p j c", j=PACK, h=2)
+        for h in range(2):
+            nc.sync.dma_start(out=w1_raw[:, h], in_=w1_rows[h])
+
+        x_codes = tile([P, PLACES], U32, "x_codes")
+        nc.vector.tensor_copy(x_codes[:], x_table[:].indirect(offs_sb[:]))
+
+        def e_product(out, t, cols):
+            nc.tensor.matmul_mx(
+                out=out, lhsT=w2_codes[:, t, :].bitcast(FP4X4), lhsT_scale=w2_plane[:, t, :],
+                rhs=x_codes[:, cols].bitcast(FP8X4), rhs_scale=x_plane[:, cols], start=True, stop=True,
+            )
+
+        e_rows = [tile([P, PLACES], F32, "e_row%d" % t) for t in range(PACK)]
+        half = PLACES // 2
+        low = ps.tile([P, half], F32, name="e_low", tag="bank0")
+        high = ps.tile([P, half], F32, name="e_high", tag="bank7")
+        e_product(low[:], 0, slice(0, half))
+        nc.scalar.copy(out=e_rows[0][:, :half], in_=low[:])
+        e_product(high[:], 0, slice(half, PLACES))
+        nc.vector.tensor_copy(out=e_rows[0][:, half:], in_=high[:])
+        for t in range(1, PACK):
+            bank = ps.tile([P, PLACES], F32, name="e_bank%d" % t, tag="bank%d" % t)
+            e_product(bank[:], t, slice(0, PLACES))
+            nc.scalar.copy(out=e_rows[t][:], in_=bank[:])
+
+        w34_plane = deal_scales(nc.gpsimd, "w34_plane", w34_rows, 2, "x_table")
+        w3_plane, w4_plane = w34_plane[:, 0], w34_plane[:, 1]
+        w3_codes = deal_words("w3_codes", w3_raw)
+        w4_codes = deal_words("w4_codes", w4_raw)
+
+        w1_bf = tile([P, PACK * WIDTH], BF16, "w1_bf", "after_w1")
+        cast_out = w1_bf[:].rearrange("p (t m j) -> p m t j", t=PACK, j=PACK)
+        for h in range(2):
+            cast_in = w1_raw[:, h].rearrange("p j (m t) -> p m t j", t=PACK)
+            for m0 in range(0, P // 2, 32):
+                nc.scalar.copy(out=cast_out[:, 64 * h + m0 : 64 * h + m0 + 32], in_=cast_in[:, m0 : m0 + 32])
+        w1_codes = tile([P, WIDTH], U32, "w1_codes")
+        w1_plane = tile([P, WIDTH], U8, "w1_plane")
+        nc.vector.quantize_mx(out=w1_codes[:].bitcast(FP8X4), scales=w1_plane[:], in_=w1_bf[:])
+
+        y_banks = []
+        y_bf = tile([P, PACK * PLACES], BF16, "y_bf")
+        y_codes = tile([P, PLACES], U32, "y_codes")
+        y_plane = tile([P, PLACES], U8, "y_plane")
+        for c in range(chunks):
+            cols = slice(c * CHUNK, (c + 1) * CHUNK)
+            bank = ps.tile([P, PACK, CHUNK], F32, name="y_bank%d" % c, tag="bank%d" % (PACK + c))
+            for t in range(PACK):
+                feats = slice(t * P, (t + 1) * P)
+                nc.tensor.matmul_mx(
+                    out=bank[:, t, :], lhsT=w1_codes[:, feats].bitcast(FP8X4), lhsT_scale=w1_plane[:, feats],
+                    rhs=x_codes[:, cols].bitcast(FP8X4), rhs_scale=x_plane[:, cols], start=True, stop=True,
+                )
+            nc.scalar.copy(
+                out=y_bf[:, PACK * c * CHUNK : PACK * (c + 1) * CHUNK].rearrange("p (n t) -> p n t", t=PACK),
+                in_=bank[:].rearrange("p t n -> p n t"),
+            )
+            y_banks.append(bank)
+        for h in range(2):
+            cols = slice(h * 256, (h + 1) * 256)
+            nc.vector.quantize_mx(
+                out=y_codes[:, cols].bitcast(FP8X4), scales=y_plane[:, cols],
+                in_=y_bf[:, PACK * h * 256 : PACK * (h + 1) * 256],
+            )
+
+        out_codes = tile([P, PLACES], U32, "out_codes")
+        out_plane = tile([P, PLACES], U8, "out_plane")
+        out_rows = out_0.rearrange("(p t) j -> p t j", t=PACK)
+        out_words = out_1[0].rearrange("p c r -> p (c r)").bitcast(I32)
+
+        def finish(c, pair_sum, first):
+            cols = slice(c * CHUNK, (c + 1) * CHUNK)
+            z_bf = tile([P, PACK * CHUNK], BF16, "z_bf%d" % c)
+            nc.vector.scalar_tensor_tensor(
+                out=z_bf[:].rearrange("p (n t) -> p n t", t=PACK),
+                in0=pair_sum[:, :, first : first + CHUNK].rearrange("p t n -> p n t"),
+                scalar=0.5,
+                in1=y_banks[c][:].rearrange("p t n -> p n t"),
+                op0=MULT, op1=MULT,
+            )
+            last = c == chunks - 1
+            if last:
+                banks = [ps.tile([P, CHUNK], F32, name="last_bank%d" % t, tag="bank%d" % (3 + t)) for t in range(PACK)]
+                sums = [one[:] for one in banks]
+            else:
+                bank = ps.tile([P, PACK, CHUNK], F32, name="out_bank%d" % c, tag="bank%d" % c)
+                sums = [bank[:, t, :] for t in range(PACK)]
+
+            def y_pass(t):
+                nc.tensor.matmul_mx(
+                    out=sums[t], lhsT=w3_codes[:, t, :].bitcast(FP4X4), lhsT_scale=w3_plane[:, t, :],
+                    rhs=y_codes[:, cols].bitcast(FP8X4), rhs_scale=y_plane[:, cols], start=True, stop=False,
+                )
+
+            z_codes = tile([P, CHUNK], U32, "z_codes%d" % c)
+            z_plane = tile([P, CHUNK], U8, "z_plane%d" % c)
+
+            def z_pass(t):
+                nc.tensor.matmul_mx(
+                    out=sums[t], lhsT=w4_codes[:, t, :].bitcast(FP4X4), lhsT_scale=w4_plane[:, t, :],
+                    rhs=z_codes[:].bitcast(FP8X4), rhs_scale=z_plane[:], start=False, stop=True,
+                )
+
+            nc.vector.quantize_mx(out=z_codes[:].bitcast(FP8X4), scales=z_plane[:], in_=z_bf[:])
+            out_bf = tile([P, PACK * CHUNK], BF16, "out_bf%d" % c)
+            woven = out_bf[:].rearrange("p (n t) -> p n t", t=PACK)
+            out_f32 = tile([P, PACK, CHUNK], F32, "out_f32_%d" % c)
+            if last:
+                for t in range(PACK):
+                    y_pass(t)
+                for t in range(PACK):
+                    z_pass(t)
+                    if t % 2:
+                        nc.vector.tensor_copy(out=out_f32[:, t, :], in_=sums[t])
+                    else:
+                        nc.scalar.copy(out=out_f32[:, t, :], in_=sums[t])
+                nc.vector.tensor_copy(out=woven, in_=out_f32[:].rearrange("p t n -> p n t"))
+            else:
+                for t in range(PACK):
+                    y_pass(t)
+                    z_pass(t)
+                nc.scalar.copy(out=woven, in_=bank[:].rearrange("p t n -> p n t"))
+                nc.scalar.copy(out=out_f32[:], in_=bank[:])
+            nc.sync.dma_start(out=out_rows[:, :, cols], in_=out_f32[:])
+            nc.vector.quantize_mx(out=out_codes[:, cols].bitcast(FP8X4), scales=out_plane[:, cols], in_=out_bf[:])
+            nc.sync.dma_start(out=out_words[:, cols], in_=out_codes[:, cols].bitcast(I32))
+
+        for start, count in STRETCHES:
+            entries = slice(start // GROUP, (start + count) // GROUP)
+            pair_sum = tile([P, PACK, count], F32, "pair_sum%d" % start, "pair_sum")
+            first_pick = tile([P, PACK, count], F32, "first_pick%d" % start, {0: None, 256: "after_w1", 384: "z_bf0"}[start])
+            for t in range(PACK):
+                nc.vector.tensor_copy(first_pick[:, t, :], e_rows[t][:].indirect(p1_sb[:, entries]))
+                nc.vector.tensor_tensor(pair_sum[:, t, :], e_rows[t][:].indirect(p2_sb[:, entries]), first_pick[:, t, :], ADD)
+            for first in range(0, count, CHUNK):
+                finish((start + first) // CHUNK, pair_sum, first)
+
+        plane_rows = out_2[0].rearrange("(q a) c -> a q c", a=PACK)
+        for a in range(PACK):
+            queue = nc.scalar if a % 2 else nc.sync
+            queue.dma_start(out=plane_rows[a].bitcast(I32), in_=out_plane[a:P:QUADRANT, :].bitcast(I32))

@@ -12,6 +12,7 @@ FP8X4 = mybir.dt.float8_e4m3fn_x4
 FP4X4 = mybir.dt.float4_e2m1fn_x4
 ADD = mybir.AluOpType.add
 MULT = mybir.AluOpType.mult
+COPY = mybir.ActivationFunctionType.Copy
 
 P = 128
 PACK = 4
@@ -21,7 +22,6 @@ WIDTH = 512
 CHUNK = 128
 GROUP = 16
 QUADRANT = 32
-STRETCHES = ((0, 256), (256, 128), (384, 128))
 
 FLOPS = 4 * 2 * 512 * 512 * 512
 
@@ -40,23 +40,29 @@ def tile_picked_pnn8_none_po_kernel(
         def tile(shape, dtype, name, tag=None):
             return sb.tile(shape, dtype, name=name, tag=tag or name, align_bytes=64)
 
+        def entries(start, count):
+            return slice(start // GROUP, (start + count) // GROUP)
+
         def load_scale_rows(queue, raw, scales):
             rows = scales[0].bitcast(I32)
-            queue.dma_start(out=raw.bitcast(I32), in_=rows.unsqueeze(1).to_broadcast([16, 8, WIDTH // 4]))
+            queue.dma_start(out=raw.bitcast(I32), in_=rows.unsqueeze(1).to_broadcast([16, 8, rows.shape[1]]))
 
-        def deal_scales(queue, name, raw, n, tag=None):
+        def deal_scales(name, raw, n, tag=None):
             plane = tile([P, n, PACK, P], U8, name, tag)
-            nc.vector.tensor_copy(out=plane[:], in_=raw[:].rearrange("p w (m t) -> p w t m", t=PACK))
+            nc.vector.tensor_copy(
+                out=plane[:].rearrange("p w t (c i) -> p w c t i", i=16),
+                in_=raw.rearrange("p (w c i t) -> p w c t i", w=n, t=PACK, i=16),
+            )
             flat = plane[:].rearrange("p w t m -> p (w t m)")
             for a in range(1, PACK):
-                queue.dma_start(out=flat[a:P:QUADRANT, :].bitcast(I32), in_=flat[8 * a : P : QUADRANT, :].bitcast(I32))
+                nc.sync.dma_start(out=flat[a:P:QUADRANT, :].bitcast(I32), in_=flat[8 * a : P : QUADRANT, :].bitcast(I32))
             return plane
 
         def deal_words(name, raw):
             words = tile([P, PACK, 2 * P], U8, name)
             nc.vector.tensor_copy(
-                out=words[:].bitcast(U16),
-                in_=raw.bitcast(U16).rearrange("p (m t) -> p t m", t=PACK),
+                out=words[:].bitcast(U16).rearrange("p t (c i) -> p c t i", i=8),
+                in_=raw.bitcast(U16).rearrange("p (c i t) -> p c t i", t=PACK, i=8),
             )
             return words
 
@@ -66,47 +72,44 @@ def tile_picked_pnn8_none_po_kernel(
         x_table = tile([P, FIELDS], U32, "x_table")
         x_scale_table = tile([P, FIELDS], U8, "x_scale_table")
         w2_raw = tile([P, 2 * WIDTH], U8, "w2_raw", "before_w1")
-        w34_rows = tile([P, 2, WIDTH], U8, "w34_rows")
-        w2_rows = tile([P, 1, WIDTH], U8, "w2_rows", "raw_rows")
+        w3_raw = tile([P, 2 * WIDTH], U8, "w3_raw")
+        w2_rows = tile([P, 1, WIDTH], U8, "w2_rows")
+        w3_rows = tile([P, WIDTH], U8, "w3_rows")
 
-        x_rows = x_scales[0].bitcast(I32).rearrange("(r b) c -> b r c", b=2)
         nc.sync.dma_start(offs_sb[:], offs)
-        for b, queue in enumerate((nc.scalar, nc.sync)):
-            queue.dma_start(
-                out=x_scale_table[b:P:2, :].bitcast(I32),
-                in_=x_rows[b].unsqueeze(1).to_broadcast([8, 8, FIELDS // 4]),
-            )
-        load_scale_rows(nc.scalar, w2_rows[:, 0, :], w2_scales)
+        load_scale_rows(nc.sync, x_scale_table[:], x_scales)
+        load_scale_rows(nc.sync, w2_rows[:, 0, :], w2_scales)
+        nc.sync.dma_start(out=w2_raw[:].bitcast(I32), in_=w2_words[0].bitcast(I32))
         nc.sync.dma_start(p1_sb[:], p1)
-        nc.scalar.dma_start(out=w2_raw[:].bitcast(I32), in_=w2_words[0].bitcast(I32))
         nc.sync.dma_start(p2_sb[:], p2)
-        nc.scalar.dma_start(out=x_table[:].bitcast(I32), in_=x_words[0].rearrange("p c r -> p (c r)").bitcast(I32))
-        load_scale_rows(nc.gpsimd, w34_rows[:, 0, :], w3_scales)
-        load_scale_rows(nc.gpsimd, w34_rows[:, 1, :], w4_scales)
+        load_scale_rows(nc.sync, w3_rows[:], w3_scales)
+        nc.sync.dma_start(out=x_table[:].bitcast(I32), in_=x_words[0].rearrange("p c r -> p (c r)").bitcast(I32))
+        nc.sync.dma_start(out=w3_raw[:].bitcast(I32), in_=w3_words[0].bitcast(I32))
 
         picked_rows = tile([P, PLACES], U8, "picked_rows")
         x_plane = tile([P, PLACES], U8, "x_plane")
         nc.vector.tensor_copy(picked_rows[:], x_scale_table[:].indirect(offs_sb[:]))
         nc.vector.tensor_copy(out=x_plane[:].bitcast(I32), in_=picked_rows[:].bitcast(I32))
-        for b in range(2):
+        for a in range(1, PACK):
             nc.scalar.dma_start(
-                out=x_plane[2 + b : P : QUADRANT, :].bitcast(I32),
-                in_=picked_rows[GROUP + b : P : QUADRANT, :].bitcast(I32),
+                out=x_plane[a:P:QUADRANT, :].bitcast(I32), in_=picked_rows[8 * a : P : QUADRANT, :].bitcast(I32)
             )
-        w2_plane = deal_scales(nc.sync, "w2_plane", w2_rows, 1)[:, 0]
+        w2_plane = deal_scales("w2_plane", w2_rows[:, 0, :], 1)[:, 0]
         w2_codes = deal_words("w2_codes", w2_raw[:])
 
-        w34_raw = tile([P, 4 * WIDTH], U8, "w34_raw", "raw_rows")
-        w3_raw, w4_raw = w34_raw[:, : 2 * WIDTH], w34_raw[:, 2 * WIDTH :]
-        nc.sync.dma_start(out=w3_raw.bitcast(I32), in_=w3_words[0].bitcast(I32))
-        nc.sync.dma_start(out=w4_raw.bitcast(I32), in_=w4_words[0].bitcast(I32))
         w1_raw = tile([P, 2, PACK, WIDTH // 2], F32, "w1_raw", "before_w1")
         w1_rows = w1.rearrange("(p j) (h c) -> h p j c", j=PACK, h=2)
         for h in range(2):
             nc.sync.dma_start(out=w1_raw[:, h], in_=w1_rows[h])
+        w4_bytes = tile([P, 3 * WIDTH], U8, "w4_bytes", "picked_rows")
+        w4_raw, w4_rows = w4_bytes[:, : 2 * WIDTH], w4_bytes[:, 2 * WIDTH :]
+        nc.sync.dma_start(out=w4_raw.bitcast(I32), in_=w4_words[0].bitcast(I32))
+        load_scale_rows(nc.sync, w4_rows, w4_scales)
 
         x_codes = tile([P, PLACES], U32, "x_codes")
-        nc.vector.tensor_copy(x_codes[:], x_table[:].indirect(offs_sb[:]))
+        half = PLACES // 2
+        for start in (0, half):
+            nc.vector.tensor_copy(x_codes[:, start : start + half], x_table[:].indirect(offs_sb[:, entries(start, half)]))
 
         def e_product(out, t, cols):
             nc.tensor.matmul_mx(
@@ -114,36 +117,39 @@ def tile_picked_pnn8_none_po_kernel(
                 rhs=x_codes[:, cols].bitcast(FP8X4), rhs_scale=x_plane[:, cols], start=True, stop=True,
             )
 
-        e_rows = [tile([P, PLACES], F32, "e_row%d" % t) for t in range(PACK)]
-        half = PLACES // 2
+        e_rows = [tile([P, PLACES], F32, "e_row%d" % t) for t in range(PACK - 1)]
         low = ps.tile([P, half], F32, name="e_low", tag="bank0")
         high = ps.tile([P, half], F32, name="e_high", tag="bank7")
         e_product(low[:], 0, slice(0, half))
-        nc.scalar.copy(out=e_rows[0][:, :half], in_=low[:])
+        nc.scalar.activation(out=e_rows[0][:, :half], in_=low[:], func=COPY, scale=0.5)
         e_product(high[:], 0, slice(half, PLACES))
-        nc.vector.tensor_copy(out=e_rows[0][:, half:], in_=high[:])
+        nc.vector.tensor_scalar_mul(e_rows[0][:, half:], high[:], 0.5)
+        e_banks = {}
         for t in range(1, PACK):
-            bank = ps.tile([P, PLACES], F32, name="e_bank%d" % t, tag="bank%d" % t)
-            e_product(bank[:], t, slice(0, PLACES))
-            nc.scalar.copy(out=e_rows[t][:], in_=bank[:])
+            e_banks[t] = ps.tile([P, PLACES], F32, name="e_bank%d" % t, tag="bank%d" % t)
+            e_product(e_banks[t][:], t, slice(0, PLACES))
+        for t in range(1, PACK - 1):
+            nc.scalar.activation(out=e_rows[t][:], in_=e_banks[t][:], func=COPY, scale=0.5)
 
-        w34_plane = deal_scales(nc.gpsimd, "w34_plane", w34_rows, 2, "x_table")
-        w3_plane, w4_plane = w34_plane[:, 0], w34_plane[:, 1]
-        w3_codes = deal_words("w3_codes", w3_raw)
+        w3_codes = deal_words("w3_codes", w3_raw[:])
+        w3_plane = deal_scales("w3_plane", w3_rows[:], 1, "x_table")[:, 0]
         w4_codes = deal_words("w4_codes", w4_raw)
+        w4_plane = deal_scales("w4_plane", w4_rows, 1)[:, 0]
 
         w1_bf = tile([P, PACK * WIDTH], BF16, "w1_bf", "after_w1")
         cast_out = w1_bf[:].rearrange("p (t m j) -> p m t j", t=PACK, j=PACK)
         for h in range(2):
-            cast_in = w1_raw[:, h].rearrange("p j (m t) -> p m t j", t=PACK)
-            for m0 in range(0, P // 2, 32):
-                nc.scalar.copy(out=cast_out[:, 64 * h + m0 : 64 * h + m0 + 32], in_=cast_in[:, m0 : m0 + 32])
+            nc.scalar.copy(
+                out=cast_out[:, 64 * h : 64 * h + 64], in_=w1_raw[:, h].rearrange("p j (m t) -> p m t j", t=PACK)
+            )
+        e_rows.append(tile([P, PLACES], F32, "e_row3", "before_w1"))
+        nc.scalar.activation(out=e_rows[3][:], in_=e_banks[3][:], func=COPY, scale=0.5)
         w1_codes = tile([P, WIDTH], U32, "w1_codes")
         w1_plane = tile([P, WIDTH], U8, "w1_plane")
         nc.vector.quantize_mx(out=w1_codes[:].bitcast(FP8X4), scales=w1_plane[:], in_=w1_bf[:])
 
         y_banks = []
-        y_bf = tile([P, PACK * PLACES], BF16, "y_bf")
+        y_bf = [tile([P, 2, PACK * CHUNK], BF16, "y_bf%d" % h) for h in range(2)]
         y_codes = tile([P, PLACES], U32, "y_codes")
         y_plane = tile([P, PLACES], U8, "y_plane")
         for c in range(chunks):
@@ -156,7 +162,7 @@ def tile_picked_pnn8_none_po_kernel(
                     rhs=x_codes[:, cols].bitcast(FP8X4), rhs_scale=x_plane[:, cols], start=True, stop=True,
                 )
             nc.scalar.copy(
-                out=y_bf[:, PACK * c * CHUNK : PACK * (c + 1) * CHUNK].rearrange("p (n t) -> p n t", t=PACK),
+                out=y_bf[c // 2][:, c % 2, :].rearrange("p (n t) -> p n t", t=PACK),
                 in_=bank[:].rearrange("p t n -> p n t"),
             )
             y_banks.append(bank)
@@ -164,7 +170,7 @@ def tile_picked_pnn8_none_po_kernel(
             cols = slice(h * 256, (h + 1) * 256)
             nc.vector.quantize_mx(
                 out=y_codes[:, cols].bitcast(FP8X4), scales=y_plane[:, cols],
-                in_=y_bf[:, PACK * h * 256 : PACK * (h + 1) * 256],
+                in_=y_bf[h][:].rearrange("p c n -> p (c n)"),
             )
 
         out_codes = tile([P, PLACES], U32, "out_codes")
@@ -172,16 +178,18 @@ def tile_picked_pnn8_none_po_kernel(
         out_rows = out_0.rearrange("(p t) j -> p t j", t=PACK)
         out_words = out_1[0].rearrange("p c r -> p (c r)").bitcast(I32)
 
-        def finish(c, pair_sum, first):
-            cols = slice(c * CHUNK, (c + 1) * CHUNK)
-            z_bf = tile([P, PACK * CHUNK], BF16, "z_bf%d" % c)
-            nc.vector.scalar_tensor_tensor(
-                out=z_bf[:].rearrange("p (n t) -> p n t", t=PACK),
-                in0=pair_sum[:, :, first : first + CHUNK].rearrange("p t n -> p n t"),
-                scalar=0.5,
-                in1=y_banks[c][:].rearrange("p t n -> p n t"),
-                op0=MULT, op1=MULT,
+        def z_values(c, pair_sum):
+            z_bf = tile([P, PACK * CHUNK], BF16, "z_bf%d" % c, "y_bf0" if c == 0 else None)
+            nc.vector.tensor_tensor(
+                z_bf[:].rearrange("p (c i t) -> p c t i", t=PACK, i=4),
+                pair_sum.rearrange("p t (c i) -> p c t i", i=4),
+                y_banks[c][:].rearrange("p t (c i) -> p c t i", i=4),
+                MULT,
             )
+            return z_bf
+
+        def products(c, z_bf):
+            cols = slice(c * CHUNK, (c + 1) * CHUNK)
             last = c == chunks - 1
             if last:
                 banks = [ps.tile([P, CHUNK], F32, name="last_bank%d" % t, tag="bank%d" % (3 + t)) for t in range(PACK)]
@@ -218,26 +226,71 @@ def tile_picked_pnn8_none_po_kernel(
                         nc.vector.tensor_copy(out=out_f32[:, t, :], in_=sums[t])
                     else:
                         nc.scalar.copy(out=out_f32[:, t, :], in_=sums[t])
-                nc.vector.tensor_copy(out=woven, in_=out_f32[:].rearrange("p t n -> p n t"))
+                nc.vector.tensor_copy(
+                    out=out_bf[:].rearrange("p (c i t) -> p c t i", t=PACK, i=4),
+                    in_=out_f32[:].rearrange("p t (c i) -> p c t i", i=4),
+                )
             else:
                 for t in range(PACK):
                     y_pass(t)
                     z_pass(t)
-                nc.scalar.copy(out=woven, in_=bank[:].rearrange("p t n -> p n t"))
                 nc.scalar.copy(out=out_f32[:], in_=bank[:])
+                nc.scalar.copy(out=woven, in_=bank[:].rearrange("p t n -> p n t"))
             nc.sync.dma_start(out=out_rows[:, :, cols], in_=out_f32[:])
+            return out_bf
+
+        def planes(c, out_bf):
+            cols = slice(c * CHUNK, (c + 1) * CHUNK)
             nc.vector.quantize_mx(out=out_codes[:, cols].bitcast(FP8X4), scales=out_plane[:, cols], in_=out_bf[:])
             nc.sync.dma_start(out=out_words[:, cols], in_=out_codes[:, cols].bitcast(I32))
 
-        for start, count in STRETCHES:
-            entries = slice(start // GROUP, (start + count) // GROUP)
-            pair_sum = tile([P, PACK, count], F32, "pair_sum%d" % start, "pair_sum")
-            first_pick = tile([P, PACK, count], F32, "first_pick%d" % start, {0: None, 256: "after_w1", 384: "z_bf0"}[start])
-            for t in range(PACK):
-                nc.vector.tensor_copy(first_pick[:, t, :], e_rows[t][:].indirect(p1_sb[:, entries]))
-                nc.vector.tensor_tensor(pair_sum[:, t, :], e_rows[t][:].indirect(p2_sb[:, entries]), first_pick[:, t, :], ADD)
-            for first in range(0, count, CHUNK):
-                finish((start + first) // CHUNK, pair_sum, first)
+        early_picks = tile([P, 5, half], F32, "early_picks")
+        late_picks = tile([P, 3, half], F32, "late_picks", "after_w1")
+        first_picks = {
+            (0, 0): early_picks[:, 0], (0, 1): early_picks[:, 1], (1, 0): early_picks[:, 2], (1, 1): early_picks[:, 3],
+            (2, 1): early_picks[:, 4], (2, 0): late_picks[:, 0], (3, 0): late_picks[:, 1], (3, 1): late_picks[:, 2],
+        }
+
+        def first_pick(t, h):
+            nc.vector.tensor_copy(first_picks[t, h], e_rows[t][:].indirect(p1_sb[:, entries(h * half, half)]))
+
+        def second_pick(out, t, start, count):
+            first = first_picks[t, start // half][:, start % half : start % half + count]
+            nc.vector.tensor_tensor(out, e_rows[t][:].indirect(p2_sb[:, entries(start, count)]), first, ADD)
+
+        sums_a = tile([P, PACK, half], F32, "sums_a")
+        for t in range(2):
+            first_pick(t, 0)
+            first_pick(t, 1)
+            second_pick(sums_a[:, t, :], t, 0, half)
+        first_pick(2, 1)
+        first_pick(2, 0)
+        first_pick(3, 0)
+        second_pick(sums_a[:, 2, :], 2, 0, half)
+        first_pick(3, 1)
+        second_pick(sums_a[:, 3, :], 3, 0, half)
+
+        z0 = z_values(0, sums_a[:, :, :CHUNK])
+        z1 = z_values(1, sums_a[:, :, CHUNK:])
+        o0 = products(0, z0)
+        sums_b = tile([P, PACK, CHUNK], F32, "sums_b", "y_bf0")
+        second_pick(sums_b[:, 0, :], 0, 2 * CHUNK, CHUNK)
+        o1 = products(1, z1)
+        for t in range(1, PACK):
+            second_pick(sums_b[:, t, :], t, 2 * CHUNK, CHUNK)
+        sums_c = tile([P, PACK, CHUNK], F32, "sums_c", "z_bf1")
+        second_pick(sums_c[:, 0, :], 0, 3 * CHUNK, CHUNK)
+        z2 = z_values(2, sums_b[:])
+        second_pick(sums_c[:, 1, :], 1, 3 * CHUNK, CHUNK)
+        o2 = products(2, z2)
+        for t in range(2, PACK):
+            second_pick(sums_c[:, t, :], t, 3 * CHUNK, CHUNK)
+        planes(0, o0)
+        z3 = z_values(3, sums_c[:])
+        planes(1, o1)
+        o3 = products(3, z3)
+        planes(2, o2)
+        planes(3, o3)
 
         plane_rows = out_2[0].rearrange("(q a) c -> a q c", a=PACK)
         for a in range(PACK):

@@ -43,20 +43,19 @@ def tile_picked_pnn8_none_po_kernel(
         def entries(start, count):
             return slice(start // GROUP, (start + count) // GROUP)
 
-        def load_scale_rows(queue, raw, scales):
+        def load_scale_rows(raw, scales):
             rows = scales[0].bitcast(I32)
-            queue.dma_start(out=raw.bitcast(I32), in_=rows.unsqueeze(1).to_broadcast([16, 8, rows.shape[1]]))
+            nc.sync.dma_start(out=raw.bitcast(I32), in_=rows.unsqueeze(1).to_broadcast([16, 8, rows.shape[1]]))
 
-        def deal_scales(name, raw, n, tag=None):
-            plane = tile([P, n, PACK, P], U8, name, tag)
+        def deal_scales(plane, raw):
             nc.vector.tensor_copy(
-                out=plane[:].rearrange("p w t (c i) -> p w c t i", i=16),
-                in_=raw.rearrange("p (w c i t) -> p w c t i", w=n, t=PACK, i=16),
+                out=plane.rearrange("p (w t c i) -> p w c t i", t=PACK, c=8, i=16),
+                in_=raw.rearrange("p (w c i t) -> p w c t i", t=PACK, c=8, i=16),
             )
-            flat = plane[:].rearrange("p w t m -> p (w t m)")
+
+        def mend_rows(queue, planes):
             for a in range(1, PACK):
-                nc.sync.dma_start(out=flat[a:P:QUADRANT, :].bitcast(I32), in_=flat[8 * a : P : QUADRANT, :].bitcast(I32))
-            return plane
+                queue.dma_start(out=planes[a:P:QUADRANT, :].bitcast(I32), in_=planes[8 * a : P : QUADRANT, :].bitcast(I32))
 
         def deal_words(name, raw):
             words = tile([P, PACK, 2 * P], U8, name)
@@ -71,40 +70,39 @@ def tile_picked_pnn8_none_po_kernel(
         p2_sb = sb.tile([P, PLACES // GROUP], U16, name="p2_sb")
         x_table = tile([P, FIELDS], U32, "x_table")
         x_scale_table = tile([P, FIELDS], U8, "x_scale_table")
-        w2_raw = tile([P, 2 * WIDTH], U8, "w2_raw", "before_w1")
-        w3_raw = tile([P, 2 * WIDTH], U8, "w3_raw")
-        w2_rows = tile([P, 1, WIDTH], U8, "w2_rows")
-        w3_rows = tile([P, WIDTH], U8, "w3_rows")
+        raw_words = {n: tile([P, 2 * WIDTH], U8, "w%d_raw" % n) for n in (2, 3, 4)}
+        w2_rows = tile([P, WIDTH], U8, "w2_rows")
+        w34_rows = tile([P, 2 * WIDTH], U8, "w34_rows")
+
+        def load_words(n, words):
+            nc.sync.dma_start(out=raw_words[n][:].bitcast(I32), in_=words[0].bitcast(I32))
 
         nc.sync.dma_start(offs_sb[:], offs)
-        load_scale_rows(nc.sync, x_scale_table[:], x_scales)
-        load_scale_rows(nc.sync, w2_rows[:, 0, :], w2_scales)
-        nc.sync.dma_start(out=w2_raw[:].bitcast(I32), in_=w2_words[0].bitcast(I32))
+        load_scale_rows(w2_rows[:], w2_scales)
+        load_scale_rows(x_scale_table[:], x_scales)
+        load_words(2, w2_words)
         nc.sync.dma_start(p1_sb[:], p1)
         nc.sync.dma_start(p2_sb[:], p2)
-        load_scale_rows(nc.sync, w3_rows[:], w3_scales)
         nc.sync.dma_start(out=x_table[:].bitcast(I32), in_=x_words[0].rearrange("p c r -> p (c r)").bitcast(I32))
-        nc.sync.dma_start(out=w3_raw[:].bitcast(I32), in_=w3_words[0].bitcast(I32))
+        load_words(3, w3_words)
+        load_words(4, w4_words)
+        load_scale_rows(w34_rows[:, :WIDTH], w3_scales)
+        load_scale_rows(w34_rows[:, WIDTH:], w4_scales)
 
         picked_rows = tile([P, PLACES], U8, "picked_rows")
-        x_plane = tile([P, PLACES], U8, "x_plane")
+        first_planes = tile([P, PLACES + WIDTH], U8, "first_planes")
+        x_plane = first_planes[:, :PLACES]
+        w2_plane = first_planes[:, PLACES:].rearrange("p (t m) -> p t m", t=PACK)
+        deal_scales(first_planes[:, PLACES:], w2_rows[:])
         nc.vector.tensor_copy(picked_rows[:], x_scale_table[:].indirect(offs_sb[:]))
-        nc.vector.tensor_copy(out=x_plane[:].bitcast(I32), in_=picked_rows[:].bitcast(I32))
-        for a in range(1, PACK):
-            nc.scalar.dma_start(
-                out=x_plane[a:P:QUADRANT, :].bitcast(I32), in_=picked_rows[8 * a : P : QUADRANT, :].bitcast(I32)
-            )
-        w2_plane = deal_scales("w2_plane", w2_rows[:, 0, :], 1)[:, 0]
-        w2_codes = deal_words("w2_codes", w2_raw[:])
+        nc.vector.tensor_copy(out=x_plane.bitcast(I32), in_=picked_rows[:].bitcast(I32))
+        mend_rows(nc.scalar, first_planes)
+        w2_codes = deal_words("w2_codes", raw_words[2][:])
 
-        w1_raw = tile([P, 2, PACK, WIDTH // 2], F32, "w1_raw", "before_w1")
+        w1_raw = tile([P, 2, PACK, WIDTH // 2], F32, "w1_raw", "picked_rows")
         w1_rows = w1.rearrange("(p j) (h c) -> h p j c", j=PACK, h=2)
         for h in range(2):
             nc.sync.dma_start(out=w1_raw[:, h], in_=w1_rows[h])
-        w4_bytes = tile([P, 3 * WIDTH], U8, "w4_bytes", "picked_rows")
-        w4_raw, w4_rows = w4_bytes[:, : 2 * WIDTH], w4_bytes[:, 2 * WIDTH :]
-        nc.sync.dma_start(out=w4_raw.bitcast(I32), in_=w4_words[0].bitcast(I32))
-        load_scale_rows(nc.sync, w4_rows, w4_scales)
 
         x_codes = tile([P, PLACES], U32, "x_codes")
         half = PLACES // 2
@@ -123,7 +121,7 @@ def tile_picked_pnn8_none_po_kernel(
         e_product(low[:], 0, slice(0, half))
         nc.scalar.activation(out=e_rows[0][:, :half], in_=low[:], func=COPY, scale=0.5)
         e_product(high[:], 0, slice(half, PLACES))
-        nc.vector.tensor_scalar_mul(e_rows[0][:, half:], high[:], 0.5)
+        nc.scalar.activation(out=e_rows[0][:, half:], in_=high[:], func=COPY, scale=0.5)
         e_banks = {}
         for t in range(1, PACK):
             e_banks[t] = ps.tile([P, PLACES], F32, name="e_bank%d" % t, tag="bank%d" % t)
@@ -131,10 +129,14 @@ def tile_picked_pnn8_none_po_kernel(
         for t in range(1, PACK - 1):
             nc.scalar.activation(out=e_rows[t][:], in_=e_banks[t][:], func=COPY, scale=0.5)
 
-        w3_codes = deal_words("w3_codes", w3_raw[:])
-        w3_plane = deal_scales("w3_plane", w3_rows[:], 1, "x_table")[:, 0]
-        w4_codes = deal_words("w4_codes", w4_raw)
-        w4_plane = deal_scales("w4_plane", w4_rows, 1)[:, 0]
+        w3_codes = deal_words("w3_codes", raw_words[3][:])
+        w4_codes = deal_words("w4_codes", raw_words[4][:])
+
+        last_planes = tile([P, 2 * WIDTH], U8, "last_planes")
+        deal_scales(last_planes[:], w34_rows[:])
+        mend_rows(nc.sync, last_planes)
+        w3_plane = last_planes[:, :WIDTH].rearrange("p (t m) -> p t m", t=PACK)
+        w4_plane = last_planes[:, WIDTH:].rearrange("p (t m) -> p t m", t=PACK)
 
         w1_bf = tile([P, PACK * WIDTH], BF16, "w1_bf", "after_w1")
         cast_out = w1_bf[:].rearrange("p (t m j) -> p m t j", t=PACK, j=PACK)
@@ -142,11 +144,42 @@ def tile_picked_pnn8_none_po_kernel(
             nc.scalar.copy(
                 out=cast_out[:, 64 * h : 64 * h + 64], in_=w1_raw[:, h].rearrange("p j (m t) -> p m t j", t=PACK)
             )
-        e_rows.append(tile([P, PLACES], F32, "e_row3", "before_w1"))
+        e_rows.append(tile([P, PLACES], F32, "e_row3", "picked_rows"))
         nc.scalar.activation(out=e_rows[3][:], in_=e_banks[3][:], func=COPY, scale=0.5)
+
+        early_picks = tile([P, 5, half], F32, "early_picks")
+        late_picks = tile([P, 3, half], F32, "late_picks", "after_w1")
+        first_picks = {
+            (0, 0): early_picks[:, 0], (1, 0): early_picks[:, 1], (2, 0): early_picks[:, 2], (0, 1): early_picks[:, 3],
+            (1, 1): early_picks[:, 4], (3, 0): late_picks[:, 0], (2, 1): late_picks[:, 1], (3, 1): late_picks[:, 2],
+        }
+
+        def first_pick(t, h):
+            nc.vector.tensor_copy(first_picks[t, h], e_rows[t][:].indirect(p1_sb[:, entries(h * half, half)]))
+
+        def second_pick(sums, t, h):
+            nc.vector.tensor_tensor(
+                sums[:, t, :], e_rows[t][:].indirect(p2_sb[:, entries(h * half, half)]), first_picks[t, h], ADD
+            )
+
+        sums_a = tile([P, PACK, half], F32, "sums_a", "sums")
+        first_pick(0, 0)
+        first_pick(1, 0)
+        second_pick(sums_a, 0, 0)
+        first_pick(2, 0)
+        second_pick(sums_a, 1, 0)
+        first_pick(0, 1)
+        second_pick(sums_a, 2, 0)
+        first_pick(1, 1)
+
         w1_codes = tile([P, WIDTH], U32, "w1_codes")
         w1_plane = tile([P, WIDTH], U8, "w1_plane")
         nc.vector.quantize_mx(out=w1_codes[:].bitcast(FP8X4), scales=w1_plane[:], in_=w1_bf[:])
+
+        first_pick(3, 0)
+        first_pick(2, 1)
+        second_pick(sums_a, 3, 0)
+        first_pick(3, 1)
 
         y_banks = []
         y_bf = [tile([P, 2, PACK * CHUNK], BF16, "y_bf%d" % h) for h in range(2)]
@@ -166,8 +199,9 @@ def tile_picked_pnn8_none_po_kernel(
                 in_=bank[:].rearrange("p t n -> p n t"),
             )
             y_banks.append(bank)
-        for h in range(2):
-            cols = slice(h * 256, (h + 1) * 256)
+
+        def quantise_y(h):
+            cols = slice(h * half, (h + 1) * half)
             nc.vector.quantize_mx(
                 out=y_codes[:, cols].bitcast(FP8X4), scales=y_plane[:, cols],
                 in_=y_bf[h][:].rearrange("p c n -> p (c n)"),
@@ -178,65 +212,74 @@ def tile_picked_pnn8_none_po_kernel(
         out_rows = out_0.rearrange("(p t) j -> p t j", t=PACK)
         out_words = out_1[0].rearrange("p c r -> p (c r)").bitcast(I32)
 
-        def z_values(c, pair_sum):
-            z_bf = tile([P, PACK * CHUNK], BF16, "z_bf%d" % c, "y_bf0" if c == 0 else None)
+        def z_values(c, sums):
+            z_bf = tile([P, PACK * CHUNK], BF16, "z_bf%d" % c)
             nc.vector.tensor_tensor(
                 z_bf[:].rearrange("p (c i t) -> p c t i", t=PACK, i=4),
-                pair_sum.rearrange("p t (c i) -> p c t i", i=4),
+                sums[:, :, c % 2 * CHUNK : (c % 2 + 1) * CHUNK].rearrange("p t (c i) -> p c t i", i=4),
                 y_banks[c][:].rearrange("p t (c i) -> p c t i", i=4),
                 MULT,
             )
             return z_bf
 
-        def products(c, z_bf):
-            cols = slice(c * CHUNK, (c + 1) * CHUNK)
-            last = c == chunks - 1
-            if last:
-                banks = [ps.tile([P, CHUNK], F32, name="last_bank%d" % t, tag="bank%d" % (3 + t)) for t in range(PACK)]
-                sums = [one[:] for one in banks]
-            else:
-                bank = ps.tile([P, PACK, CHUNK], F32, name="out_bank%d" % c, tag="bank%d" % c)
-                sums = [bank[:, t, :] for t in range(PACK)]
-
-            def y_pass(t):
-                nc.tensor.matmul_mx(
-                    out=sums[t], lhsT=w3_codes[:, t, :].bitcast(FP4X4), lhsT_scale=w3_plane[:, t, :],
-                    rhs=y_codes[:, cols].bitcast(FP8X4), rhs_scale=y_plane[:, cols], start=True, stop=False,
-                )
-
+        def quantise_z(c, z_bf):
             z_codes = tile([P, CHUNK], U32, "z_codes%d" % c)
             z_plane = tile([P, CHUNK], U8, "z_plane%d" % c)
-
-            def z_pass(t):
-                nc.tensor.matmul_mx(
-                    out=sums[t], lhsT=w4_codes[:, t, :].bitcast(FP4X4), lhsT_scale=w4_plane[:, t, :],
-                    rhs=z_codes[:].bitcast(FP8X4), rhs_scale=z_plane[:], start=False, stop=True,
-                )
-
             nc.vector.quantize_mx(out=z_codes[:].bitcast(FP8X4), scales=z_plane[:], in_=z_bf[:])
+            return z_codes, z_plane
+
+        def y_pass(out, c, t):
+            cols = slice(c * CHUNK, (c + 1) * CHUNK)
+            nc.tensor.matmul_mx(
+                out=out, lhsT=w3_codes[:, t, :].bitcast(FP4X4), lhsT_scale=w3_plane[:, t, :],
+                rhs=y_codes[:, cols].bitcast(FP8X4), rhs_scale=y_plane[:, cols], start=True, stop=False,
+            )
+
+        def z_pass(out, z, t):
+            nc.tensor.matmul_mx(
+                out=out, lhsT=w4_codes[:, t, :].bitcast(FP4X4), lhsT_scale=w4_plane[:, t, :],
+                rhs=z[0][:].bitcast(FP8X4), rhs_scale=z[1][:], start=False, stop=True,
+            )
+
+        def store_values(c, out_f32):
+            nc.sync.dma_start(out=out_rows[:, :, c * CHUNK : (c + 1) * CHUNK], in_=out_f32[:])
+
+        def one_bank_products(c, z):
+            bank = ps.tile([P, PACK, CHUNK], F32, name="out_bank%d" % c, tag="bank%d" % (PACK + c))
+            for t in range(PACK):
+                y_pass(bank[:, t, :], c, t)
+                z_pass(bank[:, t, :], z, t)
             out_bf = tile([P, PACK * CHUNK], BF16, "out_bf%d" % c)
-            woven = out_bf[:].rearrange("p (n t) -> p n t", t=PACK)
             out_f32 = tile([P, PACK, CHUNK], F32, "out_f32_%d" % c)
-            if last:
-                for t in range(PACK):
-                    y_pass(t)
-                for t in range(PACK):
-                    z_pass(t)
-                    if t % 2:
-                        nc.vector.tensor_copy(out=out_f32[:, t, :], in_=sums[t])
-                    else:
-                        nc.scalar.copy(out=out_f32[:, t, :], in_=sums[t])
-                nc.vector.tensor_copy(
-                    out=out_bf[:].rearrange("p (c i t) -> p c t i", t=PACK, i=4),
-                    in_=out_f32[:].rearrange("p t (c i) -> p c t i", i=4),
-                )
-            else:
-                for t in range(PACK):
-                    y_pass(t)
-                    z_pass(t)
-                nc.scalar.copy(out=out_f32[:], in_=bank[:])
-                nc.scalar.copy(out=woven, in_=bank[:].rearrange("p t n -> p n t"))
-            nc.sync.dma_start(out=out_rows[:, :, cols], in_=out_f32[:])
+            nc.scalar.copy(out=out_f32[:], in_=bank[:])
+            nc.scalar.copy(out=out_bf[:].rearrange("p (n t) -> p n t", t=PACK), in_=bank[:].rearrange("p t n -> p n t"))
+            store_values(c, out_f32)
+            return out_bf
+
+        def open_groups(c):
+            first = PACK * (c % 2)
+            banks = [ps.tile([P, CHUNK], F32, name="o%d_%d" % (c, t), tag="bank%d" % (first + t)) for t in range(PACK)]
+            for t in range(PACK):
+                y_pass(banks[t][:], c, t)
+            return banks
+
+        def close_groups(c, banks, z, on_vector):
+            out_f32 = tile([P, PACK, CHUNK], F32, "out_f32_%d" % c)
+            for t in range(PACK):
+                z_pass(banks[t][:], z, t)
+                if t in on_vector:
+                    nc.vector.tensor_copy(out=out_f32[:, t, :], in_=banks[t][:])
+                else:
+                    nc.scalar.copy(out=out_f32[:, t, :], in_=banks[t][:])
+            store_values(c, out_f32)
+            return out_f32
+
+        def weave(c, out_f32):
+            out_bf = tile([P, PACK * CHUNK], BF16, "out_bf%d" % c)
+            nc.vector.tensor_copy(
+                out=out_bf[:].rearrange("p (c i t) -> p c t i", t=PACK, i=4),
+                in_=out_f32[:].rearrange("p t (c i) -> p c t i", i=4),
+            )
             return out_bf
 
         def planes(c, out_bf):
@@ -244,51 +287,31 @@ def tile_picked_pnn8_none_po_kernel(
             nc.vector.quantize_mx(out=out_codes[:, cols].bitcast(FP8X4), scales=out_plane[:, cols], in_=out_bf[:])
             nc.sync.dma_start(out=out_words[:, cols], in_=out_codes[:, cols].bitcast(I32))
 
-        early_picks = tile([P, 5, half], F32, "early_picks")
-        late_picks = tile([P, 3, half], F32, "late_picks", "after_w1")
-        first_picks = {
-            (0, 0): early_picks[:, 0], (0, 1): early_picks[:, 1], (1, 0): early_picks[:, 2], (1, 1): early_picks[:, 3],
-            (2, 1): early_picks[:, 4], (2, 0): late_picks[:, 0], (3, 0): late_picks[:, 1], (3, 1): late_picks[:, 2],
-        }
-
-        def first_pick(t, h):
-            nc.vector.tensor_copy(first_picks[t, h], e_rows[t][:].indirect(p1_sb[:, entries(h * half, half)]))
-
-        def second_pick(out, t, start, count):
-            first = first_picks[t, start // half][:, start % half : start % half + count]
-            nc.vector.tensor_tensor(out, e_rows[t][:].indirect(p2_sb[:, entries(start, count)]), first, ADD)
-
-        sums_a = tile([P, PACK, half], F32, "sums_a")
-        for t in range(2):
-            first_pick(t, 0)
-            first_pick(t, 1)
-            second_pick(sums_a[:, t, :], t, 0, half)
-        first_pick(2, 1)
-        first_pick(2, 0)
-        first_pick(3, 0)
-        second_pick(sums_a[:, 2, :], 2, 0, half)
-        first_pick(3, 1)
-        second_pick(sums_a[:, 3, :], 3, 0, half)
-
-        z0 = z_values(0, sums_a[:, :, :CHUNK])
-        z1 = z_values(1, sums_a[:, :, CHUNK:])
-        o0 = products(0, z0)
-        sums_b = tile([P, PACK, CHUNK], F32, "sums_b", "y_bf0")
-        second_pick(sums_b[:, 0, :], 0, 2 * CHUNK, CHUNK)
-        o1 = products(1, z1)
-        for t in range(1, PACK):
-            second_pick(sums_b[:, t, :], t, 2 * CHUNK, CHUNK)
-        sums_c = tile([P, PACK, CHUNK], F32, "sums_c", "z_bf1")
-        second_pick(sums_c[:, 0, :], 0, 3 * CHUNK, CHUNK)
-        z2 = z_values(2, sums_b[:])
-        second_pick(sums_c[:, 1, :], 1, 3 * CHUNK, CHUNK)
-        o2 = products(2, z2)
-        for t in range(2, PACK):
-            second_pick(sums_c[:, t, :], t, 3 * CHUNK, CHUNK)
+        z0 = z_values(0, sums_a)
+        quantise_y(0)
+        z1 = z_values(1, sums_a)
+        zq0 = quantise_z(0, z0)
+        sums_b = tile([P, PACK, half], F32, "sums_b", "sums")
+        second_pick(sums_b, 0, 1)
+        zq1 = quantise_z(1, z1)
+        o0 = one_bank_products(0, zq0)
+        o1 = one_bank_products(1, zq1)
+        second_pick(sums_b, 1, 1)
+        quantise_y(1)
+        second_pick(sums_b, 2, 1)
+        second_pick(sums_b, 3, 1)
+        banks2 = open_groups(2)
+        z2 = z_values(2, sums_b)
+        z3 = z_values(3, sums_b)
+        banks3 = open_groups(3)
+        zq2 = quantise_z(2, z2)
         planes(0, o0)
-        z3 = z_values(3, sums_c[:])
+        zq3 = quantise_z(3, z3)
         planes(1, o1)
-        o3 = products(3, z3)
+        f2 = close_groups(2, banks2, zq2, ())
+        f3 = close_groups(3, banks3, zq3, (1, 3))
+        o2 = weave(2, f2)
+        o3 = weave(3, f3)
         planes(2, o2)
         planes(3, o3)
 

@@ -35,10 +35,14 @@ def tile_picked_pnn8_none_po_kernel(
 
     with ExitStack() as ctx:
         sb = ctx.enter_context(tc.tile_pool(name="sb", bufs=1))
+        reused = ctx.enter_context(tc.tile_pool(name="reused", bufs=1))
         ps = ctx.enter_context(tc.psum_pool(name="ps", bufs=1))
 
         def tile(shape, dtype, name, tag=None):
             return sb.tile(shape, dtype, name=name, tag=tag or name, align_bytes=64)
+
+        def placed(shape, dtype, name, offset):
+            return reused.tile(shape, dtype, name=name, align_bytes=64, offset=offset)
 
         def entries(start, count):
             return slice(start // GROUP, (start + count) // GROUP)
@@ -53,12 +57,11 @@ def tile_picked_pnn8_none_po_kernel(
                 in_=raw.rearrange("p (w c i t) -> p w c t i", t=PACK, c=8, i=16),
             )
 
-        def mend_rows(queue, planes):
+        def mend_rows(queues, planes):
             for a in range(1, PACK):
-                queue.dma_start(out=planes[a:P:QUADRANT, :].bitcast(I32), in_=planes[8 * a : P : QUADRANT, :].bitcast(I32))
+                queues[a - 1].dma_start(out=planes[a:P:QUADRANT, :].bitcast(I32), in_=planes[8 * a : P : QUADRANT, :].bitcast(I32))
 
-        def deal_words(name, raw):
-            words = tile([P, PACK, 2 * P], U8, name)
+        def deal_words(words, raw):
             nc.vector.tensor_copy(
                 out=words[:].bitcast(U16).rearrange("p t (c i) -> p c t i", i=8),
                 in_=raw.bitcast(U16).rearrange("p (c i t) -> p c t i", t=PACK, i=8),
@@ -70,36 +73,37 @@ def tile_picked_pnn8_none_po_kernel(
         p2_sb = sb.tile([P, PLACES // GROUP], U16, name="p2_sb")
         x_table = tile([P, FIELDS], U32, "x_table")
         x_scale_table = tile([P, FIELDS], U8, "x_scale_table")
-        raw_words = {n: tile([P, 2 * WIDTH], U8, "w%d_raw" % n) for n in (2, 3, 4)}
-        w2_rows = tile([P, WIDTH], U8, "w2_rows")
-        w34_rows = tile([P, 2 * WIDTH], U8, "w34_rows")
+        w2_raw = placed([P, 2 * WIDTH], U8, "w2_raw", 7 * WIDTH)
+        w2_rows = placed([P, WIDTH], U8, "w2_rows", WIDTH)
 
-        def load_words(n, words):
-            nc.sync.dma_start(out=raw_words[n][:].bitcast(I32), in_=words[0].bitcast(I32))
+        def load_words(raw, words):
+            nc.sync.dma_start(out=raw.bitcast(I32), in_=words[0].bitcast(I32))
 
         nc.sync.dma_start(offs_sb[:], offs)
         load_scale_rows(w2_rows[:], w2_scales)
         load_scale_rows(x_scale_table[:], x_scales)
-        load_words(2, w2_words)
+        load_words(w2_raw[:], w2_words)
         nc.sync.dma_start(p1_sb[:], p1)
         nc.sync.dma_start(p2_sb[:], p2)
         nc.sync.dma_start(out=x_table[:].bitcast(I32), in_=x_words[0].rearrange("p c r -> p (c r)").bitcast(I32))
-        load_words(3, w3_words)
-        load_words(4, w4_words)
-        load_scale_rows(w34_rows[:, :WIDTH], w3_scales)
-        load_scale_rows(w34_rows[:, WIDTH:], w4_scales)
 
-        picked_rows = tile([P, PLACES], U8, "picked_rows")
+        picked_rows = placed([P, PLACES], U8, "picked_rows", 0)
         first_planes = tile([P, PLACES + WIDTH], U8, "first_planes")
         x_plane = first_planes[:, :PLACES]
         w2_plane = first_planes[:, PLACES:].rearrange("p (t m) -> p t m", t=PACK)
         deal_scales(first_planes[:, PLACES:], w2_rows[:])
         nc.vector.tensor_copy(picked_rows[:], x_scale_table[:].indirect(offs_sb[:]))
         nc.vector.tensor_copy(out=x_plane.bitcast(I32), in_=picked_rows[:].bitcast(I32))
-        mend_rows(nc.scalar, first_planes)
-        w2_codes = deal_words("w2_codes", raw_words[2][:])
+        mend_rows((nc.sync, nc.scalar, nc.scalar), first_planes)
+        w2_codes = deal_words(placed([P, PACK, 2 * P], U8, "w2_codes", 0), w2_raw[:])
 
-        w1_raw = tile([P, 2, PACK, WIDTH // 2], F32, "w1_raw", "picked_rows")
+        w34_bytes = placed([P, 6 * WIDTH], U8, "w34_bytes", 2 * WIDTH)
+        w34_raw, w34_rows = w34_bytes[:, : 4 * WIDTH], w34_bytes[:, 4 * WIDTH :]
+        load_words(w34_raw[:, : 2 * WIDTH], w3_words)
+        load_words(w34_raw[:, 2 * WIDTH :], w4_words)
+        load_scale_rows(w34_rows[:, :WIDTH], w3_scales)
+        load_scale_rows(w34_rows[:, WIDTH:], w4_scales)
+        w1_raw = placed([P, 2, PACK, WIDTH // 2], F32, "w1_raw", 8 * WIDTH)
         w1_rows = w1.rearrange("(p j) (h c) -> h p j c", j=PACK, h=2)
         for h in range(2):
             nc.sync.dma_start(out=w1_raw[:, h], in_=w1_rows[h])
@@ -129,12 +133,12 @@ def tile_picked_pnn8_none_po_kernel(
         for t in range(1, PACK - 1):
             nc.scalar.activation(out=e_rows[t][:], in_=e_banks[t][:], func=COPY, scale=0.5)
 
-        w3_codes = deal_words("w3_codes", raw_words[3][:])
-        w4_codes = deal_words("w4_codes", raw_words[4][:])
+        w3_codes = deal_words(tile([P, PACK, 2 * P], U8, "w3_codes"), w34_raw[:, : 2 * WIDTH])
+        w4_codes = deal_words(tile([P, PACK, 2 * P], U8, "w4_codes"), w34_raw[:, 2 * WIDTH :])
 
         last_planes = tile([P, 2 * WIDTH], U8, "last_planes")
-        deal_scales(last_planes[:], w34_rows[:])
-        mend_rows(nc.sync, last_planes)
+        deal_scales(last_planes[:], w34_rows)
+        mend_rows((nc.sync, nc.sync, nc.sync), last_planes)
         w3_plane = last_planes[:, :WIDTH].rearrange("p (t m) -> p t m", t=PACK)
         w4_plane = last_planes[:, WIDTH:].rearrange("p (t m) -> p t m", t=PACK)
 
@@ -144,7 +148,7 @@ def tile_picked_pnn8_none_po_kernel(
             nc.scalar.copy(
                 out=cast_out[:, 64 * h : 64 * h + 64], in_=w1_raw[:, h].rearrange("p j (m t) -> p m t j", t=PACK)
             )
-        e_rows.append(tile([P, PLACES], F32, "e_row3", "picked_rows"))
+        e_rows.append(placed([P, PLACES], F32, "e_row3", 12 * WIDTH))
         nc.scalar.activation(out=e_rows[3][:], in_=e_banks[3][:], func=COPY, scale=0.5)
 
         early_picks = tile([P, 5, half], F32, "early_picks")
@@ -157,19 +161,18 @@ def tile_picked_pnn8_none_po_kernel(
         def first_pick(t, h):
             nc.vector.tensor_copy(first_picks[t, h], e_rows[t][:].indirect(p1_sb[:, entries(h * half, half)]))
 
-        def second_pick(sums, t, h):
-            nc.vector.tensor_tensor(
-                sums[:, t, :], e_rows[t][:].indirect(p2_sb[:, entries(h * half, half)]), first_picks[t, h], ADD
-            )
+        def second_pick(out, t, start, count):
+            first = first_picks[t, start // half][:, start % half : start % half + count]
+            nc.vector.tensor_tensor(out, e_rows[t][:].indirect(p2_sb[:, entries(start, count)]), first, ADD)
 
-        sums_a = tile([P, PACK, half], F32, "sums_a", "sums")
+        sums_a = tile([P, PACK, half], F32, "sums_a")
         first_pick(0, 0)
         first_pick(1, 0)
-        second_pick(sums_a, 0, 0)
+        second_pick(sums_a[:, 0, :], 0, 0, half)
         first_pick(2, 0)
-        second_pick(sums_a, 1, 0)
+        second_pick(sums_a[:, 1, :], 1, 0, half)
         first_pick(0, 1)
-        second_pick(sums_a, 2, 0)
+        second_pick(sums_a[:, 2, :], 2, 0, half)
         first_pick(1, 1)
 
         w1_codes = tile([P, WIDTH], U32, "w1_codes")
@@ -178,7 +181,7 @@ def tile_picked_pnn8_none_po_kernel(
 
         first_pick(3, 0)
         first_pick(2, 1)
-        second_pick(sums_a, 3, 0)
+        second_pick(sums_a[:, 3, :], 3, 0, half)
         first_pick(3, 1)
 
         y_banks = []
@@ -199,9 +202,8 @@ def tile_picked_pnn8_none_po_kernel(
                 in_=bank[:].rearrange("p t n -> p n t"),
             )
             y_banks.append(bank)
-
-        def quantise_y(h):
-            cols = slice(h * half, (h + 1) * half)
+        for h in range(2):
+            cols = slice(h * 256, (h + 1) * 256)
             nc.vector.quantize_mx(
                 out=y_codes[:, cols].bitcast(FP8X4), scales=y_plane[:, cols],
                 in_=y_bf[h][:].rearrange("p c n -> p (c n)"),
@@ -212,74 +214,65 @@ def tile_picked_pnn8_none_po_kernel(
         out_rows = out_0.rearrange("(p t) j -> p t j", t=PACK)
         out_words = out_1[0].rearrange("p c r -> p (c r)").bitcast(I32)
 
-        def z_values(c, sums):
-            z_bf = tile([P, PACK * CHUNK], BF16, "z_bf%d" % c)
+        def z_values(c, pair_sum):
+            z_bf = tile([P, PACK * CHUNK], BF16, "z_bf%d" % c, "y_bf0" if c == 0 else None)
             nc.vector.tensor_tensor(
                 z_bf[:].rearrange("p (c i t) -> p c t i", t=PACK, i=4),
-                sums[:, :, c % 2 * CHUNK : (c % 2 + 1) * CHUNK].rearrange("p t (c i) -> p c t i", i=4),
+                pair_sum.rearrange("p t (c i) -> p c t i", i=4),
                 y_banks[c][:].rearrange("p t (c i) -> p c t i", i=4),
                 MULT,
             )
             return z_bf
 
-        def quantise_z(c, z_bf):
+        def products(c, z_bf):
+            cols = slice(c * CHUNK, (c + 1) * CHUNK)
+            last = c == chunks - 1
+            if last:
+                banks = [ps.tile([P, CHUNK], F32, name="last_bank%d" % t, tag="bank%d" % (3 + t)) for t in range(PACK)]
+                sums = [one[:] for one in banks]
+            else:
+                bank = ps.tile([P, PACK, CHUNK], F32, name="out_bank%d" % c, tag="bank%d" % c)
+                sums = [bank[:, t, :] for t in range(PACK)]
+
+            def y_pass(t):
+                nc.tensor.matmul_mx(
+                    out=sums[t], lhsT=w3_codes[:, t, :].bitcast(FP4X4), lhsT_scale=w3_plane[:, t, :],
+                    rhs=y_codes[:, cols].bitcast(FP8X4), rhs_scale=y_plane[:, cols], start=True, stop=False,
+                )
+
             z_codes = tile([P, CHUNK], U32, "z_codes%d" % c)
             z_plane = tile([P, CHUNK], U8, "z_plane%d" % c)
+
+            def z_pass(t):
+                nc.tensor.matmul_mx(
+                    out=sums[t], lhsT=w4_codes[:, t, :].bitcast(FP4X4), lhsT_scale=w4_plane[:, t, :],
+                    rhs=z_codes[:].bitcast(FP8X4), rhs_scale=z_plane[:], start=False, stop=True,
+                )
+
             nc.vector.quantize_mx(out=z_codes[:].bitcast(FP8X4), scales=z_plane[:], in_=z_bf[:])
-            return z_codes, z_plane
-
-        def y_pass(out, c, t):
-            cols = slice(c * CHUNK, (c + 1) * CHUNK)
-            nc.tensor.matmul_mx(
-                out=out, lhsT=w3_codes[:, t, :].bitcast(FP4X4), lhsT_scale=w3_plane[:, t, :],
-                rhs=y_codes[:, cols].bitcast(FP8X4), rhs_scale=y_plane[:, cols], start=True, stop=False,
-            )
-
-        def z_pass(out, z, t):
-            nc.tensor.matmul_mx(
-                out=out, lhsT=w4_codes[:, t, :].bitcast(FP4X4), lhsT_scale=w4_plane[:, t, :],
-                rhs=z[0][:].bitcast(FP8X4), rhs_scale=z[1][:], start=False, stop=True,
-            )
-
-        def store_values(c, out_f32):
-            nc.sync.dma_start(out=out_rows[:, :, c * CHUNK : (c + 1) * CHUNK], in_=out_f32[:])
-
-        def one_bank_products(c, z):
-            bank = ps.tile([P, PACK, CHUNK], F32, name="out_bank%d" % c, tag="bank%d" % (PACK + c))
-            for t in range(PACK):
-                y_pass(bank[:, t, :], c, t)
-                z_pass(bank[:, t, :], z, t)
             out_bf = tile([P, PACK * CHUNK], BF16, "out_bf%d" % c)
+            woven = out_bf[:].rearrange("p (n t) -> p n t", t=PACK)
             out_f32 = tile([P, PACK, CHUNK], F32, "out_f32_%d" % c)
-            nc.scalar.copy(out=out_f32[:], in_=bank[:])
-            nc.scalar.copy(out=out_bf[:].rearrange("p (n t) -> p n t", t=PACK), in_=bank[:].rearrange("p t n -> p n t"))
-            store_values(c, out_f32)
-            return out_bf
-
-        def open_groups(c):
-            first = PACK * (c % 2)
-            banks = [ps.tile([P, CHUNK], F32, name="o%d_%d" % (c, t), tag="bank%d" % (first + t)) for t in range(PACK)]
-            for t in range(PACK):
-                y_pass(banks[t][:], c, t)
-            return banks
-
-        def close_groups(c, banks, z, on_vector):
-            out_f32 = tile([P, PACK, CHUNK], F32, "out_f32_%d" % c)
-            for t in range(PACK):
-                z_pass(banks[t][:], z, t)
-                if t in on_vector:
-                    nc.vector.tensor_copy(out=out_f32[:, t, :], in_=banks[t][:])
-                else:
-                    nc.scalar.copy(out=out_f32[:, t, :], in_=banks[t][:])
-            store_values(c, out_f32)
-            return out_f32
-
-        def weave(c, out_f32):
-            out_bf = tile([P, PACK * CHUNK], BF16, "out_bf%d" % c)
-            nc.vector.tensor_copy(
-                out=out_bf[:].rearrange("p (c i t) -> p c t i", t=PACK, i=4),
-                in_=out_f32[:].rearrange("p t (c i) -> p c t i", i=4),
-            )
+            if last:
+                for t in range(PACK):
+                    y_pass(t)
+                for t in range(PACK):
+                    z_pass(t)
+                    if t % 2:
+                        nc.vector.tensor_copy(out=out_f32[:, t, :], in_=sums[t])
+                    else:
+                        nc.scalar.copy(out=out_f32[:, t, :], in_=sums[t])
+                nc.vector.tensor_copy(
+                    out=out_bf[:].rearrange("p (c i t) -> p c t i", t=PACK, i=4),
+                    in_=out_f32[:].rearrange("p t (c i) -> p c t i", i=4),
+                )
+            else:
+                for t in range(PACK):
+                    y_pass(t)
+                    z_pass(t)
+                nc.scalar.copy(out=out_f32[:], in_=bank[:])
+                nc.scalar.copy(out=woven, in_=bank[:].rearrange("p t n -> p n t"))
+            nc.sync.dma_start(out=out_rows[:, :, cols], in_=out_f32[:])
             return out_bf
 
         def planes(c, out_bf):
@@ -287,31 +280,25 @@ def tile_picked_pnn8_none_po_kernel(
             nc.vector.quantize_mx(out=out_codes[:, cols].bitcast(FP8X4), scales=out_plane[:, cols], in_=out_bf[:])
             nc.sync.dma_start(out=out_words[:, cols], in_=out_codes[:, cols].bitcast(I32))
 
-        z0 = z_values(0, sums_a)
-        quantise_y(0)
-        z1 = z_values(1, sums_a)
-        zq0 = quantise_z(0, z0)
-        sums_b = tile([P, PACK, half], F32, "sums_b", "sums")
-        second_pick(sums_b, 0, 1)
-        zq1 = quantise_z(1, z1)
-        o0 = one_bank_products(0, zq0)
-        o1 = one_bank_products(1, zq1)
-        second_pick(sums_b, 1, 1)
-        quantise_y(1)
-        second_pick(sums_b, 2, 1)
-        second_pick(sums_b, 3, 1)
-        banks2 = open_groups(2)
-        z2 = z_values(2, sums_b)
-        z3 = z_values(3, sums_b)
-        banks3 = open_groups(3)
-        zq2 = quantise_z(2, z2)
+        z0 = z_values(0, sums_a[:, :, :CHUNK])
+        z1 = z_values(1, sums_a[:, :, CHUNK:])
+        o0 = products(0, z0)
+        sums_b = tile([P, PACK, CHUNK], F32, "sums_b", "y_bf0")
+        second_pick(sums_b[:, 0, :], 0, 2 * CHUNK, CHUNK)
+        o1 = products(1, z1)
+        for t in range(1, PACK):
+            second_pick(sums_b[:, t, :], t, 2 * CHUNK, CHUNK)
+        sums_c = tile([P, PACK, CHUNK], F32, "sums_c", "z_bf1")
+        second_pick(sums_c[:, 0, :], 0, 3 * CHUNK, CHUNK)
+        z2 = z_values(2, sums_b[:])
+        second_pick(sums_c[:, 1, :], 1, 3 * CHUNK, CHUNK)
+        o2 = products(2, z2)
+        for t in range(2, PACK):
+            second_pick(sums_c[:, t, :], t, 3 * CHUNK, CHUNK)
         planes(0, o0)
-        zq3 = quantise_z(3, z3)
+        z3 = z_values(3, sums_c[:])
         planes(1, o1)
-        f2 = close_groups(2, banks2, zq2, ())
-        f3 = close_groups(3, banks3, zq3, (1, 3))
-        o2 = weave(2, f2)
-        o3 = weave(3, f3)
+        o3 = products(3, z3)
         planes(2, o2)
         planes(3, o3)
 

@@ -80,8 +80,8 @@ def tile_picked_pnn8_none_po_kernel(
             nc.sync.dma_start(out=raw.bitcast(I32), in_=words[0].bitcast(I32))
 
         nc.sync.dma_start(offs_sb[:], offs)
-        load_scale_rows(w2_rows[:], w2_scales)
         load_scale_rows(x_scale_table[:], x_scales)
+        load_scale_rows(w2_rows[:], w2_scales)
         load_words(w2_raw[:], w2_words)
         nc.sync.dma_start(p1_sb[:], p1)
         nc.sync.dma_start(p2_sb[:], p2)
@@ -91,8 +91,8 @@ def tile_picked_pnn8_none_po_kernel(
         first_planes = tile([P, PLACES + WIDTH], U8, "first_planes")
         x_plane = first_planes[:, :PLACES]
         w2_plane = first_planes[:, PLACES:].rearrange("p (t m) -> p t m", t=PACK)
-        deal_scales(first_planes[:, PLACES:], w2_rows[:])
         nc.vector.tensor_copy(picked_rows[:], x_scale_table[:].indirect(offs_sb[:]))
+        deal_scales(first_planes[:, PLACES:], w2_rows[:])
         nc.vector.tensor_copy(out=x_plane.bitcast(I32), in_=picked_rows[:].bitcast(I32))
         mend_rows((nc.sync, nc.scalar, nc.scalar), first_planes)
         w2_codes = deal_words(placed([P, PACK, 2 * P], U8, "w2_codes", 0), w2_raw[:])
@@ -258,7 +258,7 @@ def tile_picked_pnn8_none_po_kernel(
                     y_pass(t)
                 for t in range(PACK):
                     z_pass(t)
-                    if t % 2:
+                    if t % 2 == 0:
                         nc.vector.tensor_copy(out=out_f32[:, t, :], in_=sums[t])
                     else:
                         nc.scalar.copy(out=out_f32[:, t, :], in_=sums[t])

@@ -142,7 +142,7 @@ def tile_picked_pnn8_none_po_kernel(
         w3_plane = last_planes[:, :WIDTH].rearrange("p (t m) -> p t m", t=PACK)
         w4_plane = last_planes[:, WIDTH:].rearrange("p (t m) -> p t m", t=PACK)
 
-        w1_bf = tile([P, PACK * WIDTH], BF16, "w1_bf", "after_w1")
+        w1_bf = tile([P, PACK * WIDTH], BF16, "w1_bf")
         cast_out = w1_bf[:].rearrange("p (t m j) -> p m t j", t=PACK, j=PACK)
         for h in range(2):
             nc.scalar.copy(
@@ -151,12 +151,8 @@ def tile_picked_pnn8_none_po_kernel(
         e_rows.append(placed([P, PLACES], F32, "e_row3", 12 * WIDTH))
         nc.scalar.activation(out=e_rows[3][:], in_=e_banks[3][:], func=COPY, scale=0.5)
 
-        early_picks = tile([P, 5, half], F32, "early_picks")
-        late_picks = tile([P, 3, half], F32, "late_picks", "after_w1")
-        first_picks = {
-            (0, 0): early_picks[:, 0], (1, 0): early_picks[:, 1], (2, 0): early_picks[:, 2], (0, 1): early_picks[:, 3],
-            (1, 1): early_picks[:, 4], (3, 0): late_picks[:, 0], (2, 1): late_picks[:, 1], (3, 1): late_picks[:, 2],
-        }
+        picks = tile([P, PACK, 2, half], F32, "picks")
+        first_picks = {(t, h): picks[:, t, h] for t in range(PACK) for h in range(2)}
 
         def first_pick(t, h):
             nc.vector.tensor_copy(first_picks[t, h], e_rows[t][:].indirect(p1_sb[:, entries(h * half, half)]))
@@ -166,23 +162,21 @@ def tile_picked_pnn8_none_po_kernel(
             nc.vector.tensor_tensor(out, e_rows[t][:].indirect(p2_sb[:, entries(start, count)]), first, ADD)
 
         sums_a = tile([P, PACK, half], F32, "sums_a")
-        first_pick(0, 0)
-        first_pick(1, 0)
-        second_pick(sums_a[:, 0, :], 0, 0, half)
-        first_pick(2, 0)
-        second_pick(sums_a[:, 1, :], 1, 0, half)
-        first_pick(0, 1)
-        second_pick(sums_a[:, 2, :], 2, 0, half)
-        first_pick(1, 1)
+        sums_b = tile([P, PACK, CHUNK], F32, "sums_b")
+        for t in range(PACK - 1):
+            first_pick(t, 0)
+            first_pick(t, 1)
+            second_pick(sums_a[:, t, :], t, 0, half)
+            second_pick(sums_b[:, t, :], t, 2 * CHUNK, CHUNK)
 
         w1_codes = tile([P, WIDTH], U32, "w1_codes")
         w1_plane = tile([P, WIDTH], U8, "w1_plane")
         nc.vector.quantize_mx(out=w1_codes[:].bitcast(FP8X4), scales=w1_plane[:], in_=w1_bf[:])
 
         first_pick(3, 0)
-        first_pick(2, 1)
-        second_pick(sums_a[:, 3, :], 3, 0, half)
         first_pick(3, 1)
+        second_pick(sums_a[:, 3, :], 3, 0, half)
+        second_pick(sums_b[:, 3, :], 3, 2 * CHUNK, CHUNK)
 
         y_banks = []
         y_bf = [tile([P, 2, PACK * CHUNK], BF16, "y_bf%d" % h) for h in range(2)]
@@ -202,8 +196,9 @@ def tile_picked_pnn8_none_po_kernel(
                 in_=bank[:].rearrange("p t n -> p n t"),
             )
             y_banks.append(bank)
-        for h in range(2):
-            cols = slice(h * 256, (h + 1) * 256)
+
+        def quantise_y(h):
+            cols = slice(h * half, (h + 1) * half)
             nc.vector.quantize_mx(
                 out=y_codes[:, cols].bitcast(FP8X4), scales=y_plane[:, cols],
                 in_=y_bf[h][:].rearrange("p c n -> p (c n)"),
@@ -215,7 +210,7 @@ def tile_picked_pnn8_none_po_kernel(
         out_words = out_1[0].rearrange("p c r -> p (c r)").bitcast(I32)
 
         def z_values(c, pair_sum):
-            z_bf = tile([P, PACK * CHUNK], BF16, "z_bf%d" % c, "y_bf0" if c == 0 else None)
+            z_bf = tile([P, PACK * CHUNK], BF16, "z_bf%d" % c)
             nc.vector.tensor_tensor(
                 z_bf[:].rearrange("p (c i t) -> p c t i", t=PACK, i=4),
                 pair_sum.rearrange("p t (c i) -> p c t i", i=4),
@@ -281,19 +276,16 @@ def tile_picked_pnn8_none_po_kernel(
             nc.sync.dma_start(out=out_words[:, cols], in_=out_codes[:, cols].bitcast(I32))
 
         z0 = z_values(0, sums_a[:, :, :CHUNK])
+        quantise_y(0)
         z1 = z_values(1, sums_a[:, :, CHUNK:])
         o0 = products(0, z0)
-        sums_b = tile([P, PACK, CHUNK], F32, "sums_b", "y_bf0")
-        second_pick(sums_b[:, 0, :], 0, 2 * CHUNK, CHUNK)
+        quantise_y(1)
         o1 = products(1, z1)
-        for t in range(1, PACK):
-            second_pick(sums_b[:, t, :], t, 2 * CHUNK, CHUNK)
+        z2 = z_values(2, sums_b[:])
         sums_c = tile([P, PACK, CHUNK], F32, "sums_c", "z_bf1")
         second_pick(sums_c[:, 0, :], 0, 3 * CHUNK, CHUNK)
-        z2 = z_values(2, sums_b[:])
-        second_pick(sums_c[:, 1, :], 1, 3 * CHUNK, CHUNK)
         o2 = products(2, z2)
-        for t in range(2, PACK):
+        for t in range(1, PACK):
             second_pick(sums_c[:, t, :], t, 3 * CHUNK, CHUNK)
         planes(0, o0)
         z3 = z_values(3, sums_c[:])

@@ -85,7 +85,10 @@ def tile_picked_pnn8_none_po_kernel(
         load_words(w2_raw[:], w2_words)
         nc.sync.dma_start(p1_sb[:], p1)
         nc.sync.dma_start(p2_sb[:], p2)
+        w34_rows = tile([P, 2 * WIDTH], U8, "w34_rows")
+        load_scale_rows(w34_rows[:, :WIDTH], w3_scales)
         nc.sync.dma_start(out=x_table[:].bitcast(I32), in_=x_words[0].rearrange("p c r -> p (c r)").bitcast(I32))
+        load_scale_rows(w34_rows[:, WIDTH:], w4_scales)
 
         picked_rows = placed([P, PLACES], U8, "picked_rows", 0)
         first_planes = tile([P, PLACES + WIDTH], U8, "first_planes")
@@ -97,16 +100,11 @@ def tile_picked_pnn8_none_po_kernel(
         mend_rows((nc.sync, nc.scalar, nc.scalar), first_planes)
         w2_codes = deal_words(placed([P, PACK, 2 * P], U8, "w2_codes", 0), w2_raw[:])
 
-        w34_bytes = placed([P, 6 * WIDTH], U8, "w34_bytes", 2 * WIDTH)
-        w34_raw, w34_rows = w34_bytes[:, : 4 * WIDTH], w34_bytes[:, 4 * WIDTH :]
+        w34_raw = placed([P, 4 * WIDTH], U8, "w34_raw", 4 * WIDTH)
         load_words(w34_raw[:, : 2 * WIDTH], w3_words)
         load_words(w34_raw[:, 2 * WIDTH :], w4_words)
-        load_scale_rows(w34_rows[:, :WIDTH], w3_scales)
-        load_scale_rows(w34_rows[:, WIDTH:], w4_scales)
-        w1_raw = placed([P, 2, PACK, WIDTH // 2], F32, "w1_raw", 8 * WIDTH)
-        w1_rows = w1.rearrange("(p j) (h c) -> h p j c", j=PACK, h=2)
-        for h in range(2):
-            nc.sync.dma_start(out=w1_raw[:, h], in_=w1_rows[h])
+        w1_raw = placed([P, PACK, WIDTH], F32, "w1_raw", 8 * WIDTH)
+        nc.sync.dma_start(out=w1_raw[:], in_=w1.rearrange("(p j) c -> p j c", j=PACK))
 
         x_codes = tile([P, PLACES], U32, "x_codes")
         half = PLACES // 2
@@ -137,17 +135,17 @@ def tile_picked_pnn8_none_po_kernel(
         w4_codes = deal_words(tile([P, PACK, 2 * P], U8, "w4_codes"), w34_raw[:, 2 * WIDTH :])
 
         last_planes = tile([P, 2 * WIDTH], U8, "last_planes")
-        deal_scales(last_planes[:], w34_rows)
+        for n in range(2):
+            deal_scales(last_planes[:, n * WIDTH : (n + 1) * WIDTH], w34_rows[:, n * WIDTH : (n + 1) * WIDTH])
         mend_rows((nc.sync, nc.sync, nc.sync), last_planes)
         w3_plane = last_planes[:, :WIDTH].rearrange("p (t m) -> p t m", t=PACK)
         w4_plane = last_planes[:, WIDTH:].rearrange("p (t m) -> p t m", t=PACK)
 
         w1_bf = tile([P, PACK * WIDTH], BF16, "w1_bf")
-        cast_out = w1_bf[:].rearrange("p (t m j) -> p m t j", t=PACK, j=PACK)
-        for h in range(2):
-            nc.scalar.copy(
-                out=cast_out[:, 64 * h : 64 * h + 64], in_=w1_raw[:, h].rearrange("p j (m t) -> p m t j", t=PACK)
-            )
+        nc.scalar.copy(
+            out=w1_bf[:].rearrange("p (t m j) -> p m j t", t=PACK, j=PACK),
+            in_=w1_raw[:].rearrange("p j (m t) -> p m j t", t=PACK),
+        )
         e_rows.append(placed([P, PLACES], F32, "e_row3", 12 * WIDTH))
         nc.scalar.activation(out=e_rows[3][:], in_=e_banks[3][:], func=COPY, scale=0.5)
 

@@ -51,8 +51,8 @@ def tile_picked_pnn8_none_po_kernel(
             rows = scales[0].bitcast(I32)
             nc.sync.dma_start(out=raw.bitcast(I32), in_=rows.unsqueeze(1).to_broadcast([16, 8, rows.shape[1]]))
 
-        def deal_scales(plane, raw):
-            nc.vector.tensor_copy(
+        def deal_scales(engine, plane, raw):
+            engine.tensor_copy(
                 out=plane.rearrange("p (w t c i) -> p w c t i", t=PACK, c=8, i=16),
                 in_=raw.rearrange("p (w c i t) -> p w c t i", t=PACK, c=8, i=16),
             )
@@ -80,7 +80,8 @@ def tile_picked_pnn8_none_po_kernel(
             nc.sync.dma_start(out=raw.bitcast(I32), in_=words[0].bitcast(I32))
 
         nc.sync.dma_start(offs_sb[:], offs)
-        load_scale_rows(x_scale_table[:], x_scales)
+        nc.vector.memset(x_scale_table[:].bitcast(I32), 0)
+        nc.sync.dma_start(out=x_scale_table[0:P:8, :].bitcast(I32), in_=x_scales[0].bitcast(I32))
         load_scale_rows(w2_rows[:], w2_scales)
         load_words(w2_raw[:], w2_words)
         nc.sync.dma_start(p1_sb[:], p1)
@@ -95,7 +96,7 @@ def tile_picked_pnn8_none_po_kernel(
         x_plane = first_planes[:, :PLACES]
         w2_plane = first_planes[:, PLACES:].rearrange("p (t m) -> p t m", t=PACK)
         nc.vector.tensor_copy(picked_rows[:], x_scale_table[:].indirect(offs_sb[:]))
-        deal_scales(first_planes[:, PLACES:], w2_rows[:])
+        deal_scales(nc.vector, first_planes[:, PLACES:], w2_rows[:])
         nc.vector.tensor_copy(out=x_plane.bitcast(I32), in_=picked_rows[:].bitcast(I32))
         mend_rows((nc.sync, nc.scalar, nc.scalar), first_planes)
         w2_codes = deal_words(placed([P, PACK, 2 * P], U8, "w2_codes", 0), w2_raw[:])
@@ -136,7 +137,7 @@ def tile_picked_pnn8_none_po_kernel(
 
         last_planes = tile([P, 2 * WIDTH], U8, "last_planes")
         for n in range(2):
-            deal_scales(last_planes[:, n * WIDTH : (n + 1) * WIDTH], w34_rows[:, n * WIDTH : (n + 1) * WIDTH])
+            deal_scales(nc.gpsimd, last_planes[:, n * WIDTH : (n + 1) * WIDTH], w34_rows[:, n * WIDTH : (n + 1) * WIDTH])
         mend_rows((nc.sync, nc.sync, nc.sync), last_planes)
         w3_plane = last_planes[:, :WIDTH].rearrange("p (t m) -> p t m", t=PACK)
         w4_plane = last_planes[:, WIDTH:].rearrange("p (t m) -> p t m", t=PACK)

@@ -73,11 +73,16 @@ def tile_picked_pnn8_none_po_kernel(
         p2_sb = sb.tile([P, PLACES // GROUP], U16, name="p2_sb")
         x_table = tile([P, FIELDS], U32, "x_table")
         x_scale_table = tile([P, FIELDS], U8, "x_scale_table")
-        w2_raw = placed([P, 2 * WIDTH], U8, "w2_raw", 7 * WIDTH)
+        w2_raw = placed([P, 2 * WIDTH], U8, "w2_raw", 19 * WIDTH)
         w2_rows = placed([P, WIDTH], U8, "w2_rows", WIDTH)
 
         def load_words(raw, words):
             nc.sync.dma_start(out=raw.bitcast(I32), in_=words[0].bitcast(I32))
+
+        warm_in = tile([P, 8], F32, "warm_in")
+        warm_out = tile([P, 8], F32, "warm_out")
+        nc.gpsimd.memset(warm_in[:], 0.0)
+        nc.scalar.activation(out=warm_out[:], in_=warm_in[:], func=COPY, scale=0.5)
 
         nc.sync.dma_start(offs_sb[:], offs)
         nc.vector.memset(x_scale_table[:].bitcast(I32), 0)
@@ -86,7 +91,7 @@ def tile_picked_pnn8_none_po_kernel(
         load_words(w2_raw[:], w2_words)
         nc.sync.dma_start(p1_sb[:], p1)
         nc.sync.dma_start(p2_sb[:], p2)
-        w34_rows = tile([P, 2 * WIDTH], U8, "w34_rows")
+        w34_rows = placed([P, 2 * WIDTH], U8, "w34_rows", 2 * WIDTH)
         load_scale_rows(w34_rows[:, :WIDTH], w3_scales)
         nc.sync.dma_start(out=x_table[:].bitcast(I32), in_=x_words[0].rearrange("p c r -> p (c r)").bitcast(I32))
         load_scale_rows(w34_rows[:, WIDTH:], w4_scales)
@@ -101,10 +106,10 @@ def tile_picked_pnn8_none_po_kernel(
         mend_rows((nc.sync, nc.scalar, nc.scalar), first_planes)
         w2_codes = deal_words(placed([P, PACK, 2 * P], U8, "w2_codes", 0), w2_raw[:])
 
-        w34_raw = placed([P, 4 * WIDTH], U8, "w34_raw", 4 * WIDTH)
+        w34_raw = placed([P, 4 * WIDTH], U8, "w34_raw", 16 * WIDTH)
         load_words(w34_raw[:, : 2 * WIDTH], w3_words)
         load_words(w34_raw[:, 2 * WIDTH :], w4_words)
-        w1_raw = placed([P, PACK, WIDTH], F32, "w1_raw", 8 * WIDTH)
+        w1_raw = placed([P, PACK, WIDTH], F32, "w1_raw", 20 * WIDTH)
         nc.sync.dma_start(out=w1_raw[:], in_=w1.rearrange("(p j) c -> p j c", j=PACK))
 
         x_codes = tile([P, PLACES], U32, "x_codes")
@@ -119,12 +124,11 @@ def tile_picked_pnn8_none_po_kernel(
             )
 
         e_rows = [tile([P, PLACES], F32, "e_row%d" % t) for t in range(PACK - 1)]
-        low = ps.tile([P, half], F32, name="e_low", tag="bank0")
-        high = ps.tile([P, half], F32, name="e_high", tag="bank7")
-        e_product(low[:], 0, slice(0, half))
-        nc.scalar.activation(out=e_rows[0][:, :half], in_=low[:], func=COPY, scale=0.5)
-        e_product(high[:], 0, slice(half, PLACES))
-        nc.scalar.activation(out=e_rows[0][:, half:], in_=high[:], func=COPY, scale=0.5)
+        for c in range(chunks):
+            cols = slice(c * CHUNK, (c + 1) * CHUNK)
+            piece = ps.tile([P, CHUNK], F32, name="e_piece%d" % c, tag="bank%d" % (PACK + c))
+            e_product(piece[:], 0, cols)
+            nc.scalar.activation(out=e_rows[0][:, cols], in_=piece[:], func=COPY, scale=0.5)
         e_banks = {}
         for t in range(1, PACK):
             e_banks[t] = ps.tile([P, PLACES], F32, name="e_bank%d" % t, tag="bank%d" % t)
@@ -137,7 +141,7 @@ def tile_picked_pnn8_none_po_kernel(
 
         last_planes = tile([P, 2 * WIDTH], U8, "last_planes")
         for n in range(2):
-            deal_scales(nc.gpsimd, last_planes[:, n * WIDTH : (n + 1) * WIDTH], w34_rows[:, n * WIDTH : (n + 1) * WIDTH])
+            deal_scales(nc.vector, last_planes[:, n * WIDTH : (n + 1) * WIDTH], w34_rows[:, n * WIDTH : (n + 1) * WIDTH])
         mend_rows((nc.sync, nc.sync, nc.sync), last_planes)
         w3_plane = last_planes[:, :WIDTH].rearrange("p (t m) -> p t m", t=PACK)
         w4_plane = last_planes[:, WIDTH:].rearrange("p (t m) -> p t m", t=PACK)
@@ -147,10 +151,10 @@ def tile_picked_pnn8_none_po_kernel(
             out=w1_bf[:].rearrange("p (t m j) -> p m j t", t=PACK, j=PACK),
             in_=w1_raw[:].rearrange("p j (m t) -> p m j t", t=PACK),
         )
-        e_rows.append(placed([P, PLACES], F32, "e_row3", 12 * WIDTH))
+        e_rows.append(placed([P, PLACES], F32, "e_row3", 24 * WIDTH))
         nc.scalar.activation(out=e_rows[3][:], in_=e_banks[3][:], func=COPY, scale=0.5)
 
-        picks = tile([P, PACK, 2, half], F32, "picks")
+        picks = placed([P, PACK, 2, half], F32, "picks", 2 * WIDTH)
         first_picks = {(t, h): picks[:, t, h] for t in range(PACK) for h in range(2)}
 
         def first_pick(t, h):

@@ -280,8 +280,8 @@ def tile_picked_pnn8_none_po_kernel(
 
         z0 = z_values(0, sums_a[:, :, :CHUNK])
         quantise_y(0)
-        z1 = z_values(1, sums_a[:, :, CHUNK:])
         o0 = products(0, z0)
+        z1 = z_values(1, sums_a[:, :, CHUNK:])
         quantise_y(1)
         o1 = products(1, z1)
         z2 = z_values(2, sums_b[:])

@@ -123,7 +123,7 @@ def tile_picked_pnn8_none_po_kernel(
                 rhs=x_codes[:, cols].bitcast(FP8X4), rhs_scale=x_plane[:, cols], start=True, stop=True,
             )
 
-        e_rows = [tile([P, PLACES], F32, "e_row%d" % t) for t in range(PACK - 1)]
+        e_rows = [tile([P, 2 * PLACES if t < 2 else PLACES], F32, "e_row%d" % t) for t in range(PACK - 1)]
         for c in range(chunks):
             cols = slice(c * CHUNK, (c + 1) * CHUNK)
             piece = ps.tile([P, CHUNK], F32, name="e_piece%d" % c, tag="bank%d" % (PACK + c))
@@ -134,7 +134,7 @@ def tile_picked_pnn8_none_po_kernel(
             e_banks[t] = ps.tile([P, PLACES], F32, name="e_bank%d" % t, tag="bank%d" % t)
             e_product(e_banks[t][:], t, slice(0, PLACES))
         for t in range(1, PACK - 1):
-            nc.scalar.activation(out=e_rows[t][:], in_=e_banks[t][:], func=COPY, scale=0.5)
+            nc.scalar.activation(out=e_rows[t][:, :PLACES], in_=e_banks[t][:], func=COPY, scale=0.5)
 
         w3_codes = deal_words(tile([P, PACK, 2 * P], U8, "w3_codes"), w34_raw[:, : 2 * WIDTH])
         w4_codes = deal_words(tile([P, PACK, 2 * P], U8, "w4_codes"), w34_raw[:, 2 * WIDTH :])
@@ -154,32 +154,32 @@ def tile_picked_pnn8_none_po_kernel(
         e_rows.append(placed([P, PLACES], F32, "e_row3", 24 * WIDTH))
         nc.scalar.activation(out=e_rows[3][:], in_=e_banks[3][:], func=COPY, scale=0.5)
 
-        picks = placed([P, PACK, 2, half], F32, "picks", 2 * WIDTH)
-        first_picks = {(t, h): picks[:, t, h] for t in range(PACK) for h in range(2)}
+        picks = placed([P, PACK, PLACES], F32, "picks", 2 * WIDTH)
+        sums = tile([P, PACK, PLACES], F32, "sums")
 
-        def first_pick(t, h):
-            nc.vector.tensor_copy(first_picks[t, h], e_rows[t][:].indirect(p1_sb[:, entries(h * half, half)]))
+        def first_pick(out, t, start, count):
+            nc.vector.tensor_copy(out, e_rows[t][:].indirect(p1_sb[:, entries(start, count)]))
 
-        def second_pick(out, t, start, count):
-            first = first_picks[t, start // half][:, start % half : start % half + count]
-            nc.vector.tensor_tensor(out, e_rows[t][:].indirect(p2_sb[:, entries(start, count)]), first, ADD)
+        def second_pick(first, t, start, count):
+            nc.vector.tensor_tensor(
+                sums[:, t, start : start + count], e_rows[t][:].indirect(p2_sb[:, entries(start, count)]), first, ADD
+            )
 
-        sums_a = tile([P, PACK, half], F32, "sums_a")
-        sums_b = tile([P, PACK, CHUNK], F32, "sums_b")
-        for t in range(PACK - 1):
-            first_pick(t, 0)
-            first_pick(t, 1)
-            second_pick(sums_a[:, t, :], t, 0, half)
-            second_pick(sums_b[:, t, :], t, 2 * CHUNK, CHUNK)
+        first_pick(picks[:, 0, :], 0, 0, PLACES)
+        first_pick(picks[:, 1, :], 1, 0, PLACES)
+        second_pick(picks[:, 0, :], 0, 0, PLACES)
+        first_pick(picks[:, 2, : 3 * CHUNK], 2, 0, 3 * CHUNK)
+        second_pick(picks[:, 1, :], 1, 0, PLACES)
+        second_pick(picks[:, 2, :half], 2, 0, half)
+        second_pick(picks[:, 2, half : 3 * CHUNK], 2, half, CHUNK)
 
         w1_codes = tile([P, WIDTH], U32, "w1_codes")
         w1_plane = tile([P, WIDTH], U8, "w1_plane")
         nc.vector.quantize_mx(out=w1_codes[:].bitcast(FP8X4), scales=w1_plane[:], in_=w1_bf[:])
 
-        first_pick(3, 0)
-        first_pick(3, 1)
-        second_pick(sums_a[:, 3, :], 3, 0, half)
-        second_pick(sums_b[:, 3, :], 3, 2 * CHUNK, CHUNK)
+        first_pick(picks[:, 3, : 3 * CHUNK], 3, 0, 3 * CHUNK)
+        second_pick(picks[:, 3, :half], 3, 0, half)
+        second_pick(picks[:, 3, half : 3 * CHUNK], 3, half, CHUNK)
 
         y_banks = []
         y_bf = [tile([P, 2, PACK * CHUNK], BF16, "y_bf%d" % h) for h in range(2)]
@@ -278,20 +278,24 @@ def tile_picked_pnn8_none_po_kernel(
             nc.vector.quantize_mx(out=out_codes[:, cols].bitcast(FP8X4), scales=out_plane[:, cols], in_=out_bf[:])
             nc.sync.dma_start(out=out_words[:, cols], in_=out_codes[:, cols].bitcast(I32))
 
-        z0 = z_values(0, sums_a[:, :, :CHUNK])
+        def pair_sums(c):
+            return sums[:, :, c * CHUNK : (c + 1) * CHUNK]
+
+        z0 = z_values(0, pair_sums(0))
         quantise_y(0)
         o0 = products(0, z0)
-        z1 = z_values(1, sums_a[:, :, CHUNK:])
+        z1 = z_values(1, pair_sums(1))
         quantise_y(1)
         o1 = products(1, z1)
-        z2 = z_values(2, sums_b[:])
-        sums_c = tile([P, PACK, CHUNK], F32, "sums_c", "z_bf1")
-        second_pick(sums_c[:, 0, :], 0, 3 * CHUNK, CHUNK)
+        z2 = z_values(2, pair_sums(2))
+        last_picks = tile([P, 2, CHUNK], F32, "last_picks", "z_bf1")
+        first_pick(last_picks[:, 0, :], 2, 3 * CHUNK, CHUNK)
         o2 = products(2, z2)
-        for t in range(1, PACK):
-            second_pick(sums_c[:, t, :], t, 3 * CHUNK, CHUNK)
+        first_pick(last_picks[:, 1, :], 3, 3 * CHUNK, CHUNK)
+        second_pick(last_picks[:, 0, :], 2, 3 * CHUNK, CHUNK)
+        second_pick(last_picks[:, 1, :], 3, 3 * CHUNK, CHUNK)
         planes(0, o0)
-        z3 = z_values(3, sums_c[:])
+        z3 = z_values(3, pair_sums(3))
         planes(1, o1)
         o3 = products(3, z3)
         planes(2, o2)

@@ -42,7 +42,7 @@ def tile_picked_pnn8_none_po_kernel(
             return sb.tile(shape, dtype, name=name, tag=tag or name, align_bytes=64)
 
         def placed(shape, dtype, name, offset):
-            return reused.tile(shape, dtype, name=name, align_bytes=64, offset=offset)
+            return reused.tile(shape, dtype, name=name, align_bytes=64, offset=16 * WIDTH + offset)
 
         def entries(start, count):
             return slice(start // GROUP, (start + count) // GROUP)
@@ -91,7 +91,7 @@ def tile_picked_pnn8_none_po_kernel(
         load_words(w2_raw[:], w2_words)
         nc.sync.dma_start(p1_sb[:], p1)
         nc.sync.dma_start(p2_sb[:], p2)
-        w34_rows = placed([P, 2 * WIDTH], U8, "w34_rows", 2 * WIDTH)
+        w34_rows = placed([P, 2 * WIDTH], U8, "w34_rows", 10 * WIDTH)
         load_scale_rows(w34_rows[:, :WIDTH], w3_scales)
         nc.sync.dma_start(out=x_table[:].bitcast(I32), in_=x_words[0].rearrange("p c r -> p (c r)").bitcast(I32))
         load_scale_rows(w34_rows[:, WIDTH:], w4_scales)
@@ -109,8 +109,10 @@ def tile_picked_pnn8_none_po_kernel(
         w34_raw = placed([P, 4 * WIDTH], U8, "w34_raw", 16 * WIDTH)
         load_words(w34_raw[:, : 2 * WIDTH], w3_words)
         load_words(w34_raw[:, 2 * WIDTH :], w4_words)
-        w1_raw = placed([P, PACK, WIDTH], F32, "w1_raw", 20 * WIDTH)
-        nc.sync.dma_start(out=w1_raw[:], in_=w1.rearrange("(p j) c -> p j c", j=PACK))
+        w1_rows = w1.rearrange("(p j) c -> p j c", j=PACK)
+        w1_raw = placed([P, 2, PACK, WIDTH // 2], F32, "w1_raw", 20 * WIDTH)
+        for h in range(2):
+            nc.sync.dma_start(out=w1_raw[:, h], in_=w1_rows[:, :, h * WIDTH // 2 : (h + 1) * WIDTH // 2])
 
         x_codes = tile([P, PLACES], U32, "x_codes")
         half = PLACES // 2
@@ -123,7 +125,8 @@ def tile_picked_pnn8_none_po_kernel(
                 rhs=x_codes[:, cols].bitcast(FP8X4), rhs_scale=x_plane[:, cols], start=True, stop=True,
             )
 
-        e_rows = [tile([P, 2 * PLACES if t < 2 else PLACES], F32, "e_row%d" % t) for t in range(PACK - 1)]
+        e_rows = [tile([P, 2 * PLACES], F32, "e_row%d" % t) for t in range(2)]
+        e_rows.append(tile([P, PLACES], F32, "e_row2"))
         for c in range(chunks):
             cols = slice(c * CHUNK, (c + 1) * CHUNK)
             piece = ps.tile([P, CHUNK], F32, name="e_piece%d" % c, tag="bank%d" % (PACK + c))
@@ -133,7 +136,7 @@ def tile_picked_pnn8_none_po_kernel(
         for t in range(1, PACK):
             e_banks[t] = ps.tile([P, PLACES], F32, name="e_bank%d" % t, tag="bank%d" % t)
             e_product(e_banks[t][:], t, slice(0, PLACES))
-        for t in range(1, PACK - 1):
+        for t in (1, 2):
             nc.scalar.activation(out=e_rows[t][:, :PLACES], in_=e_banks[t][:], func=COPY, scale=0.5)
 
         w3_codes = deal_words(tile([P, PACK, 2 * P], U8, "w3_codes"), w34_raw[:, : 2 * WIDTH])
@@ -147,15 +150,16 @@ def tile_picked_pnn8_none_po_kernel(
         w4_plane = last_planes[:, WIDTH:].rearrange("p (t m) -> p t m", t=PACK)
 
         w1_bf = tile([P, PACK * WIDTH], BF16, "w1_bf")
-        nc.scalar.copy(
-            out=w1_bf[:].rearrange("p (t m j) -> p m j t", t=PACK, j=PACK),
-            in_=w1_raw[:].rearrange("p j (m t) -> p m j t", t=PACK),
-        )
+        for h in range(2):
+            nc.scalar.copy(
+                out=w1_bf[:].rearrange("p (t h m j) -> p h m t j", t=PACK, h=2, j=PACK)[:, h],
+                in_=w1_raw[:, h].rearrange("p j (m t) -> p m t j", t=PACK),
+            )
         e_rows.append(placed([P, PLACES], F32, "e_row3", 24 * WIDTH))
         nc.scalar.activation(out=e_rows[3][:], in_=e_banks[3][:], func=COPY, scale=0.5)
 
-        picks = placed([P, PACK, PLACES], F32, "picks", 2 * WIDTH)
-        sums = tile([P, PACK, PLACES], F32, "sums")
+        picks = placed([P, 2, PLACES], F32, "picks", 9 * WIDTH)
+        sums = placed([P, PACK, PLACES], F32, "sums", 64 - 16 * WIDTH)
 
         def first_pick(out, t, start, count):
             nc.vector.tensor_copy(out, e_rows[t][:].indirect(p1_sb[:, entries(start, count)]))
@@ -165,26 +169,24 @@ def tile_picked_pnn8_none_po_kernel(
                 sums[:, t, start : start + count], e_rows[t][:].indirect(p2_sb[:, entries(start, count)]), first, ADD
             )
 
-        first_pick(picks[:, 0, :], 0, 0, PLACES)
-        first_pick(picks[:, 1, :], 1, 0, PLACES)
-        second_pick(picks[:, 0, :], 0, 0, PLACES)
-        first_pick(picks[:, 2, : 3 * CHUNK], 2, 0, 3 * CHUNK)
-        second_pick(picks[:, 1, :], 1, 0, PLACES)
-        second_pick(picks[:, 2, :half], 2, 0, half)
-        second_pick(picks[:, 2, half : 3 * CHUNK], 2, half, CHUNK)
+        for t in (0, 1):
+            first_pick(picks[:, t, :], t, 0, PLACES)
+        for t in (0, 1):
+            second_pick(picks[:, t, :], t, 0, PLACES)
 
         w1_codes = tile([P, WIDTH], U32, "w1_codes")
         w1_plane = tile([P, WIDTH], U8, "w1_plane")
         nc.vector.quantize_mx(out=w1_codes[:].bitcast(FP8X4), scales=w1_plane[:], in_=w1_bf[:])
 
-        first_pick(picks[:, 3, : 3 * CHUNK], 3, 0, 3 * CHUNK)
-        second_pick(picks[:, 3, :half], 3, 0, half)
-        second_pick(picks[:, 3, half : 3 * CHUNK], 3, half, CHUNK)
+        middle_picks = placed([P, 2, half], F32, "middle_picks", 28 * WIDTH)
+        for t in (2, 3):
+            first_pick(middle_picks[:, t - 2, :], t, 0, half)
+        second_pick(middle_picks[:, 0, :], 2, 0, half)
+        for c in range(2):
+            second_pick(middle_picks[:, 1, c * CHUNK : (c + 1) * CHUNK], 3, c * CHUNK, CHUNK)
 
         y_banks = []
         y_bf = [tile([P, 2, PACK * CHUNK], BF16, "y_bf%d" % h) for h in range(2)]
-        y_codes = tile([P, PLACES], U32, "y_codes")
-        y_plane = tile([P, PLACES], U8, "y_plane")
         for c in range(chunks):
             cols = slice(c * CHUNK, (c + 1) * CHUNK)
             bank = ps.tile([P, PACK, CHUNK], F32, name="y_bank%d" % c, tag="bank%d" % (PACK + c))
@@ -200,76 +202,77 @@ def tile_picked_pnn8_none_po_kernel(
             )
             y_banks.append(bank)
 
+        y_operands = {}
+
         def quantise_y(h):
-            cols = slice(h * half, (h + 1) * half)
-            nc.vector.quantize_mx(
-                out=y_codes[:, cols].bitcast(FP8X4), scales=y_plane[:, cols],
-                in_=y_bf[h][:].rearrange("p c n -> p (c n)"),
+            codes = tile([P, half], U32, "y_codes%d" % h)
+            plane = tile([P, half], U8, "y_plane%d" % h)
+            nc.vector.quantize_mx(out=codes[:].bitcast(FP8X4), scales=plane[:], in_=y_bf[h][:].rearrange("p c n -> p (c n)"))
+            for n in range(2):
+                cols = slice(n * CHUNK, (n + 1) * CHUNK)
+                y_operands[2 * h + n] = (codes[:, cols], plane[:, cols])
+
+        def z_values(c, z_bf):
+            nc.vector.tensor_tensor(
+                z_bf.rearrange("p (c i t) -> p c t i", t=PACK, i=4),
+                sums[:, :, c * CHUNK : (c + 1) * CHUNK].rearrange("p t (c i) -> p c t i", i=4),
+                y_banks[c][:].rearrange("p t (c i) -> p c t i", i=4),
+                MULT,
             )
+
+        z_operands = {}
+
+        def quantise_z(first, count, z_bf):
+            codes = tile([P, count * CHUNK], U32, "z_codes%d" % first)
+            plane = tile([P, count * CHUNK], U8, "z_plane%d" % first)
+            nc.vector.quantize_mx(out=codes[:].bitcast(FP8X4), scales=plane[:], in_=z_bf)
+            for n in range(count):
+                cols = slice(n * CHUNK, (n + 1) * CHUNK)
+                z_operands[first + n] = (codes[:, cols], plane[:, cols])
 
         out_codes = tile([P, PLACES], U32, "out_codes")
         out_plane = tile([P, PLACES], U8, "out_plane")
         out_rows = out_0.rearrange("(p t) j -> p t j", t=PACK)
         out_words = out_1[0].rearrange("p c r -> p (c r)").bitcast(I32)
 
-        def z_values(c, pair_sum):
-            z_bf = tile([P, PACK * CHUNK], BF16, "z_bf%d" % c)
-            nc.vector.tensor_tensor(
-                z_bf[:].rearrange("p (c i t) -> p c t i", t=PACK, i=4),
-                pair_sum.rearrange("p t (c i) -> p c t i", i=4),
-                y_banks[c][:].rearrange("p t (c i) -> p c t i", i=4),
-                MULT,
-            )
-            return z_bf
-
-        def products(c, z_bf):
-            cols = slice(c * CHUNK, (c + 1) * CHUNK)
+        def y_passes(c):
             last = c == chunks - 1
             if last:
-                banks = [ps.tile([P, CHUNK], F32, name="last_bank%d" % t, tag="bank%d" % (3 + t)) for t in range(PACK)]
-                sums = [one[:] for one in banks]
+                banks = [ps.tile([P, CHUNK], F32, name="last_bank%d" % t, tag="bank%d" % (3, 4, 5, 0)[t]) for t in range(PACK)]
+                sums_out = [one[:] for one in banks]
             else:
-                bank = ps.tile([P, PACK, CHUNK], F32, name="out_bank%d" % c, tag="bank%d" % c)
-                sums = [bank[:, t, :] for t in range(PACK)]
-
-            def y_pass(t):
+                banks = ps.tile([P, PACK, CHUNK], F32, name="out_bank%d" % c, tag="bank%d" % c)
+                sums_out = [banks[:, t, :] for t in range(PACK)]
+            for t in range(PACK):
                 nc.tensor.matmul_mx(
-                    out=sums[t], lhsT=w3_codes[:, t, :].bitcast(FP4X4), lhsT_scale=w3_plane[:, t, :],
-                    rhs=y_codes[:, cols].bitcast(FP8X4), rhs_scale=y_plane[:, cols], start=True, stop=False,
+                    out=sums_out[t], lhsT=w3_codes[:, t, :].bitcast(FP4X4), lhsT_scale=w3_plane[:, t, :],
+                    rhs=y_operands[c][0].bitcast(FP8X4), rhs_scale=y_operands[c][1], start=last or t == 0, stop=False,
                 )
+            return banks, sums_out
 
-            z_codes = tile([P, CHUNK], U32, "z_codes%d" % c)
-            z_plane = tile([P, CHUNK], U8, "z_plane%d" % c)
-
-            def z_pass(t):
-                nc.tensor.matmul_mx(
-                    out=sums[t], lhsT=w4_codes[:, t, :].bitcast(FP4X4), lhsT_scale=w4_plane[:, t, :],
-                    rhs=z_codes[:].bitcast(FP8X4), rhs_scale=z_plane[:], start=False, stop=True,
-                )
-
-            nc.vector.quantize_mx(out=z_codes[:].bitcast(FP8X4), scales=z_plane[:], in_=z_bf[:])
+        def products(c, opened):
+            banks, sums_out = opened
+            cols = slice(c * CHUNK, (c + 1) * CHUNK)
+            last = c == chunks - 1
             out_bf = tile([P, PACK * CHUNK], BF16, "out_bf%d" % c)
-            woven = out_bf[:].rearrange("p (n t) -> p n t", t=PACK)
             out_f32 = tile([P, PACK, CHUNK], F32, "out_f32_%d" % c)
+            for t in range(PACK):
+                nc.tensor.matmul_mx(
+                    out=sums_out[t], lhsT=w4_codes[:, t, :].bitcast(FP4X4), lhsT_scale=w4_plane[:, t, :],
+                    rhs=z_operands[c][0].bitcast(FP8X4), rhs_scale=z_operands[c][1], start=False, stop=last or t == PACK - 1,
+                )
+                if last and t % 2 == 0:
+                    nc.vector.tensor_copy(out=out_f32[:, t, :], in_=sums_out[t])
+                elif last:
+                    nc.scalar.copy(out=out_f32[:, t, :], in_=sums_out[t])
             if last:
-                for t in range(PACK):
-                    y_pass(t)
-                for t in range(PACK):
-                    z_pass(t)
-                    if t % 2 == 0:
-                        nc.vector.tensor_copy(out=out_f32[:, t, :], in_=sums[t])
-                    else:
-                        nc.scalar.copy(out=out_f32[:, t, :], in_=sums[t])
                 nc.vector.tensor_copy(
                     out=out_bf[:].rearrange("p (c i t) -> p c t i", t=PACK, i=4),
                     in_=out_f32[:].rearrange("p t (c i) -> p c t i", i=4),
                 )
             else:
-                for t in range(PACK):
-                    y_pass(t)
-                    z_pass(t)
-                nc.scalar.copy(out=out_f32[:], in_=bank[:])
-                nc.scalar.copy(out=woven, in_=bank[:].rearrange("p t n -> p n t"))
+                nc.scalar.copy(out=out_f32[:], in_=banks[:])
+                nc.scalar.copy(out=out_bf[:].rearrange("p (n t) -> p n t", t=PACK), in_=banks[:].rearrange("p t n -> p n t"))
             nc.sync.dma_start(out=out_rows[:, :, cols], in_=out_f32[:])
             return out_bf
 
@@ -278,26 +281,35 @@ def tile_picked_pnn8_none_po_kernel(
             nc.vector.quantize_mx(out=out_codes[:, cols].bitcast(FP8X4), scales=out_plane[:, cols], in_=out_bf[:])
             nc.sync.dma_start(out=out_words[:, cols], in_=out_codes[:, cols].bitcast(I32))
 
-        def pair_sums(c):
-            return sums[:, :, c * CHUNK : (c + 1) * CHUNK]
-
-        z0 = z_values(0, pair_sums(0))
         quantise_y(0)
-        o0 = products(0, z0)
-        z1 = z_values(1, pair_sums(1))
+        opened = [y_passes(0), y_passes(1)]
+        z_bf = [tile([P, PACK * CHUNK], BF16, "z_bf%d" % c) for c in range(chunks)]
+        z_values(0, z_bf[0][:])
+        z_values(1, z_bf[1][:])
+        quantise_z(0, 1, z_bf[0][:])
+        o0 = products(0, opened[0])
+        third_picks = tile([P, 2, CHUNK], F32, "third_picks", "w1_codes")
+        first_pick(third_picks[:, 0], 2, 2 * CHUNK, CHUNK)
+        quantise_z(1, 1, z_bf[1][:])
+        o1 = products(1, opened[1])
+        first_pick(third_picks[:, 1], 3, 2 * CHUNK, CHUNK)
+        for t in (2, 3):
+            second_pick(third_picks[:, t - 2], t, 2 * CHUNK, CHUNK)
         quantise_y(1)
-        o1 = products(1, z1)
-        z2 = z_values(2, pair_sums(2))
-        last_picks = tile([P, 2, CHUNK], F32, "last_picks", "z_bf1")
-        first_pick(last_picks[:, 0, :], 2, 3 * CHUNK, CHUNK)
-        o2 = products(2, z2)
-        first_pick(last_picks[:, 1, :], 3, 3 * CHUNK, CHUNK)
-        second_pick(last_picks[:, 0, :], 2, 3 * CHUNK, CHUNK)
-        second_pick(last_picks[:, 1, :], 3, 3 * CHUNK, CHUNK)
+        opened.extend([y_passes(2), y_passes(3)])
+        z_values(2, z_bf[2][:])
+        last_picks = tile([P, 2, CHUNK], F32, "last_picks", "z_codes1")
+        first_pick(last_picks[:, 0], 2, 3 * CHUNK, CHUNK)
+        quantise_z(2, 1, z_bf[2][:])
+        o2 = products(2, opened[2])
+        first_pick(last_picks[:, 1], 3, 3 * CHUNK, CHUNK)
+        for t in (2, 3):
+            second_pick(last_picks[:, t - 2], t, 3 * CHUNK, CHUNK)
         planes(0, o0)
-        z3 = z_values(3, pair_sums(3))
+        z_values(3, z_bf[3][:])
         planes(1, o1)
-        o3 = products(3, z3)
+        quantise_z(3, 1, z_bf[3][:])
+        o3 = products(3, opened[3])
         planes(2, o2)
         planes(3, o3)
 

@@ -47,9 +47,9 @@ def tile_picked_pnn8_none_po_kernel(
         def entries(start, count):
             return slice(start // GROUP, (start + count) // GROUP)
 
-        def load_scale_rows(raw, scales):
+        def load_scale_rows(queue, raw, scales):
             rows = scales[0].bitcast(I32)
-            nc.sync.dma_start(out=raw.bitcast(I32), in_=rows.unsqueeze(1).to_broadcast([16, 8, rows.shape[1]]))
+            queue.dma_start(out=raw.bitcast(I32), in_=rows.unsqueeze(1).to_broadcast([16, 8, rows.shape[1]]))
 
         def deal_scales(engine, plane, raw):
             engine.tensor_copy(
@@ -72,45 +72,49 @@ def tile_picked_pnn8_none_po_kernel(
         p1_sb = sb.tile([P, PLACES // GROUP], U16, name="p1_sb")
         p2_sb = sb.tile([P, PLACES // GROUP], U16, name="p2_sb")
         x_table = tile([P, FIELDS], U32, "x_table")
-        x_scale_table = tile([P, FIELDS], U8, "x_scale_table")
-        w2_raw = placed([P, 2 * WIDTH], U8, "w2_raw", 19 * WIDTH)
-        w2_rows = placed([P, WIDTH], U8, "w2_rows", WIDTH)
+        x_scale_table = placed([P, FIELDS], U8, "x_scale_table", 44 * WIDTH)
+        w2_raw = placed([P, 11 * WIDTH + 128], U8, "w2_raw", 15 * WIDTH - 64)
+        w2_rows = tile([P, WIDTH], U8, "w2_rows")[:]
 
-        def load_words(raw, words):
-            nc.sync.dma_start(out=raw.bitcast(I32), in_=words[0].bitcast(I32))
+        def load_words(queue, raw, words):
+            queue.dma_start(out=raw.bitcast(I32), in_=words[0].bitcast(I32))
+
+        nc.vector.memset(x_scale_table[:].bitcast(I32), 0)
+        nc.sync.dma_start(offs_sb[:], offs)
+        load_scale_rows(nc.scalar, w2_rows, w2_scales)
+        nc.sync.dma_start(p1_sb[:], p1)
+        load_words(nc.scalar, w2_raw[:, : 2 * WIDTH], w2_words)
+        nc.sync.dma_start(p2_sb[:], p2)
+        nc.sync.dma_start(out=x_scale_table[0:P:8, :].bitcast(I32), in_=x_scales[0].bitcast(I32))
+        nc.sync.dma_start(out=x_table[:].bitcast(I32), in_=x_words[0].rearrange("p c r -> p (c r)").bitcast(I32))
 
         warm_in = tile([P, 8], F32, "warm_in")
         warm_out = tile([P, 8], F32, "warm_out")
         nc.gpsimd.memset(warm_in[:], 0.0)
         nc.scalar.activation(out=warm_out[:], in_=warm_in[:], func=COPY, scale=0.5)
 
-        nc.sync.dma_start(offs_sb[:], offs)
-        nc.vector.memset(x_scale_table[:].bitcast(I32), 0)
-        nc.sync.dma_start(out=x_scale_table[0:P:8, :].bitcast(I32), in_=x_scales[0].bitcast(I32))
-        load_scale_rows(w2_rows[:], w2_scales)
-        load_words(w2_raw[:], w2_words)
-        nc.sync.dma_start(p1_sb[:], p1)
-        nc.sync.dma_start(p2_sb[:], p2)
-        w34_rows = placed([P, 2 * WIDTH], U8, "w34_rows", 10 * WIDTH)
-        load_scale_rows(w34_rows[:, :WIDTH], w3_scales)
-        nc.sync.dma_start(out=x_table[:].bitcast(I32), in_=x_words[0].rearrange("p c r -> p (c r)").bitcast(I32))
-        load_scale_rows(w34_rows[:, WIDTH:], w4_scales)
+        w2_planes = tile([P, WIDTH], U8, "w2_planes")
+        w2_plane = w2_planes[:].rearrange("p (t m) -> p t m", t=PACK)
+        deal_scales(nc.vector, w2_planes[:], w2_rows)
+        mend_rows((nc.scalar, nc.scalar, nc.scalar), w2_planes)
 
-        picked_rows = placed([P, PLACES], U8, "picked_rows", 0)
-        first_planes = tile([P, PLACES + WIDTH], U8, "first_planes")
-        x_plane = first_planes[:, :PLACES]
-        w2_plane = first_planes[:, PLACES:].rearrange("p (t m) -> p t m", t=PACK)
+        picked_rows = tile([P, PLACES], U8, "picked_rows")
+        x_plane = tile([P, PLACES], U8, "x_plane")
+        nc.gpsimd.memset(x_plane[:].bitcast(I32), 0)
         nc.vector.tensor_copy(picked_rows[:], x_scale_table[:].indirect(offs_sb[:]))
-        deal_scales(nc.vector, first_planes[:, PLACES:], w2_rows[:])
-        nc.vector.tensor_copy(out=x_plane.bitcast(I32), in_=picked_rows[:].bitcast(I32))
-        mend_rows((nc.sync, nc.scalar, nc.scalar), first_planes)
-        w2_codes = deal_words(placed([P, PACK, 2 * P], U8, "w2_codes", 0), w2_raw[:])
+        for a in range(PACK):
+            queue = nc.scalar if a % 2 else nc.sync
+            queue.dma_start(out=x_plane[a:P:QUADRANT, :].bitcast(I32), in_=picked_rows[8 * a : P : QUADRANT, :].bitcast(I32))
+        w2_codes = deal_words(placed([P, PACK, 2 * P], U8, "w2_codes", 47 * WIDTH), w2_raw[:, : 2 * WIDTH])
 
-        w34_raw = placed([P, 4 * WIDTH], U8, "w34_raw", 16 * WIDTH)
-        load_words(w34_raw[:, : 2 * WIDTH], w3_words)
-        load_words(w34_raw[:, 2 * WIDTH :], w4_words)
+        w3_raw = placed([P, 2 * WIDTH], U8, "w3_raw", 15 * WIDTH)
+        w4_raw = placed([P, 4 * WIDTH], U8, "w4_raw", 11 * WIDTH)
+        load_words(nc.sync, w3_raw[:], w3_words)
+        load_scale_rows(nc.sync, w4_raw[:, 2 * WIDTH : 3 * WIDTH], w3_scales)
+        load_scale_rows(nc.sync, w4_raw[:, 3 * WIDTH :], w4_scales)
+        load_words(nc.sync, w4_raw[:, : 2 * WIDTH], w4_words)
         w1_rows = w1.rearrange("(p j) c -> p j c", j=PACK)
-        w1_raw = placed([P, 2, PACK, WIDTH // 2], F32, "w1_raw", 20 * WIDTH)
+        w1_raw = placed([P, 2, PACK, WIDTH // 2], F32, "w1_raw", 26 * WIDTH)
         for h in range(2):
             nc.sync.dma_start(out=w1_raw[:, h], in_=w1_rows[:, :, h * WIDTH // 2 : (h + 1) * WIDTH // 2])
 
@@ -139,13 +143,19 @@ def tile_picked_pnn8_none_po_kernel(
         for t in (1, 2):
             nc.scalar.activation(out=e_rows[t][:, :PLACES], in_=e_banks[t][:], func=COPY, scale=0.5)
 
-        w3_codes = deal_words(tile([P, PACK, 2 * P], U8, "w3_codes"), w34_raw[:, : 2 * WIDTH])
-        w4_codes = deal_words(tile([P, PACK, 2 * P], U8, "w4_codes"), w34_raw[:, 2 * WIDTH :])
+        def deal_words_as_bytes(words, raw):
+            nc.gpsimd.tensor_copy(
+                out=words[:].rearrange("p t (m b) -> p m t b", b=2),
+                in_=raw.rearrange("p (m t b) -> p m t b", t=PACK, b=2),
+            )
+            return words
 
         last_planes = tile([P, 2 * WIDTH], U8, "last_planes")
-        for n in range(2):
-            deal_scales(nc.vector, last_planes[:, n * WIDTH : (n + 1) * WIDTH], w34_rows[:, n * WIDTH : (n + 1) * WIDTH])
+        deal_scales(nc.gpsimd, last_planes[:, :WIDTH], w4_raw[:, 2 * WIDTH : 3 * WIDTH])
+        w3_codes = deal_words(tile([P, PACK, 2 * P], U8, "w3_codes"), w3_raw[:])
+        deal_scales(nc.gpsimd, last_planes[:, WIDTH:], w4_raw[:, 3 * WIDTH :])
         mend_rows((nc.sync, nc.sync, nc.sync), last_planes)
+        w4_codes = deal_words_as_bytes(tile([P, PACK, 2 * P], U8, "w4_codes"), w4_raw[:, : 2 * WIDTH])
         w3_plane = last_planes[:, :WIDTH].rearrange("p (t m) -> p t m", t=PACK)
         w4_plane = last_planes[:, WIDTH:].rearrange("p (t m) -> p t m", t=PACK)
 
@@ -155,11 +165,11 @@ def tile_picked_pnn8_none_po_kernel(
                 out=w1_bf[:].rearrange("p (t h m j) -> p h m t j", t=PACK, h=2, j=PACK)[:, h],
                 in_=w1_raw[:, h].rearrange("p j (m t) -> p m t j", t=PACK),
             )
-        e_rows.append(placed([P, PLACES], F32, "e_row3", 24 * WIDTH))
+        e_rows.append(placed([P, PLACES], F32, "e_row3", 30 * WIDTH))
         nc.scalar.activation(out=e_rows[3][:], in_=e_banks[3][:], func=COPY, scale=0.5)
 
-        picks = placed([P, 2, PLACES], F32, "picks", 9 * WIDTH)
-        sums = placed([P, PACK, PLACES], F32, "sums", 64 - 16 * WIDTH)
+        picks = placed([P, 2, PLACES], F32, "picks", 17 * WIDTH - 64)
+        sums = placed([P, PACK, PLACES], F32, "sums", 64 - 5 * WIDTH)
 
         def first_pick(out, t, start, count):
             nc.vector.tensor_copy(out, e_rows[t][:].indirect(p1_sb[:, entries(start, count)]))
@@ -178,7 +188,7 @@ def tile_picked_pnn8_none_po_kernel(
         w1_plane = tile([P, WIDTH], U8, "w1_plane")
         nc.vector.quantize_mx(out=w1_codes[:].bitcast(FP8X4), scales=w1_plane[:], in_=w1_bf[:])
 
-        middle_picks = placed([P, 2, half], F32, "middle_picks", 28 * WIDTH)
+        middle_picks = placed([P, 2, half], F32, "middle_picks", 34 * WIDTH)
         for t in (2, 3):
             first_pick(middle_picks[:, t - 2, :], t, 0, half)
         second_pick(middle_picks[:, 0, :], 2, 0, half)

@@ -162,8 +162,8 @@ def tile_picked_pnn8_none_po_kernel(
         w1_bf = tile([P, PACK * WIDTH], BF16, "w1_bf")
         for h in range(2):
             nc.scalar.copy(
-                out=w1_bf[:].rearrange("p (t h m j) -> p h m t j", t=PACK, h=2, j=PACK)[:, h],
-                in_=w1_raw[:, h].rearrange("p j (m t) -> p m t j", t=PACK),
+                out=w1_bf[:].rearrange("p (t h m j) -> p h m j t", t=PACK, h=2, j=PACK)[:, h],
+                in_=w1_raw[:, h].rearrange("p j (m t) -> p m j t", t=PACK),
             )
         e_rows.append(placed([P, PLACES], F32, "e_row3", 30 * WIDTH))
         nc.scalar.activation(out=e_rows[3][:], in_=e_banks[3][:], func=COPY, scale=0.5)
@@ -207,8 +207,8 @@ def tile_picked_pnn8_none_po_kernel(
                     rhs=x_codes[:, cols].bitcast(FP8X4), rhs_scale=x_plane[:, cols], start=True, stop=True,
                 )
             nc.scalar.copy(
-                out=y_bf[c // 2][:, c % 2, :].rearrange("p (n t) -> p n t", t=PACK),
-                in_=bank[:].rearrange("p t n -> p n t"),
+                out=y_bf[c // 2][:, c % 2, :].rearrange("p (c i t) -> p c t i", t=PACK, i=4),
+                in_=bank[:].rearrange("p t (c i) -> p c t i", i=4),
             )
             y_banks.append(bank)
 
@@ -282,7 +282,10 @@ def tile_picked_pnn8_none_po_kernel(
                 )
             else:
                 nc.scalar.copy(out=out_f32[:], in_=banks[:])
-                nc.scalar.copy(out=out_bf[:].rearrange("p (n t) -> p n t", t=PACK), in_=banks[:].rearrange("p t n -> p n t"))
+                nc.scalar.copy(
+                    out=out_bf[:].rearrange("p (c i t) -> p c t i", t=PACK, i=4),
+                    in_=banks[:].rearrange("p t (c i) -> p c t i", i=4),
+                )
             nc.sync.dma_start(out=out_rows[:, :, cols], in_=out_f32[:])
             return out_bf
 

@@ -88,11 +88,6 @@ def tile_picked_pnn8_none_po_kernel(
         nc.sync.dma_start(out=x_scale_table[0:P:8, :].bitcast(I32), in_=x_scales[0].bitcast(I32))
         nc.sync.dma_start(out=x_table[:].bitcast(I32), in_=x_words[0].rearrange("p c r -> p (c r)").bitcast(I32))
 
-        warm_in = tile([P, 8], F32, "warm_in")
-        warm_out = tile([P, 8], F32, "warm_out")
-        nc.gpsimd.memset(warm_in[:], 0.0)
-        nc.scalar.activation(out=warm_out[:], in_=warm_in[:], func=COPY, scale=0.5)
-
         w2_planes = tile([P, WIDTH], U8, "w2_planes")
         w2_plane = w2_planes[:].rearrange("p (t m) -> p t m", t=PACK)
         deal_scales(nc.vector, w2_planes[:], w2_rows)

@@ -20,8 +20,10 @@ FIELDS = 2048
 PLACES = 512
 WIDTH = 512
 CHUNK = 128
+HALF = PLACES // 2
 GROUP = 16
 QUADRANT = 32
+TOUCH = 64
 
 FLOPS = 4 * 2 * 512 * 512 * 512
 
@@ -38,14 +40,20 @@ def tile_picked_pnn8_none_po_kernel(
         reused = ctx.enter_context(tc.tile_pool(name="reused", bufs=1))
         ps = ctx.enter_context(tc.psum_pool(name="ps", bufs=1))
 
-        def tile(shape, dtype, name, tag=None):
-            return sb.tile(shape, dtype, name=name, tag=tag or name, align_bytes=64)
+        def tile(shape, dtype, name):
+            return sb.tile(shape, dtype, name=name, align_bytes=64)
 
         def placed(shape, dtype, name, offset):
-            return reused.tile(shape, dtype, name=name, align_bytes=64, offset=16 * WIDTH + offset)
+            return reused.tile(shape, dtype, name=name, align_bytes=64, offset=offset)
+
+        def bank(shape, name, number):
+            return ps.tile(shape, F32, name=name, tag="bank%d" % number)
 
         def entries(start, count):
             return slice(start // GROUP, (start + count) // GROUP)
+
+        def load_words(queue, raw, words):
+            queue.dma_start(out=raw.bitcast(I32), in_=words[0].bitcast(I32))
 
         def load_scale_rows(queue, raw, scales):
             rows = scales[0].bitcast(I32)
@@ -57,66 +65,89 @@ def tile_picked_pnn8_none_po_kernel(
                 in_=raw.rearrange("p (w c i t) -> p w c t i", t=PACK, c=8, i=16),
             )
 
-        def mend_rows(queues, planes):
-            for a in range(1, PACK):
-                queues[a - 1].dma_start(out=planes[a:P:QUADRANT, :].bitcast(I32), in_=planes[8 * a : P : QUADRANT, :].bitcast(I32))
-
-        def deal_words(words, raw):
-            nc.vector.tensor_copy(
+        def deal_words(copy, words, raw):
+            copy(
                 out=words[:].bitcast(U16).rearrange("p t (c i) -> p c t i", i=8),
                 in_=raw.bitcast(U16).rearrange("p (c i t) -> p c t i", t=PACK, i=8),
             )
             return words
 
+        def mend_rows(queue, planes):
+            for a in range(1, PACK):
+                queue.dma_start(out=planes[a:P:QUADRANT, :].bitcast(I32), in_=planes[8 * a : P : QUADRANT, :].bitcast(I32))
+
+        def woven(bf):
+            return bf.rearrange("p (c i t) -> p c t i", t=PACK, i=4)
+
+        def sliced(f32):
+            return f32.rearrange("p t (c i) -> p c t i", i=4)
+
+        sums_at = 0
+        late_at = sums_at + 4 * PACK * PLACES - TOUCH
+        w2_raw_at = late_at + 2 * WIDTH - TOUCH
+        w1_raw_at = w2_raw_at + 2 * WIDTH - TOUCH
+        table_at = w1_raw_at + 4 * PACK * WIDTH
+        w2_codes_at = table_at + FIELDS - TOUCH
+        late_words_at = w2_codes_at + 2 * WIDTH
+        picked_rows_at = late_words_at + 4 * WIDTH - TOUCH
+
         offs_sb = sb.tile([P, PLACES // GROUP], U16, name="offs_sb")
         p1_sb = sb.tile([P, PLACES // GROUP], U16, name="p1_sb")
         p2_sb = sb.tile([P, PLACES // GROUP], U16, name="p2_sb")
         x_table = tile([P, FIELDS], U32, "x_table")
-        x_scale_table = placed([P, FIELDS], U8, "x_scale_table", 44 * WIDTH)
-        w2_raw = placed([P, 11 * WIDTH + 128], U8, "w2_raw", 15 * WIDTH - 64)
-        w2_rows = tile([P, WIDTH], U8, "w2_rows")[:]
-
-        def load_words(queue, raw, words):
-            queue.dma_start(out=raw.bitcast(I32), in_=words[0].bitcast(I32))
+        x_scale_table = placed([P, FIELDS], U8, "x_scale_table", table_at)
+        w2_raw = placed([P, 2 * WIDTH], U8, "w2_raw", w2_raw_at)
+        w2_rows = tile([P, WIDTH], U8, "w2_rows")
 
         nc.vector.memset(x_scale_table[:].bitcast(I32), 0)
         nc.sync.dma_start(offs_sb[:], offs)
-        load_scale_rows(nc.scalar, w2_rows, w2_scales)
+        w2_pairs = w2_scales[0].bitcast(I32).rearrange("(m b) c -> b m c", b=2)
+        for b in range(2):
+            nc.scalar.dma_start(out=w2_rows[b:P:2, :].bitcast(I32), in_=w2_pairs[b].unsqueeze(1).to_broadcast([8, 8, WIDTH // 4]))
         nc.sync.dma_start(p1_sb[:], p1)
-        load_words(nc.scalar, w2_raw[:, : 2 * WIDTH], w2_words)
+        load_words(nc.scalar, w2_raw[:], w2_words)
         nc.sync.dma_start(p2_sb[:], p2)
         nc.sync.dma_start(out=x_scale_table[0:P:8, :].bitcast(I32), in_=x_scales[0].bitcast(I32))
         nc.sync.dma_start(out=x_table[:].bitcast(I32), in_=x_words[0].rearrange("p c r -> p (c r)").bitcast(I32))
 
         w2_planes = tile([P, WIDTH], U8, "w2_planes")
         w2_plane = w2_planes[:].rearrange("p (t m) -> p t m", t=PACK)
-        deal_scales(nc.vector, w2_planes[:], w2_rows)
-        mend_rows((nc.scalar, nc.scalar, nc.scalar), w2_planes)
+        deal_scales(nc.vector, w2_planes[:], w2_rows[:])
+        for b in range(2):
+            nc.scalar.dma_start(
+                out=w2_planes[2 + b : P : QUADRANT, :].bitcast(I32), in_=w2_planes[GROUP + b : P : QUADRANT, :].bitcast(I32)
+            )
 
-        picked_rows = tile([P, PLACES], U8, "picked_rows")
+        picked_rows = placed([P, PLACES], U8, "picked_rows", picked_rows_at)
         x_plane = tile([P, PLACES], U8, "x_plane")
         nc.gpsimd.memset(x_plane[:].bitcast(I32), 0)
         nc.vector.tensor_copy(picked_rows[:], x_scale_table[:].indirect(offs_sb[:]))
         for a in range(PACK):
             queue = nc.scalar if a % 2 else nc.sync
             queue.dma_start(out=x_plane[a:P:QUADRANT, :].bitcast(I32), in_=picked_rows[8 * a : P : QUADRANT, :].bitcast(I32))
-        w2_codes = deal_words(placed([P, PACK, 2 * P], U8, "w2_codes", 47 * WIDTH), w2_raw[:, : 2 * WIDTH])
+        w2_codes = deal_words(nc.vector.tensor_copy, placed([P, PACK, 2 * P], U8, "w2_codes", w2_codes_at), w2_raw[:])
 
-        w3_raw = placed([P, 2 * WIDTH], U8, "w3_raw", 15 * WIDTH)
-        w4_raw = placed([P, 4 * WIDTH], U8, "w4_raw", 11 * WIDTH)
-        load_words(nc.sync, w3_raw[:], w3_words)
-        load_scale_rows(nc.sync, w4_raw[:, 2 * WIDTH : 3 * WIDTH], w3_scales)
-        load_scale_rows(nc.sync, w4_raw[:, 3 * WIDTH :], w4_scales)
-        load_words(nc.sync, w4_raw[:, : 2 * WIDTH], w4_words)
+        late = placed([P, 2 * WIDTH], U8, "late", late_at)
         w1_rows = w1.rearrange("(p j) c -> p j c", j=PACK)
-        w1_raw = placed([P, 2, PACK, WIDTH // 2], F32, "w1_raw", 26 * WIDTH)
-        for h in range(2):
-            nc.sync.dma_start(out=w1_raw[:, h], in_=w1_rows[:, :, h * WIDTH // 2 : (h + 1) * WIDTH // 2])
+        w1_raw = placed([P, 2, PACK, WIDTH // 2], F32, "w1_raw", w1_raw_at)
+        nc.sync.dma_start(out=w1_raw[:, 0], in_=w1_rows[:, :, : WIDTH // 2])
+        load_scale_rows(nc.sync, late[:, :WIDTH], w3_scales)
+        load_scale_rows(nc.sync, late[:, WIDTH:], w4_scales)
+        nc.sync.dma_start(out=w1_raw[:, 1], in_=w1_rows[:, :, WIDTH // 2 :])
+        late_words = placed([P, 4 * WIDTH], U8, "late_words", late_words_at)
+        load_words(nc.sync, late_words[:, : 2 * WIDTH], w3_words)
+        load_words(nc.sync, late_words[:, 2 * WIDTH :], w4_words)
 
         x_codes = tile([P, PLACES], U32, "x_codes")
-        half = PLACES // 2
-        for start in (0, half):
-            nc.vector.tensor_copy(x_codes[:, start : start + half], x_table[:].indirect(offs_sb[:, entries(start, half)]))
+        for start in (0, HALF):
+            nc.vector.tensor_copy(x_codes[:, start : start + HALF], x_table[:].indirect(offs_sb[:, entries(start, HALF)]))
+
+        last_planes = tile([P, 2 * WIDTH], U8, "last_planes")
+        for n in range(2):
+            deal_scales(nc.gpsimd, last_planes[:, n * WIDTH : (n + 1) * WIDTH], late[:, n * WIDTH : (n + 1) * WIDTH])
+        mend_rows(nc.sync, last_planes)
+        w3_plane = last_planes[:, :WIDTH].rearrange("p (t m) -> p t m", t=PACK)
+        w4_plane = last_planes[:, WIDTH:].rearrange("p (t m) -> p t m", t=PACK)
 
         def e_product(out, t, cols):
             nc.tensor.matmul_mx(
@@ -124,202 +155,175 @@ def tile_picked_pnn8_none_po_kernel(
                 rhs=x_codes[:, cols].bitcast(FP8X4), rhs_scale=x_plane[:, cols], start=True, stop=True,
             )
 
-        e_rows = [tile([P, 2 * PLACES], F32, "e_row%d" % t) for t in range(2)]
-        e_rows.append(tile([P, PLACES], F32, "e_row2"))
+        e_rows = [tile([P, (2 if t < 2 else 1) * PLACES], F32, "e_row%d" % t) for t in range(PACK)]
         for c in range(chunks):
             cols = slice(c * CHUNK, (c + 1) * CHUNK)
-            piece = ps.tile([P, CHUNK], F32, name="e_piece%d" % c, tag="bank%d" % (PACK + c))
+            piece = bank([P, CHUNK], "e_piece%d" % c, PACK + c)
             e_product(piece[:], 0, cols)
             nc.scalar.activation(out=e_rows[0][:, cols], in_=piece[:], func=COPY, scale=0.5)
-        e_banks = {}
         for t in range(1, PACK):
-            e_banks[t] = ps.tile([P, PLACES], F32, name="e_bank%d" % t, tag="bank%d" % t)
-            e_product(e_banks[t][:], t, slice(0, PLACES))
-        for t in (1, 2):
-            nc.scalar.activation(out=e_rows[t][:, :PLACES], in_=e_banks[t][:], func=COPY, scale=0.5)
+            e_bank = bank([P, PLACES], "e_bank%d" % t, t)
+            e_product(e_bank[:], t, slice(0, PLACES))
+            nc.scalar.activation(out=e_rows[t][:, :PLACES], in_=e_bank[:], func=COPY, scale=0.5)
 
-        def deal_words_as_bytes(words, raw):
-            nc.gpsimd.tensor_copy(
-                out=words[:].rearrange("p t (m b) -> p m t b", b=2),
-                in_=raw.rearrange("p (m t b) -> p m t b", t=PACK, b=2),
-            )
-            return words
-
-        last_planes = tile([P, 2 * WIDTH], U8, "last_planes")
-        deal_scales(nc.gpsimd, last_planes[:, :WIDTH], w4_raw[:, 2 * WIDTH : 3 * WIDTH])
-        w3_codes = deal_words(tile([P, PACK, 2 * P], U8, "w3_codes"), w3_raw[:])
-        deal_scales(nc.gpsimd, last_planes[:, WIDTH:], w4_raw[:, 3 * WIDTH :])
-        mend_rows((nc.sync, nc.sync, nc.sync), last_planes)
-        w4_codes = deal_words_as_bytes(tile([P, PACK, 2 * P], U8, "w4_codes"), w4_raw[:, : 2 * WIDTH])
-        w3_plane = last_planes[:, :WIDTH].rearrange("p (t m) -> p t m", t=PACK)
-        w4_plane = last_planes[:, WIDTH:].rearrange("p (t m) -> p t m", t=PACK)
-
-        w1_bf = tile([P, PACK * WIDTH], BF16, "w1_bf")
-        for h in range(2):
-            nc.scalar.copy(
-                out=w1_bf[:].rearrange("p (t h m j) -> p h m j t", t=PACK, h=2, j=PACK)[:, h],
-                in_=w1_raw[:, h].rearrange("p j (m t) -> p m j t", t=PACK),
-            )
-        e_rows.append(placed([P, PLACES], F32, "e_row3", 30 * WIDTH))
-        nc.scalar.activation(out=e_rows[3][:], in_=e_banks[3][:], func=COPY, scale=0.5)
-
-        picks = placed([P, 2, PLACES], F32, "picks", 17 * WIDTH - 64)
-        sums = placed([P, PACK, PLACES], F32, "sums", 64 - 5 * WIDTH)
+        picks = tile([P, 2, PLACES], F32, "picks")
+        middle_picks = tile([P, 2, HALF], F32, "middle_picks")
+        sums = placed([P, PACK, PLACES], F32, "sums", sums_at)
 
         def first_pick(out, t, start, count):
-            nc.vector.tensor_copy(out, e_rows[t][:].indirect(p1_sb[:, entries(start, count)]))
+            window = e_rows[t][:].indirect(p1_sb[:, entries(start, count)])
+            if t == 0:
+                nc.vector.tensor_copy(out, window)
+            else:
+                nc.scalar.activation(out=out, in_=window, func=COPY)
 
         def second_pick(first, t, start, count):
             nc.vector.tensor_tensor(
                 sums[:, t, start : start + count], e_rows[t][:].indirect(p2_sb[:, entries(start, count)]), first, ADD
             )
 
-        for t in (0, 1):
-            first_pick(picks[:, t, :], t, 0, PLACES)
-        for t in (0, 1):
-            second_pick(picks[:, t, :], t, 0, PLACES)
+        w1_bf = tile([P, PACK * WIDTH], BF16, "w1_bf")
 
+        def round_w1(copy, h):
+            copy(
+                out=w1_bf[:].rearrange("p (t h m j) -> p h m j t", t=PACK, h=2, j=PACK)[:, h],
+                in_=w1_raw[:, h].rearrange("p j (m t) -> p m j t", t=PACK),
+            )
+
+        round_w1(nc.vector.tensor_copy, 0)
+        first_pick(picks[:, 0], 0, 0, PLACES)
+        round_w1(nc.vector.tensor_copy, 1)
+        first_pick(picks[:, 1], 1, 0, PLACES)
+        second_pick(picks[:, 0], 0, 0, PLACES)
         w1_codes = tile([P, WIDTH], U32, "w1_codes")
         w1_plane = tile([P, WIDTH], U8, "w1_plane")
         nc.vector.quantize_mx(out=w1_codes[:].bitcast(FP8X4), scales=w1_plane[:], in_=w1_bf[:])
-
-        middle_picks = placed([P, 2, half], F32, "middle_picks", 34 * WIDTH)
+        second_pick(picks[:, 1], 1, 0, PLACES)
         for t in (2, 3):
-            first_pick(middle_picks[:, t - 2, :], t, 0, half)
-        second_pick(middle_picks[:, 0, :], 2, 0, half)
-        for c in range(2):
-            second_pick(middle_picks[:, 1, c * CHUNK : (c + 1) * CHUNK], 3, c * CHUNK, CHUNK)
+            first_pick(middle_picks[:, t - 2], t, 0, HALF)
+            second_pick(middle_picks[:, t - 2], t, 0, HALF)
+        w3_codes = deal_words(nc.scalar.copy, tile([P, PACK, 2 * P], U8, "w3_codes"), late_words[:, : 2 * WIDTH])
+        w4_codes = deal_words(nc.scalar.copy, tile([P, PACK, 2 * P], U8, "w4_codes"), late_words[:, 2 * WIDTH :])
 
         y_banks = []
         y_bf = [tile([P, 2, PACK * CHUNK], BF16, "y_bf%d" % h) for h in range(2)]
         for c in range(chunks):
             cols = slice(c * CHUNK, (c + 1) * CHUNK)
-            bank = ps.tile([P, PACK, CHUNK], F32, name="y_bank%d" % c, tag="bank%d" % (PACK + c))
+            y_bank = bank([P, PACK, CHUNK], "y_bank%d" % c, PACK + c)
             for t in range(PACK):
                 feats = slice(t * P, (t + 1) * P)
                 nc.tensor.matmul_mx(
-                    out=bank[:, t, :], lhsT=w1_codes[:, feats].bitcast(FP8X4), lhsT_scale=w1_plane[:, feats],
+                    out=y_bank[:, t, :], lhsT=w1_codes[:, feats].bitcast(FP8X4), lhsT_scale=w1_plane[:, feats],
                     rhs=x_codes[:, cols].bitcast(FP8X4), rhs_scale=x_plane[:, cols], start=True, stop=True,
                 )
-            nc.scalar.copy(
-                out=y_bf[c // 2][:, c % 2, :].rearrange("p (c i t) -> p c t i", t=PACK, i=4),
-                in_=bank[:].rearrange("p t (c i) -> p c t i", i=4),
-            )
-            y_banks.append(bank)
+            y_banks.append(y_bank)
+
+        def weave_y(c):
+            nc.scalar.copy(out=woven(y_bf[c // 2][:, c % 2, :]), in_=sliced(y_banks[c][:]))
+
+        weave_y(0)
+        weave_y(1)
+        late_picks = sb.tile([P, 2, HALF], F32, name="late_picks", tag="w1_codes", align_bytes=64)
+        for t in (2, 3):
+            first_pick(late_picks[:, t - 2], t, HALF, HALF)
+        weave_y(2)
+        weave_y(3)
+
+        def late_pick(t, c):
+            second_pick(late_picks[:, t - 2, (c - 2) * CHUNK : (c - 1) * CHUNK], t, c * CHUNK, CHUNK)
+
+        def quantised(name, bf, width):
+            codes = tile([P, width], U32, name + "_codes")
+            plane = tile([P, width], U8, name + "_plane")
+            nc.vector.quantize_mx(out=codes[:].bitcast(FP8X4), scales=plane[:], in_=bf)
+            return codes, plane
 
         y_operands = {}
 
         def quantise_y(h):
-            codes = tile([P, half], U32, "y_codes%d" % h)
-            plane = tile([P, half], U8, "y_plane%d" % h)
-            nc.vector.quantize_mx(out=codes[:].bitcast(FP8X4), scales=plane[:], in_=y_bf[h][:].rearrange("p c n -> p (c n)"))
+            codes, plane = quantised("y%d" % h, y_bf[h][:].rearrange("p c n -> p (c n)"), HALF)
             for n in range(2):
                 cols = slice(n * CHUNK, (n + 1) * CHUNK)
                 y_operands[2 * h + n] = (codes[:, cols], plane[:, cols])
 
-        def z_values(c, z_bf):
-            nc.vector.tensor_tensor(
-                z_bf.rearrange("p (c i t) -> p c t i", t=PACK, i=4),
-                sums[:, :, c * CHUNK : (c + 1) * CHUNK].rearrange("p t (c i) -> p c t i", i=4),
-                y_banks[c][:].rearrange("p t (c i) -> p c t i", i=4),
-                MULT,
-            )
+        z_bf = [tile([P, PACK * CHUNK], BF16, "z_bf%d" % c) for c in range(chunks)]
 
-        z_operands = {}
-
-        def quantise_z(first, count, z_bf):
-            codes = tile([P, count * CHUNK], U32, "z_codes%d" % first)
-            plane = tile([P, count * CHUNK], U8, "z_plane%d" % first)
-            nc.vector.quantize_mx(out=codes[:].bitcast(FP8X4), scales=plane[:], in_=z_bf)
-            for n in range(count):
-                cols = slice(n * CHUNK, (n + 1) * CHUNK)
-                z_operands[first + n] = (codes[:, cols], plane[:, cols])
+        def z_values(c):
+            nc.vector.tensor_tensor(woven(z_bf[c][:]), sliced(sums[:, :, c * CHUNK : (c + 1) * CHUNK]), sliced(y_banks[c][:]), MULT)
 
         out_codes = tile([P, PLACES], U32, "out_codes")
         out_plane = tile([P, PLACES], U8, "out_plane")
         out_rows = out_0.rearrange("(p t) j -> p t j", t=PACK)
         out_words = out_1[0].rearrange("p c r -> p (c r)").bitcast(I32)
+        last = chunks - 1
+        out_banks = {}
 
         def y_passes(c):
-            last = c == chunks - 1
-            if last:
-                banks = [ps.tile([P, CHUNK], F32, name="last_bank%d" % t, tag="bank%d" % (3, 4, 5, 0)[t]) for t in range(PACK)]
-                sums_out = [one[:] for one in banks]
+            if c == last:
+                parts = [bank([P, CHUNK], "last_bank%d" % t, (3, 4, 5, 0)[t])[:] for t in range(PACK)]
             else:
-                banks = ps.tile([P, PACK, CHUNK], F32, name="out_bank%d" % c, tag="bank%d" % c)
-                sums_out = [banks[:, t, :] for t in range(PACK)]
+                whole = bank([P, PACK, CHUNK], "out_bank%d" % c, c)
+                parts = [whole[:, t, :] for t in range(PACK)]
+                out_banks[c] = whole
             for t in range(PACK):
                 nc.tensor.matmul_mx(
-                    out=sums_out[t], lhsT=w3_codes[:, t, :].bitcast(FP4X4), lhsT_scale=w3_plane[:, t, :],
-                    rhs=y_operands[c][0].bitcast(FP8X4), rhs_scale=y_operands[c][1], start=last or t == 0, stop=False,
+                    out=parts[t], lhsT=w3_codes[:, t, :].bitcast(FP4X4), lhsT_scale=w3_plane[:, t, :],
+                    rhs=y_operands[c][0].bitcast(FP8X4), rhs_scale=y_operands[c][1], start=c == last or t == 0, stop=False,
                 )
-            return banks, sums_out
+            return parts
 
-        def products(c, opened):
-            banks, sums_out = opened
-            cols = slice(c * CHUNK, (c + 1) * CHUNK)
-            last = c == chunks - 1
-            out_bf = tile([P, PACK * CHUNK], BF16, "out_bf%d" % c)
-            out_f32 = tile([P, PACK, CHUNK], F32, "out_f32_%d" % c)
+        out_bf = [tile([P, PACK * CHUNK], BF16, "out_bf%d" % c) for c in range(chunks)]
+        out_f32 = [tile([P, PACK, CHUNK], F32, "out_f32_%d" % c) for c in range(chunks)]
+
+        def z_passes(c, parts):
+            codes, plane = quantised("z%d" % c, z_bf[c][:], CHUNK)
             for t in range(PACK):
                 nc.tensor.matmul_mx(
-                    out=sums_out[t], lhsT=w4_codes[:, t, :].bitcast(FP4X4), lhsT_scale=w4_plane[:, t, :],
-                    rhs=z_operands[c][0].bitcast(FP8X4), rhs_scale=z_operands[c][1], start=False, stop=last or t == PACK - 1,
+                    out=parts[t], lhsT=w4_codes[:, t, :].bitcast(FP4X4), lhsT_scale=w4_plane[:, t, :],
+                    rhs=codes[:].bitcast(FP8X4), rhs_scale=plane[:], start=False, stop=c == last or t == PACK - 1,
                 )
-                if last and t % 2 == 0:
-                    nc.vector.tensor_copy(out=out_f32[:, t, :], in_=sums_out[t])
-                elif last:
-                    nc.scalar.copy(out=out_f32[:, t, :], in_=sums_out[t])
-            if last:
-                nc.vector.tensor_copy(
-                    out=out_bf[:].rearrange("p (c i t) -> p c t i", t=PACK, i=4),
-                    in_=out_f32[:].rearrange("p t (c i) -> p c t i", i=4),
-                )
-            else:
-                nc.scalar.copy(out=out_f32[:], in_=banks[:])
-                nc.scalar.copy(
-                    out=out_bf[:].rearrange("p (c i t) -> p c t i", t=PACK, i=4),
-                    in_=banks[:].rearrange("p t (c i) -> p c t i", i=4),
-                )
-            nc.sync.dma_start(out=out_rows[:, :, cols], in_=out_f32[:])
-            return out_bf
+                if c == last:
+                    copy = nc.scalar.copy if t % 2 else nc.vector.tensor_copy
+                    copy(out=out_f32[c][:, t, :], in_=parts[t])
+            if c != last:
+                nc.scalar.copy(out=out_f32[c][:], in_=out_banks[c][:])
+            nc.sync.dma_start(out=out_rows[:, :, c * CHUNK : (c + 1) * CHUNK], in_=out_f32[c][:])
 
-        def planes(c, out_bf):
+        def weave_from_bank(c):
+            nc.scalar.copy(out=woven(out_bf[c][:]), in_=sliced(out_banks[c][:]))
+
+        def weave_from_copy(c):
+            nc.vector.tensor_copy(out=woven(out_bf[c][:]), in_=sliced(out_f32[c][:]))
+
+        def planes(c):
             cols = slice(c * CHUNK, (c + 1) * CHUNK)
-            nc.vector.quantize_mx(out=out_codes[:, cols].bitcast(FP8X4), scales=out_plane[:, cols], in_=out_bf[:])
+            nc.vector.quantize_mx(out=out_codes[:, cols].bitcast(FP8X4), scales=out_plane[:, cols], in_=out_bf[c][:])
             nc.sync.dma_start(out=out_words[:, cols], in_=out_codes[:, cols].bitcast(I32))
 
+        z_values(0)
         quantise_y(0)
         opened = [y_passes(0), y_passes(1)]
-        z_bf = [tile([P, PACK * CHUNK], BF16, "z_bf%d" % c) for c in range(chunks)]
-        z_values(0, z_bf[0][:])
-        z_values(1, z_bf[1][:])
-        quantise_z(0, 1, z_bf[0][:])
-        o0 = products(0, opened[0])
-        third_picks = tile([P, 2, CHUNK], F32, "third_picks", "w1_codes")
-        first_pick(third_picks[:, 0], 2, 2 * CHUNK, CHUNK)
-        quantise_z(1, 1, z_bf[1][:])
-        o1 = products(1, opened[1])
-        first_pick(third_picks[:, 1], 3, 2 * CHUNK, CHUNK)
-        for t in (2, 3):
-            second_pick(third_picks[:, t - 2], t, 2 * CHUNK, CHUNK)
+        z_passes(0, opened[0])
+        weave_from_bank(0)
+        z_values(1)
+        late_pick(2, 2)
+        z_passes(1, opened[1])
+        weave_from_bank(1)
+        late_pick(3, 2)
         quantise_y(1)
         opened.extend([y_passes(2), y_passes(3)])
-        z_values(2, z_bf[2][:])
-        last_picks = tile([P, 2, CHUNK], F32, "last_picks", "z_codes1")
-        first_pick(last_picks[:, 0], 2, 3 * CHUNK, CHUNK)
-        quantise_z(2, 1, z_bf[2][:])
-        o2 = products(2, opened[2])
-        first_pick(last_picks[:, 1], 3, 3 * CHUNK, CHUNK)
-        for t in (2, 3):
-            second_pick(last_picks[:, t - 2], t, 3 * CHUNK, CHUNK)
-        planes(0, o0)
-        z_values(3, z_bf[3][:])
-        planes(1, o1)
-        quantise_z(3, 1, z_bf[3][:])
-        o3 = products(3, opened[3])
-        planes(2, o2)
-        planes(3, o3)
+        z_values(2)
+        late_pick(2, 3)
+        z_passes(2, opened[2])
+        late_pick(3, 3)
+        planes(0)
+        z_values(3)
+        planes(1)
+        z_passes(3, opened[3])
+        weave_from_copy(2)
+        weave_from_copy(3)
+        planes(2)
+        planes(3)
 
         plane_rows = out_2[0].rearrange("(q a) c -> a q c", a=PACK)
         for a in range(PACK):

@@ -55,10 +55,6 @@ def tile_picked_pnn8_none_po_kernel(
         def load_words(queue, raw, words):
             queue.dma_start(out=raw.bitcast(I32), in_=words[0].bitcast(I32))
 
-        def load_scale_rows(queue, raw, scales):
-            rows = scales[0].bitcast(I32)
-            queue.dma_start(out=raw.bitcast(I32), in_=rows.unsqueeze(1).to_broadcast([16, 8, rows.shape[1]]))
-
         def deal_scales(engine, plane, raw):
             engine.tensor_copy(
                 out=plane.rearrange("p (w t c i) -> p w c t i", t=PACK, c=8, i=16),
@@ -83,20 +79,20 @@ def tile_picked_pnn8_none_po_kernel(
             return f32.rearrange("p t (c i) -> p c t i", i=4)
 
         sums_at = 0
-        late_at = sums_at + 4 * PACK * PLACES - TOUCH
-        w2_raw_at = late_at + 2 * WIDTH - TOUCH
-        w1_raw_at = w2_raw_at + 2 * WIDTH - TOUCH
+        late_rows_at = sums_at + 4 * PACK * PLACES - TOUCH
+        late_words_at = late_rows_at + 2 * WIDTH
+        w1_raw_at = late_words_at + 4 * WIDTH
+        w2_raw_at = late_words_at - TOUCH
+        w2_raw_bytes = 4 * WIDTH + 2 * TOUCH
         table_at = w1_raw_at + 4 * PACK * WIDTH
         w2_codes_at = table_at + FIELDS - TOUCH
-        late_words_at = w2_codes_at + 2 * WIDTH
-        picked_rows_at = late_words_at + 4 * WIDTH - TOUCH
 
         offs_sb = sb.tile([P, PLACES // GROUP], U16, name="offs_sb")
         p1_sb = sb.tile([P, PLACES // GROUP], U16, name="p1_sb")
         p2_sb = sb.tile([P, PLACES // GROUP], U16, name="p2_sb")
         x_table = tile([P, FIELDS], U32, "x_table")
         x_scale_table = placed([P, FIELDS], U8, "x_scale_table", table_at)
-        w2_raw = placed([P, 2 * WIDTH], U8, "w2_raw", w2_raw_at)
+        w2_raw = placed([P, w2_raw_bytes], U8, "w2_raw", w2_raw_at)
         w2_rows = tile([P, WIDTH], U8, "w2_rows")
 
         nc.vector.memset(x_scale_table[:].bitcast(I32), 0)
@@ -105,7 +101,7 @@ def tile_picked_pnn8_none_po_kernel(
         for b in range(2):
             nc.scalar.dma_start(out=w2_rows[b:P:2, :].bitcast(I32), in_=w2_pairs[b].unsqueeze(1).to_broadcast([8, 8, WIDTH // 4]))
         nc.sync.dma_start(p1_sb[:], p1)
-        load_words(nc.scalar, w2_raw[:], w2_words)
+        load_words(nc.scalar, w2_raw[:, : 2 * WIDTH], w2_words)
         nc.sync.dma_start(p2_sb[:], p2)
         nc.sync.dma_start(out=x_scale_table[0:P:8, :].bitcast(I32), in_=x_scales[0].bitcast(I32))
         nc.sync.dma_start(out=x_table[:].bitcast(I32), in_=x_words[0].rearrange("p c r -> p (c r)").bitcast(I32))
@@ -118,33 +114,36 @@ def tile_picked_pnn8_none_po_kernel(
                 out=w2_planes[2 + b : P : QUADRANT, :].bitcast(I32), in_=w2_planes[GROUP + b : P : QUADRANT, :].bitcast(I32)
             )
 
-        picked_rows = placed([P, PLACES], U8, "picked_rows", picked_rows_at)
+        picked_rows = tile([P, PLACES], U8, "picked_rows")
         x_plane = tile([P, PLACES], U8, "x_plane")
         nc.gpsimd.memset(x_plane[:].bitcast(I32), 0)
         nc.vector.tensor_copy(picked_rows[:], x_scale_table[:].indirect(offs_sb[:]))
         for a in range(PACK):
             queue = nc.scalar if a % 2 else nc.sync
             queue.dma_start(out=x_plane[a:P:QUADRANT, :].bitcast(I32), in_=picked_rows[8 * a : P : QUADRANT, :].bitcast(I32))
-        w2_codes = deal_words(nc.vector.tensor_copy, placed([P, PACK, 2 * P], U8, "w2_codes", w2_codes_at), w2_raw[:])
+        w2_codes = deal_words(nc.vector.tensor_copy, placed([P, PACK, 2 * P], U8, "w2_codes", w2_codes_at), w2_raw[:, : 2 * WIDTH])
 
-        late = placed([P, 2 * WIDTH], U8, "late", late_at)
-        w1_rows = w1.rearrange("(p j) c -> p j c", j=PACK)
-        w1_raw = placed([P, 2, PACK, WIDTH // 2], F32, "w1_raw", w1_raw_at)
-        nc.sync.dma_start(out=w1_raw[:, 0], in_=w1_rows[:, :, : WIDTH // 2])
-        load_scale_rows(nc.sync, late[:, :WIDTH], w3_scales)
-        load_scale_rows(nc.sync, late[:, WIDTH:], w4_scales)
-        nc.sync.dma_start(out=w1_raw[:, 1], in_=w1_rows[:, :, WIDTH // 2 :])
         late_words = placed([P, 4 * WIDTH], U8, "late_words", late_words_at)
+        late_rows = placed([P, 2 * WIDTH], U8, "late_rows", late_rows_at)
+        nc.gpsimd.memset(late_rows[:].bitcast(I32), 0)
         load_words(nc.sync, late_words[:, : 2 * WIDTH], w3_words)
         load_words(nc.sync, late_words[:, 2 * WIDTH :], w4_words)
+        nc.sync.dma_start(out=late_rows[0:P:8, :WIDTH].bitcast(I32), in_=w3_scales[0].bitcast(I32))
+        nc.sync.dma_start(out=late_rows[0:P:8, WIDTH:].bitcast(I32), in_=w4_scales[0].bitcast(I32))
+        w1_rows = w1.rearrange("(p j) c -> p j c", j=PACK)
+        w1_raw = placed([P, 2, PACK, WIDTH // 2], F32, "w1_raw", w1_raw_at)
+        for h in range(2):
+            nc.sync.dma_start(out=w1_raw[:, h], in_=w1_rows[:, :, h * WIDTH // 2 : (h + 1) * WIDTH // 2])
 
         x_codes = tile([P, PLACES], U32, "x_codes")
         for start in (0, HALF):
             nc.vector.tensor_copy(x_codes[:, start : start + HALF], x_table[:].indirect(offs_sb[:, entries(start, HALF)]))
 
-        last_planes = tile([P, 2 * WIDTH], U8, "last_planes")
+        w3_codes = deal_words(nc.vector.tensor_copy, tile([P, PACK, 2 * P], U8, "w3_codes"), late_words[:, : 2 * WIDTH])
+        w4_codes = deal_words(nc.vector.tensor_copy, tile([P, PACK, 2 * P], U8, "w4_codes"), late_words[:, 2 * WIDTH :])
+        last_planes = placed([P, 2 * WIDTH], U8, "last_planes", late_words_at + WIDTH)
         for n in range(2):
-            deal_scales(nc.gpsimd, last_planes[:, n * WIDTH : (n + 1) * WIDTH], late[:, n * WIDTH : (n + 1) * WIDTH])
+            deal_scales(nc.gpsimd, last_planes[:, n * WIDTH : (n + 1) * WIDTH], late_rows[:, n * WIDTH : (n + 1) * WIDTH])
         mend_rows(nc.sync, last_planes)
         w3_plane = last_planes[:, :WIDTH].rearrange("p (t m) -> p t m", t=PACK)
         w4_plane = last_planes[:, WIDTH:].rearrange("p (t m) -> p t m", t=PACK)
@@ -167,7 +166,7 @@ def tile_picked_pnn8_none_po_kernel(
             nc.scalar.activation(out=e_rows[t][:, :PLACES], in_=e_bank[:], func=COPY, scale=0.5)
 
         picks = tile([P, 2, PLACES], F32, "picks")
-        middle_picks = tile([P, 2, HALF], F32, "middle_picks")
+        middle_picks = placed([P, 3, HALF], F32, "middle_picks", w1_raw_at + 2 * PACK * WIDTH)
         sums = placed([P, PACK, PLACES], F32, "sums", sums_at)
 
         def first_pick(out, t, start, count):
@@ -190,20 +189,19 @@ def tile_picked_pnn8_none_po_kernel(
                 in_=w1_raw[:, h].rearrange("p j (m t) -> p m j t", t=PACK),
             )
 
-        round_w1(nc.vector.tensor_copy, 0)
         first_pick(picks[:, 0], 0, 0, PLACES)
-        round_w1(nc.vector.tensor_copy, 1)
+        round_w1(nc.vector.tensor_copy, 0)
         first_pick(picks[:, 1], 1, 0, PLACES)
+        round_w1(nc.scalar.copy, 1)
         second_pick(picks[:, 0], 0, 0, PLACES)
+        second_pick(picks[:, 1], 1, 0, PLACES)
         w1_codes = tile([P, WIDTH], U32, "w1_codes")
         w1_plane = tile([P, WIDTH], U8, "w1_plane")
         nc.vector.quantize_mx(out=w1_codes[:].bitcast(FP8X4), scales=w1_plane[:], in_=w1_bf[:])
-        second_pick(picks[:, 1], 1, 0, PLACES)
-        for t in (2, 3):
-            first_pick(middle_picks[:, t - 2], t, 0, HALF)
-            second_pick(middle_picks[:, t - 2], t, 0, HALF)
-        w3_codes = deal_words(nc.scalar.copy, tile([P, PACK, 2 * P], U8, "w3_codes"), late_words[:, : 2 * WIDTH])
-        w4_codes = deal_words(nc.scalar.copy, tile([P, PACK, 2 * P], U8, "w4_codes"), late_words[:, 2 * WIDTH :])
+        for t, start in ((2, 0), (3, 0), (2, HALF)):
+            first = middle_picks[:, t - 2 + 2 * start // HALF]
+            first_pick(first, t, start, HALF)
+            second_pick(first, t, start, HALF)
 
         y_banks = []
         y_bf = [tile([P, 2, PACK * CHUNK], BF16, "y_bf%d" % h) for h in range(2)]
@@ -223,14 +221,10 @@ def tile_picked_pnn8_none_po_kernel(
 
         weave_y(0)
         weave_y(1)
-        late_picks = sb.tile([P, 2, HALF], F32, name="late_picks", tag="w1_codes", align_bytes=64)
-        for t in (2, 3):
-            first_pick(late_picks[:, t - 2], t, HALF, HALF)
         weave_y(2)
+        late_picks = sb.tile([P, HALF], F32, name="late_picks", tag="w1_codes", align_bytes=64)
+        first_pick(late_picks[:], 3, HALF, HALF)
         weave_y(3)
-
-        def late_pick(t, c):
-            second_pick(late_picks[:, t - 2, (c - 2) * CHUNK : (c - 1) * CHUNK], t, c * CHUNK, CHUNK)
 
         def quantised(name, bf, width):
             codes = tile([P, width], U32, name + "_codes")
@@ -298,7 +292,9 @@ def tile_picked_pnn8_none_po_kernel(
         def planes(c):
             cols = slice(c * CHUNK, (c + 1) * CHUNK)
             nc.vector.quantize_mx(out=out_codes[:, cols].bitcast(FP8X4), scales=out_plane[:, cols], in_=out_bf[c][:])
-            nc.sync.dma_start(out=out_words[:, cols], in_=out_codes[:, cols].bitcast(I32))
+            if c % 2:
+                pair = slice((c - 1) * CHUNK, (c + 1) * CHUNK)
+                nc.sync.dma_start(out=out_words[:, pair], in_=out_codes[:, pair].bitcast(I32))
 
         z_values(0)
         quantise_y(0)
@@ -306,17 +302,14 @@ def tile_picked_pnn8_none_po_kernel(
         z_passes(0, opened[0])
         weave_from_bank(0)
         z_values(1)
-        late_pick(2, 2)
+        second_pick(late_picks[:], 3, HALF, HALF)
         z_passes(1, opened[1])
         weave_from_bank(1)
-        late_pick(3, 2)
         quantise_y(1)
         opened.extend([y_passes(2), y_passes(3)])
         z_values(2)
-        late_pick(2, 3)
-        z_passes(2, opened[2])
-        late_pick(3, 3)
         planes(0)
+        z_passes(2, opened[2])
         z_values(3)
         planes(1)
         z_passes(3, opened[3])

@@ -79,7 +79,8 @@ def tile_picked_pnn8_none_po_kernel(
             return f32.rearrange("p t (c i) -> p c t i", i=4)
 
         sums_at = 0
-        late_rows_at = sums_at + 4 * PACK * PLACES - TOUCH
+        half_at = sums_at + 4 * PACK * PLACES - TOUCH
+        late_rows_at = half_at + TOUCH
         late_words_at = late_rows_at + 2 * WIDTH
         w1_raw_at = late_words_at + 4 * WIDTH
         w2_raw_at = late_words_at - TOUCH
@@ -97,9 +98,8 @@ def tile_picked_pnn8_none_po_kernel(
 
         nc.vector.memset(x_scale_table[:].bitcast(I32), 0)
         nc.sync.dma_start(offs_sb[:], offs)
-        w2_pairs = w2_scales[0].bitcast(I32).rearrange("(m b) c -> b m c", b=2)
-        for b in range(2):
-            nc.scalar.dma_start(out=w2_rows[b:P:2, :].bitcast(I32), in_=w2_pairs[b].unsqueeze(1).to_broadcast([8, 8, WIDTH // 4]))
+        w2_scale_words = w2_scales[0].bitcast(I32)
+        nc.scalar.dma_start(out=w2_rows[:].bitcast(I32), in_=w2_scale_words.unsqueeze(1).to_broadcast([16, 8, WIDTH // 4]))
         nc.sync.dma_start(p1_sb[:], p1)
         load_words(nc.scalar, w2_raw[:, : 2 * WIDTH], w2_words)
         nc.sync.dma_start(p2_sb[:], p2)
@@ -109,10 +109,7 @@ def tile_picked_pnn8_none_po_kernel(
         w2_planes = tile([P, WIDTH], U8, "w2_planes")
         w2_plane = w2_planes[:].rearrange("p (t m) -> p t m", t=PACK)
         deal_scales(nc.vector, w2_planes[:], w2_rows[:])
-        for b in range(2):
-            nc.scalar.dma_start(
-                out=w2_planes[2 + b : P : QUADRANT, :].bitcast(I32), in_=w2_planes[GROUP + b : P : QUADRANT, :].bitcast(I32)
-            )
+        mend_rows(nc.scalar, w2_planes)
 
         picked_rows = tile([P, PLACES], U8, "picked_rows")
         x_plane = tile([P, PLACES], U8, "x_plane")
@@ -141,9 +138,8 @@ def tile_picked_pnn8_none_po_kernel(
 
         w3_codes = deal_words(nc.vector.tensor_copy, tile([P, PACK, 2 * P], U8, "w3_codes"), late_words[:, : 2 * WIDTH])
         w4_codes = deal_words(nc.vector.tensor_copy, tile([P, PACK, 2 * P], U8, "w4_codes"), late_words[:, 2 * WIDTH :])
-        last_planes = placed([P, 2 * WIDTH], U8, "last_planes", late_words_at + WIDTH)
-        for n in range(2):
-            deal_scales(nc.gpsimd, last_planes[:, n * WIDTH : (n + 1) * WIDTH], late_rows[:, n * WIDTH : (n + 1) * WIDTH])
+        last_planes = tile([P, 2 * WIDTH], U8, "last_planes")
+        deal_scales(nc.vector, last_planes[:], late_rows[:])
         mend_rows(nc.sync, last_planes)
         w3_plane = last_planes[:, :WIDTH].rearrange("p (t m) -> p t m", t=PACK)
         w4_plane = last_planes[:, WIDTH:].rearrange("p (t m) -> p t m", t=PACK)
@@ -155,6 +151,8 @@ def tile_picked_pnn8_none_po_kernel(
             )
 
         e_rows = [tile([P, (2 if t < 2 else 1) * PLACES], F32, "e_row%d" % t) for t in range(PACK)]
+        half = placed([P, 1], F32, "half", half_at)
+        nc.gpsimd.memset(half[:], 0.5)
         for c in range(chunks):
             cols = slice(c * CHUNK, (c + 1) * CHUNK)
             piece = bank([P, CHUNK], "e_piece%d" % c, PACK + c)
@@ -163,7 +161,7 @@ def tile_picked_pnn8_none_po_kernel(
         for t in range(1, PACK):
             e_bank = bank([P, PLACES], "e_bank%d" % t, t)
             e_product(e_bank[:], t, slice(0, PLACES))
-            nc.scalar.activation(out=e_rows[t][:, :PLACES], in_=e_bank[:], func=COPY, scale=0.5)
+            nc.scalar.activation(out=e_rows[t][:, :PLACES], in_=e_bank[:], func=COPY, scale=half[:])
 
         picks = tile([P, 2, PLACES], F32, "picks")
         middle_picks = placed([P, 3, HALF], F32, "middle_picks", w1_raw_at + 2 * PACK * WIDTH)
@@ -286,12 +284,16 @@ def tile_picked_pnn8_none_po_kernel(
         def weave_from_bank(c):
             nc.scalar.copy(out=woven(out_bf[c][:]), in_=sliced(out_banks[c][:]))
 
-        def weave_from_copy(c):
-            nc.vector.tensor_copy(out=woven(out_bf[c][:]), in_=sliced(out_f32[c][:]))
+        def weave_from_copy(c, start, width):
+            rounded = out_bf[c][:, PACK * start : PACK * (start + width)]
+            nc.vector.tensor_copy(out=woven(rounded), in_=sliced(out_f32[c][:, :, start : start + width]))
 
         def planes(c):
-            cols = slice(c * CHUNK, (c + 1) * CHUNK)
-            nc.vector.quantize_mx(out=out_codes[:, cols].bitcast(FP8X4), scales=out_plane[:, cols], in_=out_bf[c][:])
+            width = CHUNK // 2 if c == last else CHUNK
+            for start in range(0, CHUNK, width):
+                cols = slice(c * CHUNK + start, c * CHUNK + start + width)
+                rounded = out_bf[c][:, PACK * start : PACK * (start + width)]
+                nc.vector.quantize_mx(out=out_codes[:, cols].bitcast(FP8X4), scales=out_plane[:, cols], in_=rounded)
             if c % 2:
                 pair = slice((c - 1) * CHUNK, (c + 1) * CHUNK)
                 nc.sync.dma_start(out=out_words[:, pair], in_=out_codes[:, pair].bitcast(I32))
@@ -313,9 +315,10 @@ def tile_picked_pnn8_none_po_kernel(
         z_values(3)
         planes(1)
         z_passes(3, opened[3])
-        weave_from_copy(2)
-        weave_from_copy(3)
+        weave_from_copy(2, 0, CHUNK)
         planes(2)
+        weave_from_copy(last, 0, CHUNK // 2)
+        weave_from_copy(last, CHUNK // 2, CHUNK // 2)
         planes(3)
 
         plane_rows = out_2[0].rearrange("(q a) c -> a q c", a=PACK)

@@ -24,6 +24,7 @@ HALF = PLACES // 2
 GROUP = 16
 QUADRANT = 32
 TOUCH = 64
+W1_SPLIT = 320
 
 FLOPS = 4 * 2 * 512 * 512 * 512
 
@@ -96,10 +97,10 @@ def tile_picked_pnn8_none_po_kernel(
         w2_raw = placed([P, w2_raw_bytes], U8, "w2_raw", w2_raw_at)
         w2_rows = tile([P, WIDTH], U8, "w2_rows")
 
+        nc.vector.memset(w2_rows[:].bitcast(I32), 0)
         nc.vector.memset(x_scale_table[:].bitcast(I32), 0)
         nc.sync.dma_start(offs_sb[:], offs)
-        w2_scale_words = w2_scales[0].bitcast(I32)
-        nc.scalar.dma_start(out=w2_rows[:].bitcast(I32), in_=w2_scale_words.unsqueeze(1).to_broadcast([16, 8, WIDTH // 4]))
+        nc.scalar.dma_start(out=w2_rows[0:P:8, :].bitcast(I32), in_=w2_scales[0].bitcast(I32))
         nc.sync.dma_start(p1_sb[:], p1)
         load_words(nc.scalar, w2_raw[:, : 2 * WIDTH], w2_words)
         nc.sync.dma_start(p2_sb[:], p2)
@@ -128,9 +129,12 @@ def tile_picked_pnn8_none_po_kernel(
         nc.sync.dma_start(out=late_rows[0:P:8, :WIDTH].bitcast(I32), in_=w3_scales[0].bitcast(I32))
         nc.sync.dma_start(out=late_rows[0:P:8, WIDTH:].bitcast(I32), in_=w4_scales[0].bitcast(I32))
         w1_rows = w1.rearrange("(p j) c -> p j c", j=PACK)
-        w1_raw = placed([P, 2, PACK, WIDTH // 2], F32, "w1_raw", w1_raw_at)
-        for h in range(2):
-            nc.sync.dma_start(out=w1_raw[:, h], in_=w1_rows[:, :, h * WIDTH // 2 : (h + 1) * WIDTH // 2])
+        w1_raw = placed([P, PACK * WIDTH], F32, "w1_raw", w1_raw_at)
+        w1_parts = []
+        for start, stop in ((0, W1_SPLIT), (W1_SPLIT, WIDTH)):
+            part = w1_raw[:, PACK * start : PACK * stop].rearrange("p (j c) -> p j c", j=PACK)
+            nc.sync.dma_start(out=part, in_=w1_rows[:, :, start:stop])
+            w1_parts.append((part, slice(start // PACK, stop // PACK)))
 
         x_codes = tile([P, PLACES], U32, "x_codes")
         for start in (0, HALF):
@@ -182,9 +186,10 @@ def tile_picked_pnn8_none_po_kernel(
         w1_bf = tile([P, PACK * WIDTH], BF16, "w1_bf")
 
         def round_w1(copy, h):
+            part, columns = w1_parts[h]
             copy(
-                out=w1_bf[:].rearrange("p (t h m j) -> p h m j t", t=PACK, h=2, j=PACK)[:, h],
-                in_=w1_raw[:, h].rearrange("p j (m t) -> p m j t", t=PACK),
+                out=w1_bf[:].rearrange("p (t m j) -> p m j t", t=PACK, j=PACK)[:, columns],
+                in_=part.rearrange("p j (m t) -> p m j t", t=PACK),
             )
 
         first_pick(picks[:, 0], 0, 0, PLACES)
@@ -220,8 +225,8 @@ def tile_picked_pnn8_none_po_kernel(
         weave_y(0)
         weave_y(1)
         weave_y(2)
-        late_picks = sb.tile([P, HALF], F32, name="late_picks", tag="w1_codes", align_bytes=64)
-        first_pick(late_picks[:], 3, HALF, HALF)
+        late_picks = sb.tile([P, CHUNK], F32, name="late_picks", tag="w1_codes", align_bytes=64)
+        first_pick(late_picks[:], 3, 2 * CHUNK, CHUNK)
         weave_y(3)
 
         def quantised(name, bf, width):
@@ -277,6 +282,8 @@ def tile_picked_pnn8_none_po_kernel(
                 if c == last:
                     copy = nc.scalar.copy if t % 2 else nc.vector.tensor_copy
                     copy(out=out_f32[c][:, t, :], in_=parts[t])
+
+        def store_chunk(c):
             if c != last:
                 nc.scalar.copy(out=out_f32[c][:], in_=out_banks[c][:])
             nc.sync.dma_start(out=out_rows[:, :, c * CHUNK : (c + 1) * CHUNK], in_=out_f32[c][:])
@@ -302,19 +309,26 @@ def tile_picked_pnn8_none_po_kernel(
         quantise_y(0)
         opened = [y_passes(0), y_passes(1)]
         z_passes(0, opened[0])
+        last_picks = sb.tile([P, CHUNK], F32, name="last_picks", tag="z0_codes", align_bytes=64)
+        first_pick(last_picks[:], 3, 3 * CHUNK, CHUNK)
+        store_chunk(0)
         weave_from_bank(0)
         z_values(1)
-        second_pick(late_picks[:], 3, HALF, HALF)
+        second_pick(late_picks[:], 3, 2 * CHUNK, CHUNK)
         z_passes(1, opened[1])
-        weave_from_bank(1)
+        store_chunk(1)
         quantise_y(1)
         opened.extend([y_passes(2), y_passes(3)])
         z_values(2)
-        planes(0)
+        second_pick(last_picks[:], 3, 3 * CHUNK, CHUNK)
         z_passes(2, opened[2])
+        store_chunk(2)
+        planes(0)
         z_values(3)
-        planes(1)
+        weave_from_copy(1, 0, CHUNK)
         z_passes(3, opened[3])
+        store_chunk(3)
+        planes(1)
         weave_from_copy(2, 0, CHUNK)
         planes(2)
         weave_from_copy(last, 0, CHUNK // 2)

@@ -97,10 +97,10 @@ def tile_picked_pnn8_none_po_kernel(
         w2_raw = placed([P, w2_raw_bytes], U8, "w2_raw", w2_raw_at)
         w2_rows = tile([P, WIDTH], U8, "w2_rows")
 
-        nc.vector.memset(w2_rows[:].bitcast(I32), 0)
         nc.vector.memset(x_scale_table[:].bitcast(I32), 0)
         nc.sync.dma_start(offs_sb[:], offs)
-        nc.scalar.dma_start(out=w2_rows[0:P:8, :].bitcast(I32), in_=w2_scales[0].bitcast(I32))
+        w2_scale_words = w2_scales[0].bitcast(I32)
+        nc.scalar.dma_start(out=w2_rows[:].bitcast(I32), in_=w2_scale_words.unsqueeze(1).to_broadcast([16, 8, WIDTH // 4]))
         nc.sync.dma_start(p1_sb[:], p1)
         load_words(nc.scalar, w2_raw[:, : 2 * WIDTH], w2_words)
         nc.sync.dma_start(p2_sb[:], p2)

@@ -24,7 +24,7 @@ HALF = PLACES // 2
 GROUP = 16
 QUADRANT = 32
 TOUCH = 64
-W1_SPLIT = 320
+W1_PARTS = (0, 192, 384, 512)
 
 FLOPS = 4 * 2 * 512 * 512 * 512
 
@@ -82,7 +82,7 @@ def tile_picked_pnn8_none_po_kernel(
         sums_at = 0
         half_at = sums_at + 4 * PACK * PLACES - TOUCH
         late_rows_at = half_at + TOUCH
-        late_words_at = late_rows_at + 2 * WIDTH
+        late_words_at = late_rows_at + 3 * WIDTH
         w1_raw_at = late_words_at + 4 * WIDTH
         w2_raw_at = late_words_at - TOUCH
         w2_raw_bytes = 4 * WIDTH + 2 * TOUCH
@@ -109,7 +109,7 @@ def tile_picked_pnn8_none_po_kernel(
 
         w2_planes = tile([P, WIDTH], U8, "w2_planes")
         w2_plane = w2_planes[:].rearrange("p (t m) -> p t m", t=PACK)
-        deal_scales(nc.vector, w2_planes[:], w2_rows[:])
+        deal_scales(nc.gpsimd, w2_planes[:], w2_rows[:])
         mend_rows(nc.scalar, w2_planes)
 
         picked_rows = tile([P, PLACES], U8, "picked_rows")
@@ -122,16 +122,16 @@ def tile_picked_pnn8_none_po_kernel(
         w2_codes = deal_words(nc.vector.tensor_copy, placed([P, PACK, 2 * P], U8, "w2_codes", w2_codes_at), w2_raw[:, : 2 * WIDTH])
 
         late_words = placed([P, 4 * WIDTH], U8, "late_words", late_words_at)
-        late_rows = placed([P, 2 * WIDTH], U8, "late_rows", late_rows_at)
-        nc.gpsimd.memset(late_rows[:].bitcast(I32), 0)
+        late_rows = placed([P, 3 * WIDTH], U8, "late_rows", late_rows_at)
+        nc.gpsimd.memset(late_rows[:, WIDTH:].bitcast(I32), 0)
         load_words(nc.sync, late_words[:, : 2 * WIDTH], w3_words)
         load_words(nc.sync, late_words[:, 2 * WIDTH :], w4_words)
-        nc.sync.dma_start(out=late_rows[0:P:8, :WIDTH].bitcast(I32), in_=w3_scales[0].bitcast(I32))
-        nc.sync.dma_start(out=late_rows[0:P:8, WIDTH:].bitcast(I32), in_=w4_scales[0].bitcast(I32))
+        nc.sync.dma_start(out=late_rows[0:P:8, WIDTH : 2 * WIDTH].bitcast(I32), in_=w3_scales[0].bitcast(I32))
+        nc.sync.dma_start(out=late_rows[0:P:8, 2 * WIDTH :].bitcast(I32), in_=w4_scales[0].bitcast(I32))
         w1_rows = w1.rearrange("(p j) c -> p j c", j=PACK)
         w1_raw = placed([P, PACK * WIDTH], F32, "w1_raw", w1_raw_at)
         w1_parts = []
-        for start, stop in ((0, W1_SPLIT), (W1_SPLIT, WIDTH)):
+        for start, stop in zip(W1_PARTS, W1_PARTS[1:]):
             part = w1_raw[:, PACK * start : PACK * stop].rearrange("p (j c) -> p j c", j=PACK)
             nc.sync.dma_start(out=part, in_=w1_rows[:, :, start:stop])
             w1_parts.append((part, slice(start // PACK, stop // PACK)))
@@ -142,8 +142,9 @@ def tile_picked_pnn8_none_po_kernel(
 
         w3_codes = deal_words(nc.vector.tensor_copy, tile([P, PACK, 2 * P], U8, "w3_codes"), late_words[:, : 2 * WIDTH])
         w4_codes = deal_words(nc.vector.tensor_copy, tile([P, PACK, 2 * P], U8, "w4_codes"), late_words[:, 2 * WIDTH :])
-        last_planes = tile([P, 2 * WIDTH], U8, "last_planes")
-        deal_scales(nc.vector, last_planes[:], late_rows[:])
+        last_planes = late_rows[:, : 2 * WIDTH]
+        deal_scales(nc.vector, late_rows[:, :WIDTH], late_rows[:, WIDTH : 2 * WIDTH])
+        deal_scales(nc.gpsimd, late_rows[:, WIDTH : 2 * WIDTH], late_rows[:, 2 * WIDTH :])
         mend_rows(nc.sync, last_planes)
         w3_plane = last_planes[:, :WIDTH].rearrange("p (t m) -> p t m", t=PACK)
         w4_plane = last_planes[:, WIDTH:].rearrange("p (t m) -> p t m", t=PACK)
@@ -162,10 +163,12 @@ def tile_picked_pnn8_none_po_kernel(
             piece = bank([P, CHUNK], "e_piece%d" % c, PACK + c)
             e_product(piece[:], 0, cols)
             nc.scalar.activation(out=e_rows[0][:, cols], in_=piece[:], func=COPY, scale=0.5)
+        e_banks = {}
         for t in range(1, PACK):
-            e_bank = bank([P, PLACES], "e_bank%d" % t, t)
-            e_product(e_bank[:], t, slice(0, PLACES))
-            nc.scalar.activation(out=e_rows[t][:, :PLACES], in_=e_bank[:], func=COPY, scale=half[:])
+            e_banks[t] = bank([P, PLACES], "e_bank%d" % t, t)
+            e_product(e_banks[t][:], t, slice(0, PLACES))
+        for t in (1, 2):
+            nc.scalar.activation(out=e_rows[t][:, :PLACES], in_=e_banks[t][:], func=COPY, scale=half[:])
 
         picks = tile([P, 2, PLACES], F32, "picks")
         middle_picks = placed([P, 3, HALF], F32, "middle_picks", w1_raw_at + 2 * PACK * WIDTH)
@@ -195,8 +198,10 @@ def tile_picked_pnn8_none_po_kernel(
         first_pick(picks[:, 0], 0, 0, PLACES)
         round_w1(nc.vector.tensor_copy, 0)
         first_pick(picks[:, 1], 1, 0, PLACES)
-        round_w1(nc.scalar.copy, 1)
+        nc.scalar.activation(out=e_rows[3][:], in_=e_banks[3][:], func=COPY, scale=0.5)
+        round_w1(nc.scalar.copy, 2)
         second_pick(picks[:, 0], 0, 0, PLACES)
+        round_w1(nc.vector.tensor_copy, 1)
         second_pick(picks[:, 1], 1, 0, PLACES)
         w1_codes = tile([P, WIDTH], U32, "w1_codes")
         w1_plane = tile([P, WIDTH], U8, "w1_plane")

@@ -212,7 +212,6 @@ def tile_picked_pnn8_none_po_kernel(
             second_pick(first, t, start, HALF)
 
         y_banks = []
-        y_bf = [tile([P, 2, PACK * CHUNK], BF16, "y_bf%d" % h) for h in range(2)]
         for c in range(chunks):
             cols = slice(c * CHUNK, (c + 1) * CHUNK)
             y_bank = bank([P, PACK, CHUNK], "y_bank%d" % c, PACK + c)
@@ -224,15 +223,18 @@ def tile_picked_pnn8_none_po_kernel(
                 )
             y_banks.append(y_bank)
 
-        def weave_y(c):
-            nc.scalar.copy(out=woven(y_bf[c // 2][:, c % 2, :]), in_=sliced(y_banks[c][:]))
+        def weave_y(c, rounded):
+            nc.scalar.copy(out=woven(rounded), in_=sliced(y_banks[c][:]))
 
-        weave_y(0)
-        weave_y(1)
-        weave_y(2)
+        y_pair = tile([P, 2 * PACK * CHUNK], BF16, "y_pair")
+        y_third = tile([P, PACK * CHUNK], BF16, "y_third")
+        weave_y(0, y_pair[:, : PACK * CHUNK])
+        weave_y(1, y_pair[:, PACK * CHUNK :])
+        weave_y(2, y_third[:])
         late_picks = sb.tile([P, CHUNK], F32, name="late_picks", tag="w1_codes", align_bytes=64)
         first_pick(late_picks[:], 3, 2 * CHUNK, CHUNK)
-        weave_y(3)
+        y_last = tile([P, PACK * CHUNK], BF16, "y_last")
+        weave_y(3, y_last[:])
 
         def quantised(name, bf, width):
             codes = tile([P, width], U32, name + "_codes")
@@ -242,11 +244,11 @@ def tile_picked_pnn8_none_po_kernel(
 
         y_operands = {}
 
-        def quantise_y(h):
-            codes, plane = quantised("y%d" % h, y_bf[h][:].rearrange("p c n -> p (c n)"), HALF)
-            for n in range(2):
+        def quantise_y(first, count, rounded):
+            codes, plane = quantised("y%d" % first, rounded[:], count * CHUNK)
+            for n in range(count):
                 cols = slice(n * CHUNK, (n + 1) * CHUNK)
-                y_operands[2 * h + n] = (codes[:, cols], plane[:, cols])
+                y_operands[first + n] = (codes[:, cols], plane[:, cols])
 
         z_bf = [tile([P, PACK * CHUNK], BF16, "z_bf%d" % c) for c in range(chunks)]
 
@@ -274,7 +276,7 @@ def tile_picked_pnn8_none_po_kernel(
                 )
             return parts
 
-        out_bf = [tile([P, PACK * CHUNK], BF16, "out_bf%d" % c) for c in range(chunks)]
+        out_bf = {c: tile([P, PACK * CHUNK], BF16, "out_bf%d" % c) for c in range(1, chunks)}
         out_f32 = [tile([P, PACK, CHUNK], F32, "out_f32_%d" % c) for c in range(chunks)]
 
         def z_passes(c, parts):
@@ -285,16 +287,13 @@ def tile_picked_pnn8_none_po_kernel(
                     rhs=codes[:].bitcast(FP8X4), rhs_scale=plane[:], start=False, stop=c == last or t == PACK - 1,
                 )
                 if c == last:
-                    copy = nc.scalar.copy if t % 2 else nc.vector.tensor_copy
+                    copy = nc.vector.tensor_copy if t == 2 else nc.scalar.copy
                     copy(out=out_f32[c][:, t, :], in_=parts[t])
 
         def store_chunk(c):
             if c != last:
                 nc.scalar.copy(out=out_f32[c][:], in_=out_banks[c][:])
             nc.sync.dma_start(out=out_rows[:, :, c * CHUNK : (c + 1) * CHUNK], in_=out_f32[c][:])
-
-        def weave_from_bank(c):
-            nc.scalar.copy(out=woven(out_bf[c][:]), in_=sliced(out_banks[c][:]))
 
         def weave_from_copy(c, start, width):
             rounded = out_bf[c][:, PACK * start : PACK * (start + width)]
@@ -311,30 +310,34 @@ def tile_picked_pnn8_none_po_kernel(
                 nc.sync.dma_start(out=out_words[:, pair], in_=out_codes[:, pair].bitcast(I32))
 
         z_values(0)
-        quantise_y(0)
+        quantise_y(0, 2, y_pair)
         opened = [y_passes(0), y_passes(1)]
         z_passes(0, opened[0])
         last_picks = sb.tile([P, CHUNK], F32, name="last_picks", tag="z0_codes", align_bytes=64)
         first_pick(last_picks[:], 3, 3 * CHUNK, CHUNK)
         store_chunk(0)
-        weave_from_bank(0)
         z_values(1)
         second_pick(late_picks[:], 3, 2 * CHUNK, CHUNK)
         z_passes(1, opened[1])
         store_chunk(1)
-        quantise_y(1)
-        opened.extend([y_passes(2), y_passes(3)])
+        nc.scalar.copy(out=woven(out_bf[1][:, : PACK * CHUNK // 2]), in_=sliced(out_banks[1][:, :, : CHUNK // 2]))
+        quantise_y(2, 1, y_third)
+        opened.append(y_passes(2))
         z_values(2)
         second_pick(last_picks[:], 3, 3 * CHUNK, CHUNK)
         z_passes(2, opened[2])
         store_chunk(2)
-        planes(0)
+        quantise_y(last, 1, y_last)
+        opened.append(y_passes(last))
         z_values(3)
-        weave_from_copy(1, 0, CHUNK)
+        out_bf[0] = sb.tile([P, PACK * CHUNK], BF16, name="out_bf0", tag="y_last", align_bytes=64)
+        weave_from_copy(0, 0, CHUNK)
         z_passes(3, opened[3])
         store_chunk(3)
-        planes(1)
+        weave_from_copy(1, CHUNK // 2, CHUNK // 2)
+        planes(0)
         weave_from_copy(2, 0, CHUNK)
+        planes(1)
         planes(2)
         weave_from_copy(last, 0, CHUNK // 2)
         weave_from_copy(last, CHUNK // 2, CHUNK // 2)

@@ -24,7 +24,7 @@ HALF = PLACES // 2
 GROUP = 16
 QUADRANT = 32
 TOUCH = 64
-W1_PARTS = (0, 192, 384, 512)
+W1_PARTS = (0, 192, 320, 512)
 
 FLOPS = 4 * 2 * 512 * 512 * 512
 

@@ -313,14 +313,14 @@ def tile_picked_pnn8_none_po_kernel(
         quantise_y(0, 2, y_pair)
         opened = [y_passes(0), y_passes(1)]
         z_passes(0, opened[0])
-        last_picks = sb.tile([P, CHUNK], F32, name="last_picks", tag="z0_codes", align_bytes=64)
+        last_picks = sb.tile([P, CHUNK], F32, name="last_picks", tag="z_bf0", align_bytes=64)
         first_pick(last_picks[:], 3, 3 * CHUNK, CHUNK)
         store_chunk(0)
         z_values(1)
         second_pick(late_picks[:], 3, 2 * CHUNK, CHUNK)
         z_passes(1, opened[1])
         store_chunk(1)
-        nc.scalar.copy(out=woven(out_bf[1][:, : PACK * CHUNK // 2]), in_=sliced(out_banks[1][:, :, : CHUNK // 2]))
+        nc.scalar.copy(out=woven(out_bf[1][:]), in_=sliced(out_banks[1][:]))
         quantise_y(2, 1, y_third)
         opened.append(y_passes(2))
         z_values(2)
@@ -334,7 +334,6 @@ def tile_picked_pnn8_none_po_kernel(
         weave_from_copy(0, 0, CHUNK)
         z_passes(3, opened[3])
         store_chunk(3)
-        weave_from_copy(1, CHUNK // 2, CHUNK // 2)
         planes(0)
         weave_from_copy(2, 0, CHUNK)
         planes(1)

@@ -24,6 +24,7 @@ HALF = PLACES // 2
 GROUP = 16
 QUADRANT = 32
 TOUCH = 64
+EARLY_FIELDS = 256
 W1_PARTS = (0, 192, 320, 512)
 
 FLOPS = 4 * 2 * 512 * 512 * 512
@@ -99,13 +100,15 @@ def tile_picked_pnn8_none_po_kernel(
 
         nc.vector.memset(x_scale_table[:].bitcast(I32), 0)
         nc.sync.dma_start(offs_sb[:], offs)
+        x_rows = x_words[0].rearrange("p c r -> p (c r)").bitcast(I32)
+        nc.sync.dma_start(out=x_table[:, :EARLY_FIELDS].bitcast(I32), in_=x_rows[:, :EARLY_FIELDS])
         w2_scale_words = w2_scales[0].bitcast(I32)
         nc.scalar.dma_start(out=w2_rows[:].bitcast(I32), in_=w2_scale_words.unsqueeze(1).to_broadcast([16, 8, WIDTH // 4]))
         nc.sync.dma_start(p1_sb[:], p1)
         load_words(nc.scalar, w2_raw[:, : 2 * WIDTH], w2_words)
         nc.sync.dma_start(p2_sb[:], p2)
         nc.sync.dma_start(out=x_scale_table[0:P:8, :].bitcast(I32), in_=x_scales[0].bitcast(I32))
-        nc.sync.dma_start(out=x_table[:].bitcast(I32), in_=x_words[0].rearrange("p c r -> p (c r)").bitcast(I32))
+        nc.sync.dma_start(out=x_table[:, EARLY_FIELDS:].bitcast(I32), in_=x_rows[:, EARLY_FIELDS:])
 
         w2_planes = tile([P, WIDTH], U8, "w2_planes")
         w2_plane = w2_planes[:].rearrange("p (t m) -> p t m", t=PACK)

@@ -323,7 +323,7 @@ def tile_picked_pnn8_none_po_kernel(
         second_pick(late_picks[:], 3, 2 * CHUNK, CHUNK)
         z_passes(1, opened[1])
         store_chunk(1)
-        nc.scalar.copy(out=woven(out_bf[1][:]), in_=sliced(out_banks[1][:]))
+        nc.scalar.copy(out=woven(out_bf[1][:, : 2 * CHUNK]), in_=sliced(out_banks[1][:, :, : CHUNK // 2]))
         quantise_y(2, 1, y_third)
         opened.append(y_passes(2))
         z_values(2)
@@ -337,6 +337,7 @@ def tile_picked_pnn8_none_po_kernel(
         weave_from_copy(0, 0, CHUNK)
         z_passes(3, opened[3])
         store_chunk(3)
+        weave_from_copy(1, CHUNK // 2, CHUNK // 2)
         planes(0)
         weave_from_copy(2, 0, CHUNK)
         planes(1)

from contextlib import ExitStack

import concourse.mybir as mybir

F32 = mybir.dt.float32
BF16 = mybir.dt.bfloat16
I32 = mybir.dt.int32
U32 = mybir.dt.uint32
U16 = mybir.dt.uint16
U8 = mybir.dt.uint8
FP8X4 = mybir.dt.float8_e4m3fn_x4
FP4X4 = mybir.dt.float4_e2m1fn_x4
ADD = mybir.AluOpType.add
MULT = mybir.AluOpType.mult
COPY = mybir.ActivationFunctionType.Copy

P = 128
PACK = 4
FIELDS = 2048
PLACES = 512
WIDTH = 512
CHUNK = 128
HALF = PLACES // 2
GROUP = 16
QUADRANT = 32
TOUCH = 64
EARLY_FIELDS = 256
W1_PARTS = (0, 192, 320, 512)

FLOPS = 4 * 2 * 512 * 512 * 512


def tile_picked_pnn8_none_po_kernel(
    tc, x_words, x_scales, w1, w2_words, w2_scales, w3_words, w3_scales, w4_words, w4_scales, offs, p1, p2,
    out_0, out_1, out_2,
):
    nc = tc.nc
    chunks = PLACES // CHUNK

    with ExitStack() as ctx:
        sb = ctx.enter_context(tc.tile_pool(name="sb", bufs=1))
        reused = ctx.enter_context(tc.tile_pool(name="reused", bufs=1))
        ps = ctx.enter_context(tc.psum_pool(name="ps", bufs=1))

        def tile(shape, dtype, name):
            return sb.tile(shape, dtype, name=name, align_bytes=64)

        def placed(shape, dtype, name, offset):
            return reused.tile(shape, dtype, name=name, align_bytes=64, offset=offset)

        def bank(shape, name, number):
            return ps.tile(shape, F32, name=name, tag="bank%d" % number)

        def entries(start, count):
            return slice(start // GROUP, (start + count) // GROUP)

        def load_words(queue, raw, words):
            queue.dma_start(out=raw.bitcast(I32), in_=words[0].bitcast(I32))

        def deal_scales(engine, plane, raw):
            engine.tensor_copy(
                out=plane.rearrange("p (w t c i) -> p w c t i", t=PACK, c=8, i=16),
                in_=raw.rearrange("p (w c i t) -> p w c t i", t=PACK, c=8, i=16),
            )

        def deal_words(copy, words, raw):
            copy(
                out=words[:].bitcast(U16).rearrange("p t (c i) -> p c t i", i=8),
                in_=raw.bitcast(U16).rearrange("p (c i t) -> p c t i", t=PACK, i=8),
            )
            return words

        def mend_rows(queue, planes):
            for a in range(1, PACK):
                queue.dma_start(out=planes[a:P:QUADRANT, :].bitcast(I32), in_=planes[8 * a : P : QUADRANT, :].bitcast(I32))

        def woven(bf):
            return bf.rearrange("p (c i t) -> p c t i", t=PACK, i=4)

        def sliced(f32):
            return f32.rearrange("p t (c i) -> p c t i", i=4)

        sums_at = 0
        half_at = sums_at + 4 * PACK * PLACES - TOUCH
        late_rows_at = half_at + TOUCH
        late_words_at = late_rows_at + 3 * WIDTH
        w1_raw_at = late_words_at + 4 * WIDTH
        w2_raw_at = late_words_at - TOUCH
        w2_raw_bytes = 4 * WIDTH + 2 * TOUCH
        table_at = w1_raw_at + 4 * PACK * WIDTH
        w2_codes_at = table_at + FIELDS - TOUCH

        offs_sb = sb.tile([P, PLACES // GROUP], U16, name="offs_sb")
        p1_sb = sb.tile([P, PLACES // GROUP], U16, name="p1_sb")
        p2_sb = sb.tile([P, PLACES // GROUP], U16, name="p2_sb")
        x_table = tile([P, FIELDS], U32, "x_table")
        x_scale_table = placed([P, FIELDS], U8, "x_scale_table", table_at)
        w2_raw = placed([P, w2_raw_bytes], U8, "w2_raw", w2_raw_at)
        w2_rows = tile([P, WIDTH], U8, "w2_rows")

        nc.vector.memset(x_scale_table[:].bitcast(I32), 0)
        nc.sync.dma_start(offs_sb[:], offs)
        x_rows = x_words[0].rearrange("p c r -> p (c r)").bitcast(I32)
        nc.sync.dma_start(out=x_table[:, :EARLY_FIELDS].bitcast(I32), in_=x_rows[:, :EARLY_FIELDS])
        w2_scale_words = w2_scales[0].bitcast(I32)
        nc.scalar.dma_start(out=w2_rows[:].bitcast(I32), in_=w2_scale_words.unsqueeze(1).to_broadcast([16, 8, WIDTH // 4]))
        nc.sync.dma_start(p1_sb[:], p1)
        load_words(nc.scalar, w2_raw[:, : 2 * WIDTH], w2_words)
        nc.sync.dma_start(p2_sb[:], p2)
        nc.sync.dma_start(out=x_scale_table[0:P:8, :].bitcast(I32), in_=x_scales[0].bitcast(I32))
        nc.sync.dma_start(out=x_table[:, EARLY_FIELDS:].bitcast(I32), in_=x_rows[:, EARLY_FIELDS:])

        w2_planes = tile([P, WIDTH], U8, "w2_planes")
        w2_plane = w2_planes[:].rearrange("p (t m) -> p t m", t=PACK)
        deal_scales(nc.gpsimd, w2_planes[:], w2_rows[:])
        mend_rows(nc.scalar, w2_planes)

        picked_rows = tile([P, PLACES], U8, "picked_rows")
        x_plane = tile([P, PLACES], U8, "x_plane")
        nc.gpsimd.memset(x_plane[:].bitcast(I32), 0)
        nc.vector.tensor_copy(picked_rows[:], x_scale_table[:].indirect(offs_sb[:]))
        for a in range(PACK):
            queue = nc.scalar if a % 2 else nc.sync
            queue.dma_start(out=x_plane[a:P:QUADRANT, :].bitcast(I32), in_=picked_rows[8 * a : P : QUADRANT, :].bitcast(I32))
        w2_codes = deal_words(nc.vector.tensor_copy, placed([P, PACK, 2 * P], U8, "w2_codes", w2_codes_at), w2_raw[:, : 2 * WIDTH])

        late_words = placed([P, 4 * WIDTH], U8, "late_words", late_words_at)
        late_rows = placed([P, 3 * WIDTH], U8, "late_rows", late_rows_at)
        nc.gpsimd.memset(late_rows[:, WIDTH:].bitcast(I32), 0)
        load_words(nc.sync, late_words[:, : 2 * WIDTH], w3_words)
        load_words(nc.sync, late_words[:, 2 * WIDTH :], w4_words)
        nc.sync.dma_start(out=late_rows[0:P:8, WIDTH : 2 * WIDTH].bitcast(I32), in_=w3_scales[0].bitcast(I32))
        nc.sync.dma_start(out=late_rows[0:P:8, 2 * WIDTH :].bitcast(I32), in_=w4_scales[0].bitcast(I32))
        w1_rows = w1.rearrange("(p j) c -> p j c", j=PACK)
        w1_raw = placed([P, PACK * WIDTH], F32, "w1_raw", w1_raw_at)
        w1_parts = []
        for start, stop in zip(W1_PARTS, W1_PARTS[1:]):
            part = w1_raw[:, PACK * start : PACK * stop].rearrange("p (j c) -> p j c", j=PACK)
            nc.sync.dma_start(out=part, in_=w1_rows[:, :, start:stop])
            w1_parts.append((part, slice(start // PACK, stop // PACK)))

        x_codes = tile([P, PLACES], U32, "x_codes")
        for start in (0, HALF):
            nc.vector.tensor_copy(x_codes[:, start : start + HALF], x_table[:].indirect(offs_sb[:, entries(start, HALF)]))

        w3_codes = deal_words(nc.vector.tensor_copy, tile([P, PACK, 2 * P], U8, "w3_codes"), late_words[:, : 2 * WIDTH])
        w4_codes = deal_words(nc.vector.tensor_copy, tile([P, PACK, 2 * P], U8, "w4_codes"), late_words[:, 2 * WIDTH :])
        last_planes = late_rows[:, : 2 * WIDTH]
        deal_scales(nc.vector, late_rows[:, :WIDTH], late_rows[:, WIDTH : 2 * WIDTH])
        deal_scales(nc.gpsimd, late_rows[:, WIDTH : 2 * WIDTH], late_rows[:, 2 * WIDTH :])
        mend_rows(nc.sync, last_planes)
        w3_plane = last_planes[:, :WIDTH].rearrange("p (t m) -> p t m", t=PACK)
        w4_plane = last_planes[:, WIDTH:].rearrange("p (t m) -> p t m", t=PACK)

        def e_product(out, t, cols):
            nc.tensor.matmul_mx(
                out=out, lhsT=w2_codes[:, t, :].bitcast(FP4X4), lhsT_scale=w2_plane[:, t, :],
                rhs=x_codes[:, cols].bitcast(FP8X4), rhs_scale=x_plane[:, cols], start=True, stop=True,
            )

        e_rows = [tile([P, (2 if t < 2 else 1) * PLACES], F32, "e_row%d" % t) for t in range(PACK)]
        half = placed([P, 1], F32, "half", half_at)
        nc.gpsimd.memset(half[:], 0.5)
        for c in range(chunks):
            cols = slice(c * CHUNK, (c + 1) * CHUNK)
            piece = bank([P, CHUNK], "e_piece%d" % c, PACK + c)
            e_product(piece[:], 0, cols)
            nc.scalar.activation(out=e_rows[0][:, cols], in_=piece[:], func=COPY, scale=0.5)
        e_banks = {}
        for t in range(1, PACK):
            e_banks[t] = bank([P, PLACES], "e_bank%d" % t, t)
            e_product(e_banks[t][:], t, slice(0, PLACES))
        for t in (1, 2):
            nc.scalar.activation(out=e_rows[t][:, :PLACES], in_=e_banks[t][:], func=COPY, scale=half[:])

        picks = tile([P, 2, PLACES], F32, "picks")
        middle_picks = placed([P, 3, HALF], F32, "middle_picks", w1_raw_at + 2 * PACK * WIDTH)
        sums = placed([P, PACK, PLACES], F32, "sums", sums_at)

        def first_pick(out, t, start, count):
            window = e_rows[t][:].indirect(p1_sb[:, entries(start, count)])
            if t == 0:
                nc.vector.tensor_copy(out, window)
            else:
                nc.scalar.activation(out=out, in_=window, func=COPY)

        def second_pick(first, t, start, count):
            nc.vector.tensor_tensor(
                sums[:, t, start : start + count], e_rows[t][:].indirect(p2_sb[:, entries(start, count)]), first, ADD
            )

        w1_bf = tile([P, PACK * WIDTH], BF16, "w1_bf")

        def round_w1(copy, h):
            part, columns = w1_parts[h]
            copy(
                out=w1_bf[:].rearrange("p (t m j) -> p m j t", t=PACK, j=PACK)[:, columns],
                in_=part.rearrange("p j (m t) -> p m j t", t=PACK),
            )

        first_pick(picks[:, 0], 0, 0, PLACES)
        round_w1(nc.vector.tensor_copy, 0)
        first_pick(picks[:, 1], 1, 0, PLACES)
        nc.scalar.activation(out=e_rows[3][:], in_=e_banks[3][:], func=COPY, scale=0.5)
        round_w1(nc.scalar.copy, 2)
        second_pick(picks[:, 0], 0, 0, PLACES)
        round_w1(nc.vector.tensor_copy, 1)
        second_pick(picks[:, 1], 1, 0, PLACES)
        w1_codes = tile([P, WIDTH], U32, "w1_codes")
        w1_plane = tile([P, WIDTH], U8, "w1_plane")
        nc.vector.quantize_mx(out=w1_codes[:].bitcast(FP8X4), scales=w1_plane[:], in_=w1_bf[:])
        for t, start in ((2, 0), (3, 0), (2, HALF)):
            first = middle_picks[:, t - 2 + 2 * start // HALF]
            first_pick(first, t, start, HALF)
            second_pick(first, t, start, HALF)

        y_banks = []
        for c in range(chunks):
            cols = slice(c * CHUNK, (c + 1) * CHUNK)
            y_bank = bank([P, PACK, CHUNK], "y_bank%d" % c, PACK + c)
            for t in range(PACK):
                feats = slice(t * P, (t + 1) * P)
                nc.tensor.matmul_mx(
                    out=y_bank[:, t, :], lhsT=w1_codes[:, feats].bitcast(FP8X4), lhsT_scale=w1_plane[:, feats],
                    rhs=x_codes[:, cols].bitcast(FP8X4), rhs_scale=x_plane[:, cols], start=True, stop=True,
                )
            y_banks.append(y_bank)

        def weave_y(c, rounded):
            nc.scalar.copy(out=woven(rounded), in_=sliced(y_banks[c][:]))

        y_pair = tile([P, 2 * PACK * CHUNK], BF16, "y_pair")
        y_third = tile([P, PACK * CHUNK], BF16, "y_third")
        weave_y(0, y_pair[:, : PACK * CHUNK])
        weave_y(1, y_pair[:, PACK * CHUNK :])
        weave_y(2, y_third[:])
        late_picks = sb.tile([P, CHUNK], F32, name="late_picks", tag="w1_codes", align_bytes=64)
        first_pick(late_picks[:], 3, 2 * CHUNK, CHUNK)
        y_last = tile([P, PACK * CHUNK], BF16, "y_last")
        weave_y(3, y_last[:])

        def quantised(name, bf, width):
            codes = tile([P, width], U32, name + "_codes")
            plane = tile([P, width], U8, name + "_plane")
            nc.vector.quantize_mx(out=codes[:].bitcast(FP8X4), scales=plane[:], in_=bf)
            return codes, plane

        y_operands = {}

        def quantise_y(first, count, rounded):
            codes, plane = quantised("y%d" % first, rounded[:], count * CHUNK)
            for n in range(count):
                cols = slice(n * CHUNK, (n + 1) * CHUNK)
                y_operands[first + n] = (codes[:, cols], plane[:, cols])

        z_bf = [tile([P, PACK * CHUNK], BF16, "z_bf%d" % c) for c in range(chunks)]

        def z_values(c):
            nc.vector.tensor_tensor(woven(z_bf[c][:]), sliced(sums[:, :, c * CHUNK : (c + 1) * CHUNK]), sliced(y_banks[c][:]), MULT)

        out_codes = tile([P, PLACES], U32, "out_codes")
        out_plane = tile([P, PLACES], U8, "out_plane")
        out_rows = out_0.rearrange("(p t) j -> p t j", t=PACK)
        out_words = out_1[0].rearrange("p c r -> p (c r)").bitcast(I32)
        last = chunks - 1
        out_banks = {}

        def y_passes(c):
            if c == last:
                parts = [bank([P, CHUNK], "last_bank%d" % t, (3, 4, 5, 0)[t])[:] for t in range(PACK)]
            else:
                whole = bank([P, PACK, CHUNK], "out_bank%d" % c, c)
                parts = [whole[:, t, :] for t in range(PACK)]
                out_banks[c] = whole
            for t in range(PACK):
                nc.tensor.matmul_mx(
                    out=parts[t], lhsT=w3_codes[:, t, :].bitcast(FP4X4), lhsT_scale=w3_plane[:, t, :],
                    rhs=y_operands[c][0].bitcast(FP8X4), rhs_scale=y_operands[c][1], start=c == last or t == 0, stop=False,
                )
            return parts

        out_bf = {c: tile([P, PACK * CHUNK], BF16, "out_bf%d" % c) for c in range(1, chunks)}
        out_f32 = [tile([P, PACK, CHUNK], F32, "out_f32_%d" % c) for c in range(chunks)]

        def z_passes(c, parts):
            codes, plane = quantised("z%d" % c, z_bf[c][:], CHUNK)
            for t in range(PACK):
                nc.tensor.matmul_mx(
                    out=parts[t], lhsT=w4_codes[:, t, :].bitcast(FP4X4), lhsT_scale=w4_plane[:, t, :],
                    rhs=codes[:].bitcast(FP8X4), rhs_scale=plane[:], start=False, stop=c == last or t == PACK - 1,
                )
                if c == last:
                    copy = nc.vector.tensor_copy if t == 2 else nc.scalar.copy
                    copy(out=out_f32[c][:, t, :], in_=parts[t])

        def store_chunk(c):
            if c != last:
                nc.scalar.copy(out=out_f32[c][:], in_=out_banks[c][:])
            nc.sync.dma_start(out=out_rows[:, :, c * CHUNK : (c + 1) * CHUNK], in_=out_f32[c][:])

        def weave_from_copy(c, start, width):
            rounded = out_bf[c][:, PACK * start : PACK * (start + width)]
            nc.vector.tensor_copy(out=woven(rounded), in_=sliced(out_f32[c][:, :, start : start + width]))

        def planes(c):
            width = CHUNK // 2 if c == last else CHUNK
            for start in range(0, CHUNK, width):
                cols = slice(c * CHUNK + start, c * CHUNK + start + width)
                rounded = out_bf[c][:, PACK * start : PACK * (start + width)]
                nc.vector.quantize_mx(out=out_codes[:, cols].bitcast(FP8X4), scales=out_plane[:, cols], in_=rounded)
            if c % 2:
                pair = slice((c - 1) * CHUNK, (c + 1) * CHUNK)
                nc.sync.dma_start(out=out_words[:, pair], in_=out_codes[:, pair].bitcast(I32))

        z_values(0)
        quantise_y(0, 2, y_pair)
        opened = [y_passes(0), y_passes(1)]
        z_passes(0, opened[0])
        last_picks = sb.tile([P, CHUNK], F32, name="last_picks", tag="z_bf0", align_bytes=64)
        first_pick(last_picks[:], 3, 3 * CHUNK, CHUNK)
        store_chunk(0)
        z_values(1)
        second_pick(late_picks[:], 3, 2 * CHUNK, CHUNK)
        z_passes(1, opened[1])
        store_chunk(1)
        nc.scalar.copy(out=woven(out_bf[1][:, : 2 * CHUNK]), in_=sliced(out_banks[1][:, :, : CHUNK // 2]))
        quantise_y(2, 1, y_third)
        opened.append(y_passes(2))
        z_values(2)
        second_pick(last_picks[:], 3, 3 * CHUNK, CHUNK)
        z_passes(2, opened[2])
        store_chunk(2)
        quantise_y(last, 1, y_last)
        opened.append(y_passes(last))
        z_values(3)
        out_bf[0] = sb.tile([P, PACK * CHUNK], BF16, name="out_bf0", tag="y_last", align_bytes=64)
        weave_from_copy(0, 0, CHUNK)
        z_passes(3, opened[3])
        store_chunk(3)
        weave_from_copy(1, CHUNK // 2, CHUNK // 2)
        planes(0)
        weave_from_copy(2, 0, CHUNK)
        planes(1)
        planes(2)
        weave_from_copy(last, 0, CHUNK // 2)
        weave_from_copy(last, CHUNK // 2, CHUNK // 2)
        planes(3)

        plane_rows = out_2[0].rearrange("(q a) c -> a q c", a=PACK)
        for a in range(PACK):
            queue = nc.scalar if a % 2 else nc.sync
            queue.dma_start(out=plane_rows[a].bitcast(I32), in_=out_plane[a:P:QUADRANT, :].bitcast(I32))
